import numpy as np
import ml_dtypes


def mxq(x, axis, fmt="e4m3"):
    dtype, down = {"e4m3": (ml_dtypes.float8_e4m3fn, 7), "e5m2": (ml_dtypes.float8_e5m2, 14)}[fmt]
    v = np.moveaxis(np.asarray(x, np.float32).astype(ml_dtypes.bfloat16).astype(np.float64), axis, -1)
    blocks = v.reshape(v.shape[:-1] + (-1, 32))
    amax = np.abs(blocks).max(-1, keepdims=True)
    byte = np.maximum(np.where(amax > 0, np.frexp(amax)[1] - 1 + 127, 0) - down, 1)
    scale = np.exp2(byte - 127.0)
    codes = (blocks / scale).astype(np.float32).astype(dtype).astype(np.float64)
    return np.moveaxis((codes * scale).reshape(v.shape), -1, axis)


WIDE = False


def mx_kscale(k):
    if not WIDE:
        return np.ones(k)
    levels = np.array([10, -10, 5, -5, 0])
    if k % 512:
        return np.exp2(np.random.permutation(np.resize(levels, k // 32))).repeat(32)
    a = np.empty((k // 512, 16))
    for p in range(k // 512):
        a[p, :8] = np.random.permutation(np.resize(levels, 8))
        for g in range(8):
            far = levels[np.abs(levels - a[p, g]) >= 10]
            a[p, g + 8] = far[np.random.randint(len(far))]
    return np.exp2(a.ravel()).repeat(32)


def f64(x):
    return np.asarray(x).astype(np.float64)


def striped(idx):
    return np.tile(idx.reshape(-1, 16).T, (8, 1)).astype(np.uint16)


def unstriped(offs):
    return offs[:16].T.reshape(-1).astype(np.int64)


E2M1 = np.array([0.0, 0.5, 1.0, 1.5, 2.0, 3.0, 4.0, 6.0, -0.0, -0.5, -1.0, -1.5, -2.0, -3.0, -4.0, -6.0])


def pack_weight(w, fmt):
    k, n = w.shape
    w = f64(np.asarray(w, np.float32).astype(ml_dtypes.bfloat16)).reshape(k // 32, 32, n)
    amax = np.abs(w).max(1)
    if fmt == "e4m3":
        byte = np.frexp(amax)[1] - 1 + 127 - 7
    else:
        mant, ex = np.frexp(amax / 6.0)
        byte = np.where(mant > 0.5, ex, ex - 1) + 127
    byte = np.clip(np.where(amax > 0, byte, 1), 1, 254)
    scaled = (w * np.exp2(127.0 - byte)[:, None, :]).reshape(k, n).astype(np.float32)
    by_word = np.ascontiguousarray(scaled.reshape(k // 512, 128, 4, n).transpose(0, 1, 3, 2))
    if fmt == "e4m3":
        words = by_word.astype(ml_dtypes.float8_e4m3fn).view(np.uint8)
    else:
        c = by_word.astype(ml_dtypes.float4_e2m1fn).view(np.uint8) & 0xF
        words = (c[..., 0::2] | (c[..., 1::2] << 4)).reshape(k // 512, 128, 2 * n)
    return np.ascontiguousarray(words), np.ascontiguousarray(byte.astype(np.uint8).reshape(k // 512, 16, n))


def unpack_weight(words, scales, fmt):
    g, _, n = scales.shape
    words = np.ascontiguousarray(words).reshape(g, 128, n, -1)
    if fmt == "e4m3":
        vals = words.view(ml_dtypes.float8_e4m3fn).astype(np.float64)
    else:
        nib = np.empty((g, 128, n, 4), np.uint8)
        nib[..., 0::2] = words & 0xF
        nib[..., 1::2] = words >> 4
        vals = E2M1[nib]
    vals = vals * np.repeat(np.exp2(scales.astype(np.float64) - 127.0), 8, axis=1)[..., None]
    return vals.transpose(0, 1, 3, 2).reshape(g * 512, n)


def relu2(v):
    return np.maximum(v, 0.0) ** 2


K, T, E, C, H, N = 1536, 768, 2, 256, 512, 128


def by_expert(wq, xq):
    return np.concatenate([wq[e].T @ xq[:, e * C:(e + 1) * C] for e in range(E)], axis=1)


def setup_inputs():
    n = np.random.standard_normal
    s = mx_kscale(K)[:, None]
    u = mx_kscale(H)
    w1 = [pack_weight(m, "e2m1") for m in n((E + 1, K, H)) / np.sqrt(K) / s[None] * u[None, None, :]]
    w2 = [pack_weight(m, "e2m1") for m in n((E + 1, H, N)) / np.sqrt(H) / u[None, :, None] ** 2]
    x = pack_weight(n((K, T)) * s, "e4m3")
    return {
        "x_words": x[0],
        "x_scales": x[1],
        "w1_words": np.stack([m[0] for m in w1]),
        "w1_scales": np.stack([m[1] for m in w1]),
        "w2_words": np.stack([m[0] for m in w2]),
        "w2_scales": np.stack([m[1] for m in w2]),
        "gate": np.tile(np.random.uniform(0.2, 1.0, E * C), (N, 1)).astype(np.float32),
        "offs": striped(np.random.permutation(T)[:E * C]),
    }


def reference(x_words, x_scales, w1_words, w1_scales, w2_words, w2_scales, gate, offs):
    idx = unstriped(offs)
    w1 = np.stack([unpack_weight(w1_words[e], w1_scales[e], "e2m1") for e in range(E + 1)])
    w2 = np.stack([unpack_weight(w2_words[e], w2_scales[e], "e2m1") for e in range(E + 1)])
    w1q, w2q = w1, w2
    xs = unpack_weight(x_words, x_scales, "e4m3")
    hs = relu2(w1q[E].T @ xs)
    ys = w2q[E].T @ mxq(hs, 0, "e4m3")
    xq = unpack_weight(x_words, x_scales, "e4m3")[:, idx]
    h = relu2(by_expert(w1q, xq))
    y = by_expert(w2q, mxq(h, 0, "e4m3"))
    out = ys
    out[:, idx] += f64(gate) * y
    return out

@@ -1,0 +1,348 @@
+from contextlib import ExitStack
+
+import concourse.mybir as mybir
+from concourse.masks import make_identity
+
+K, T, E, C, H, N = 1536, 768, 2, 256, 512, 128
+FLOPS = 2 * (T + E * C) * (K * H + H * N)
+
+F32 = mybir.dt.float32
+BF16 = mybir.dt.bfloat16
+I32 = mybir.dt.int32
+U32 = mybir.dt.uint32
+U16 = mybir.dt.uint16
+U8 = mybir.dt.uint8
+FP8X4 = mybir.dt.float8_e4m3fn_x4
+FP4X4 = mybir.dt.float4_e2m1fn_x4
+ACT = mybir.ActivationFunctionType
+ALU = mybir.AluOpType
+
+P = 128
+PASSES = K // 512
+SHARED = E
+UNIT = 256
+BANK = 512
+UNITS = [(2, 0), (2, 256), (0, 0), (1, 256), (2, 512)]
+MODE = [2, 2, 2, 2, 2]
+L1_BANK = [[0, 1], [2, 3], [0, 1], [2, 3], [0, 1]]
+T_BANK = [[4, 5], [6, 4], [5, 6], [4, 5], [6, 4]]
+Y_BANK = [(3, 0), (3, 256), (7, 0), (7, 256), (0, 0)]
+W1S_GROUPS = [1, 2]
+W1S_ORDER = [2, 0, 1]
+
+
+def tile_moe_shr_mlp_relu2_kernel(
+    tc, x_words, x_scales, w1_words, w1_scales, w2_words, w2_scales, gate, offs, out
+):
+    nc = tc.nc
+    with ExitStack() as ctx:
+        keep = ctx.enter_context(tc.tile_pool(name="keep", bufs=1))
+        psum = ctx.enter_context(tc.psum_pool(name="psum", bufs=1))
+        queue = {"Q": nc.sync, "S": nc.scalar, "G": nc.gpsimd}
+        engine = {"V": nc.vector, "G": nc.gpsimd}
+
+        offsets = keep.tile([P, E * C // 16], U16, name="offsets")
+        xw = [keep.tile([P, T], I32, name="xw%d" % o, align_bytes=64) for o in range(PASSES)]
+        xs = keep.tile([P, PASSES, T], U8, name="xs", align_bytes=64)
+        w1w = [keep.tile([P, PASSES, 2 * H], U8, name="w1w%d" % e, align_bytes=64) for e in range(E + 1)]
+        w1s = [keep.tile([P, n * PASSES, H], U8, name="w1s%d" % j, align_bytes=64) for j, n in enumerate(W1S_GROUPS)]
+        w2w = keep.tile([P, E + 1, 2 * N], U8, name="w2w", align_bytes=64)
+        w2s = keep.tile([P, E + 1, N], U8, name="w2s", align_bytes=64)
+        gates = keep.tile([P, E * C], F32, name="gates")
+        ident = keep.tile([P, P], F32, name="ident")
+        zero = keep.tile([P, 1], F32, name="zero")
+        window = keep.tile([P, T], F32, name="window")
+        gw = [keep.tile([P, E * C], U32, name="gw%d" % o, align_bytes=64) for o in range(PASSES)]
+        gs = [keep.tile([P, E * C], U8, name="gs%d" % o, align_bytes=64) for o in range(PASSES)]
+        banks = [psum.tile([P, BANK], F32, name="bank%d" % b) for b in range(8)]
+        relus = [[keep.tile([P, H], F32, name="r%d_%d" % (k, a)) for a in range(2)] for k in range(5)]
+        hidden = [keep.tile([P, 2, H], BF16, name="h%d" % k, align_bytes=64) for k in range(5)]
+        grouped = [keep.tile([P, 4 * UNIT], BF16, name="g%d" % k, align_bytes=64) for k in range(5)]
+        hw = [keep.tile([P, UNIT], U32, name="hw%d" % k, align_bytes=64) for k in range(5)]
+        hs = [keep.tile([P, UNIT], U8, name="hs%d" % k, align_bytes=64) for k in range(5)]
+        yv = [keep.tile([P, C], F32, name="yv%d" % e) for e in range(E)]
+        res = keep.tile([P, T], F32, name="res")
+
+        def w1_plane(e, o):
+            first = 0
+            for j, n in enumerate(W1S_GROUPS):
+                if W1S_ORDER.index(e) < first + n:
+                    return w1s[j][:, (W1S_ORDER.index(e) - first) * PASSES + o, :]
+                first += n
+
+        def zero_plane(eng, tile):
+            engine[eng].memset(tile[:].rearrange("p a b -> p (a b)").bitcast(I32), 0)
+
+        def load_scales(q, plane, rows, r):
+            by_row = rows.rearrange("a (q r) w -> r q a w", r=4)
+            queue[q].dma_start(out=plane[r:P:32, :, :].bitcast(I32), in_=by_row[r].bitcast(I32))
+
+        def load_xs(q, r):
+            load_scales(q, xs, x_scales, r)
+
+        def load_w1s(q, j, e0, e1, r):
+            load_scales(q, w1s[j], w1_scales[e0:e1].rearrange("e s q i -> (e s) q i"), r)
+
+        def load_w2s(q, r):
+            load_scales(q, w2s, w2_scales.rearrange("e s q n -> (e s) q n"), r)
+
+        def load_x(q, o, c0, c1):
+            words = x_words[o].rearrange("p t r -> p (t r)").bitcast(I32)
+            queue[q].dma_start(out=xw[o][:, c0:c1], in_=words[:, c0:c1])
+
+        def load_w1(q, e, s0, s1):
+            queue[q].dma_start(
+                out=w1w[e][:, s0:s1, :].bitcast(I32),
+                in_=w1_words[e, s0:s1].rearrange("s p b -> p s b").bitcast(I32),
+            )
+
+        def load_w2(q):
+            queue[q].dma_start(out=w2w[:].bitcast(I32), in_=w2_words.rearrange("e s p b -> p (e s) b").bitcast(I32))
+
+        def load_gate(q):
+            queue[q].dma_start(out=gates[:], in_=gate)
+
+        def slots(j0, j1):
+            return offsets[:, j0 // 16 : j1 // 16]
+
+        def gather_scales(o, j0, j1):
+            nc.vector.tensor_copy(gs[o][:, j0:j1], xs[:, o, :].indirect(slots(j0, j1)))
+
+        def gather_words(o, j0, j1):
+            nc.vector.tensor_copy(gw[o][:, j0:j1], xw[o][:].bitcast(U32).indirect(slots(j0, j1)))
+
+        def layer1(k, a, o):
+            e, c0 = UNITS[k]
+            cols = slice(c0 + a * P, c0 + (a + 1) * P)
+            if e == SHARED:
+                tok, tok_s = xw[o][:, cols], xs[:, o, cols]
+            else:
+                tok, tok_s = gw[o][:, cols], gs[o][:, cols]
+            nc.tensor.matmul_mx(
+                out=banks[L1_BANK[k][a]][:],
+                lhsT=tok.bitcast(FP8X4),
+                lhsT_scale=tok_s,
+                rhs=w1w[e][:, o, :].bitcast(FP4X4),
+                rhs_scale=w1_plane(e, o),
+                start=(o == 0),
+                stop=(o == PASSES - 1),
+            )
+
+        def relu(eng, k, a):
+            if MODE[k] == 1:
+                src = banks[L1_BANK[k][a]][:].rearrange("t (p u e) -> t u p e", u=2, e=2)
+                dst = relus[k][a][:].rearrange("t (u p e) -> t u p e", u=2, e=2)
+            else:
+                src = banks[L1_BANK[k][a]][:].rearrange("t (p j) -> t j p", j=4)
+                dst = relus[k][a][:].rearrange("t (j p) -> t j p", j=4)
+            if eng == "S":
+                nc.scalar.activation(dst, src, ACT.Relu)
+            else:
+                nc.vector.tensor_scalar_max(dst, src, 0.0)
+
+        def square1(eng, k, a):
+            r = relus[k][a][:]
+            if eng == "S":
+                nc.scalar.activation(hidden[k][:, a, :], r, ACT.Square)
+            else:
+                engine[eng].tensor_tensor(hidden[k][:, a, :], r, r, ALU.mult)
+
+        def turn1(k, a):
+            words = hidden[k][:, a, :].bitcast(F32)
+            for u in range(2):
+                j = 2 * a + u
+                nc.tensor.transpose(banks[T_BANK[k][0]][:, j * P : (j + 1) * P], words[:, u * P : (u + 1) * P], ident[:])
+
+        def leave1(eng, k):
+            src = banks[T_BANK[k][0]][:].rearrange("p (a u t) -> p a t u", a=2, u=2)
+            dst = grouped[k][:].bitcast(F32).rearrange("p (a t u) -> p a t u", a=2, u=2)
+            if eng == "S":
+                nc.scalar.copy(dst, src)
+            else:
+                nc.vector.tensor_copy(dst, src)
+
+        def turn2(k, a):
+            for j in range(4):
+                nc.tensor.transpose(banks[T_BANK[k][a]][:, j * P : (j + 1) * P], relus[k][a][:, j * P : (j + 1) * P], ident[:])
+
+        def square2(k, a):
+            src = banks[T_BANK[k][a]][:].rearrange("p (j t) -> p t j", j=4)
+            dst = grouped[k][:, a * H : (a + 1) * H].rearrange("p (t j) -> p t j", j=4)
+            nc.scalar.activation(dst, src, ACT.Square)
+
+        def quantize(k, c0, c1):
+            nc.vector.quantize_mx(out=hw[k][:, c0:c1].bitcast(FP8X4), scales=hs[k][:, c0:c1], in_=grouped[k][:, 4 * c0 : 4 * c1])
+
+        def y_of(k, c0, c1):
+            b, first = Y_BANK[k]
+            return banks[b][:, first + c0 : first + c1]
+
+        def layer2(k, c0, c1):
+            e = UNITS[k][0]
+            nc.tensor.matmul_mx(
+                out=y_of(k, c0, c1),
+                lhsT=w2w[:, e, :].bitcast(FP4X4),
+                lhsT_scale=w2s[:, e, :],
+                rhs=hw[k][:, c0:c1].bitcast(FP8X4),
+                rhs_scale=hs[k][:, c0:c1],
+                start=True,
+                stop=True,
+            )
+
+        def leave_y(form, k, j0, j1):
+            e, c0 = UNITS[k]
+            if form == "d":
+                nc.scalar.copy(yv[e][:, j0:j1], y_of(k, j0, j1))
+            else:
+                nc.vector.tensor_tensor(yv[e][:, j0:j1], y_of(k, j0, j1), gates[:, c0 + j0 : c0 + j1], ALU.mult)
+
+        def scatter(form, k, j0, j1):
+            e, c0 = UNITS[k]
+            if form == "d":
+                nc.vector.tensor_tensor(window[:].indirect(slots(c0 + j0, c0 + j1)), yv[e][:, j0:j1], gates[:, c0 + j0 : c0 + j1], ALU.mult)
+            else:
+                nc.vector.tensor_copy(window[:].indirect(slots(c0 + j0, c0 + j1)), yv[e][:, j0:j1])
+
+        def add(b, b0, c0, c1):
+            nc.vector.tensor_tensor(res[:, c0:c1], banks[b][:, b0 : b0 + c1 - c0], window[:, c0:c1], ALU.add)
+
+        def store(q, c0, c1):
+            queue[q].dma_start(out=out[:, c0:c1], in_=res[:, c0:c1])
+
+        def warm(n):
+            for j in range(n):
+                nc.tensor.transpose(banks[7][:, (j % 4) * P : (j % 4 + 1) * P], ident[:], ident[:])
+
+        zero_plane("V", w2s)
+        nc.sync.dma_start(offsets[:], offs)
+        zero_plane("V", xs)
+        engine["V"].memset(ident[:], 0.0)
+        load_xs("Q", 2)
+        load_x("Q", 0, 0, 256)
+        load_xs("Q", 0)
+        load_xs("S", 3)
+        zero_plane("V", w1s[0])
+        load_w1s("Q", 0, 2, 3, 2)
+        load_xs("S", 1)
+        load_w1s("Q", 0, 2, 3, 0)
+        load_w1("S", 2, 0, 1)
+        gather_scales(0, 0, 256)
+        load_w1s("Q", 0, 2, 3, 1)
+        nc.vector.memset(zero[:], 0.0)
+        zero_plane("V", w1s[1])
+        gather_scales(2, 0, 256)
+        load_w1s("S", 0, 2, 3, 3)
+        load_x("Q", 1, 0, 256)
+        load_w1("Q", 2, 1, 3)
+        load_x("Q", 0, 256, 768)
+        load_x("S", 2, 0, 256)
+        load_w1s("S", 1, 0, 2, 2)
+        layer1(1, 0, 0)
+        load_x("Q", 1, 256, 768)
+        layer1(0, 0, 0)
+        gather_scales(0, 256, 512)
+        load_w1("S", 1, 0, 3)
+        load_w2s("S", 2)
+        load_x("S", 2, 256, 768)
+        layer1(1, 0, 1)
+        load_w1s("S", 1, 0, 2, 0)
+        gather_words(1, 0, 256)
+        load_w1s("Q", 1, 0, 2, 3)
+        layer1(0, 0, 1)
+        load_w2("Q")
+        load_w1("Q", 0, 0, 3)
+        layer1(0, 1, 0)
+        load_w1s("Q", 1, 0, 2, 1)
+        layer1(1, 1, 0)
+        gather_scales(1, 0, 256)
+        layer1(0, 1, 1)
+        load_w2s("Q", 3)
+        gather_words(0, 256, 512)
+        nc.scalar.activation(window[:], zero[:].to_broadcast([P, T]), ACT.Relu)
+        gather_words(2, 256, 512)
+        gather_words(0, 0, 256)
+        layer1(0, 0, 2)
+        load_w2s("S", 0)
+        load_w2s("Q", 1)
+        make_identity(nc, ident[:], nomemset=True)
+        layer1(1, 0, 2)
+        gather_scales(2, 256, 512)
+        gather_scales(1, 256, 512)
+        load_gate("S")
+        layer1(0, 1, 2)
+        relu("S", 0, 0)
+        gather_words(2, 0, 256)
+        turn2(0, 0)
+        relu("S", 0, 1)
+        relu("S", 1, 0)
+        layer1(1, 1, 1)
+        turn2(1, 0)
+        layer1(1, 1, 2)
+        turn2(0, 1)
+        layer1(2, 0, 0)
+        square2(1, 0)
+        relu("S", 1, 1)
+        layer1(2, 0, 1)
+        square2(0, 1)
+        square2(0, 0)
+        turn2(1, 1)
+        layer1(2, 0, 2)
+        layer1(2, 1, 0)
+        relu("V", 2, 0)
+        layer1(2, 1, 1)
+        layer1(2, 1, 2)
+        turn2(2, 0)
+        gather_words(1, 256, 512)
+        relu("S", 2, 1)
+        turn2(2, 1)
+        layer1(3, 0, 0)
+        square2(2, 0)
+        square2(2, 1)
+        square2(1, 1)
+        layer1(3, 0, 1)
+        layer1(3, 0, 2)
+        quantize(2, 0, 256)
+        layer1(4, 1, 0)
+        quantize(0, 0, 256)
+        relu("V", 3, 0)
+        turn2(3, 0)
+        square2(3, 0)
+        layer2(2, 0, 256)
+        quantize(3, 0, 128)
+        layer1(3, 1, 0)
+        leave_y("d", 2, 0, 256)
+        layer1(3, 1, 1)
+        layer2(3, 0, 128)
+        scatter("d", 2, 0, 256)
+        layer1(3, 1, 2)
+        relu("V", 3, 1)
+        turn2(3, 1)
+        layer1(4, 0, 0)
+        square2(3, 1)
+        layer1(4, 0, 1)
+        layer1(4, 0, 2)
+        relu("S", 4, 0)
+        quantize(3, 128, 256)
+        turn2(4, 0)
+        leave_y("d", 3, 0, 128)
+        square2(4, 0)
+        quantize(4, 0, 128)
+        layer2(4, 0, 128)
+        scatter("d", 3, 0, 128)
+        layer1(4, 1, 1)
+        layer2(3, 128, 256)
+        layer1(4, 1, 2)
+        relu("S", 4, 1)
+        turn2(4, 1)
+        square2(4, 1)
+        quantize(4, 128, 256)
+        quantize(1, 0, 256)
+        leave_y("d", 3, 128, 256)
+        layer2(0, 0, 256)
+        layer2(4, 128, 256)
+        layer2(1, 0, 256)
+        scatter("d", 3, 128, 256)
+        add(3, 0, 0, 512)
+        add(0, 0, 512, 768)
+        store("Q", 512, 768)
+        store("S", 0, 512)

@@ -23,12 +23,14 @@ SHARED = E
 UNIT = 256
 BANK = 512
 UNITS = [(2, 0), (2, 256), (0, 0), (1, 256), (2, 512)]
-MODE = [2, 2, 2, 2, 2]
-L1_BANK = [[0, 1], [2, 3], [0, 1], [2, 3], [0, 1]]
-T_BANK = [[4, 5], [6, 4], [5, 6], [4, 5], [6, 4]]
-Y_BANK = [(3, 0), (3, 256), (7, 0), (7, 256), (0, 0)]
+MODE = [1, 1, 2, 2, 2]
+L1_BANK = [[1, 5], [4, 3], [7, 6], [0, 4], [6, 7]]
+T_BANK = [[7, 7], [4, 4], [1, 2], [3, 3], [1, 3]]
+Y_BANK = [[(6, 0), (6, 0)], [(6, 256), (6, 256)], [(1, 0), (0, 0)], [(5, 0), (5, 0)], [(7, 0), (7, 0)]]
 W1S_GROUPS = [1, 2]
 W1S_ORDER = [2, 0, 1]
+NBANKS = 8
+WARM_BANK = 6
 
 
 def tile_moe_shr_mlp_relu2_kernel(
@@ -42,7 +44,8 @@ def tile_moe_shr_mlp_relu2_kernel(
         engine = {"V": nc.vector, "G": nc.gpsimd}
 
         offsets = keep.tile([P, E * C // 16], U16, name="offsets")
-        xw = [keep.tile([P, T], I32, name="xw%d" % o, align_bytes=64) for o in range(PASSES)]
+        xw_all = keep.tile([P, PASSES, T], I32, name="xw", align_bytes=64)
+        xw = [xw_all[:, o, :] for o in range(PASSES)]
         xs = keep.tile([P, PASSES, T], U8, name="xs", align_bytes=64)
         w1w = [keep.tile([P, PASSES, 2 * H], U8, name="w1w%d" % e, align_bytes=64) for e in range(E + 1)]
         w1s = [keep.tile([P, n * PASSES, H], U8, name="w1s%d" % j, align_bytes=64) for j, n in enumerate(W1S_GROUPS)]
@@ -54,13 +57,16 @@ def tile_moe_shr_mlp_relu2_kernel(
         window = keep.tile([P, T], F32, name="window")
         gw = [keep.tile([P, E * C], U32, name="gw%d" % o, align_bytes=64) for o in range(PASSES)]
         gs = [keep.tile([P, E * C], U8, name="gs%d" % o, align_bytes=64) for o in range(PASSES)]
-        banks = [psum.tile([P, BANK], F32, name="bank%d" % b) for b in range(8)]
+        banks = [psum.tile([P, BANK], F32, name="bank%d" % b) for b in range(NBANKS)]
         relus = [[keep.tile([P, H], F32, name="r%d_%d" % (k, a)) for a in range(2)] for k in range(5)]
         hidden = [keep.tile([P, 2, H], BF16, name="h%d" % k, align_bytes=64) for k in range(5)]
         grouped = [keep.tile([P, 4 * UNIT], BF16, name="g%d" % k, align_bytes=64) for k in range(5)]
         hw = [keep.tile([P, UNIT], U32, name="hw%d" % k, align_bytes=64) for k in range(5)]
         hs = [keep.tile([P, UNIT], U8, name="hs%d" % k, align_bytes=64) for k in range(5)]
         yv = [keep.tile([P, C], F32, name="yv%d" % e) for e in range(E)]
+        idle = keep.tile([P, 4 * BANK], BF16, name="idle", align_bytes=64)
+        idle_w = keep.tile([P, BANK], U32, name="idle_w", align_bytes=64)
+        idle_s = keep.tile([P, BANK], U8, name="idle_s", align_bytes=64)
         res = keep.tile([P, T], F32, name="res")
 
         def w1_plane(e, o):
@@ -90,6 +96,10 @@ def tile_moe_shr_mlp_relu2_kernel(
             words = x_words[o].rearrange("p t r -> p (t r)").bitcast(I32)
             queue[q].dma_start(out=xw[o][:, c0:c1], in_=words[:, c0:c1])
 
+        def load_xa(q, o0, o1, c0, c1):
+            words = x_words[o0:o1].rearrange("o p t r -> p o (t r)").bitcast(I32)
+            queue[q].dma_start(out=xw_all[:, o0:o1, c0:c1], in_=words[:, :, c0:c1])
+
         def load_w1(q, e, s0, s1):
             queue[q].dma_start(
                 out=w1w[e][:, s0:s1, :].bitcast(I32),
@@ -109,7 +119,7 @@ def tile_moe_shr_mlp_relu2_kernel(
             nc.vector.tensor_copy(gs[o][:, j0:j1], xs[:, o, :].indirect(slots(j0, j1)))
 
         def gather_words(o, j0, j1):
-            nc.vector.tensor_copy(gw[o][:, j0:j1], xw[o][:].bitcast(U32).indirect(slots(j0, j1)))
+            nc.vector.tensor_copy(gw[o][:, j0:j1], xw[o].bitcast(U32).indirect(slots(j0, j1)))
 
         def layer1(k, a, o):
             e, c0 = UNITS[k]
@@ -129,7 +139,7 @@ def tile_moe_shr_mlp_relu2_kernel(
             )
 
         def relu(eng, k, a):
-            if MODE[k] == 1:
+            if MODE[k] != 2:
                 src = banks[L1_BANK[k][a]][:].rearrange("t (p u e) -> t u p e", u=2, e=2)
                 dst = relus[k][a][:].rearrange("t (u p e) -> t u p e", u=2, e=2)
             else:
@@ -151,11 +161,19 @@ def tile_moe_shr_mlp_relu2_kernel(
             words = hidden[k][:, a, :].bitcast(F32)
             for u in range(2):
                 j = 2 * a + u
-                nc.tensor.transpose(banks[T_BANK[k][0]][:, j * P : (j + 1) * P], words[:, u * P : (u + 1) * P], ident[:])
+                nc.tensor.transpose(banks[T_BANK[k][a]][:, j * P : (j + 1) * P], words[:, u * P : (u + 1) * P], ident[:])
 
         def leave1(eng, k):
             src = banks[T_BANK[k][0]][:].rearrange("p (a u t) -> p a t u", a=2, u=2)
             dst = grouped[k][:].bitcast(F32).rearrange("p (a t u) -> p a t u", a=2, u=2)
+            if eng == "S":
+                nc.scalar.copy(dst, src)
+            else:
+                nc.vector.tensor_copy(dst, src)
+
+        def leave3(eng, k, a):
+            src = banks[T_BANK[k][a]][:, 2 * a * P : 2 * (a + 1) * P].rearrange("p (u t) -> p t u", u=2)
+            dst = grouped[k][:, a * H : (a + 1) * H].bitcast(F32).rearrange("p (t u) -> p t u", u=2)
             if eng == "S":
                 nc.scalar.copy(dst, src)
             else:
@@ -174,7 +192,7 @@ def tile_moe_shr_mlp_relu2_kernel(
             nc.vector.quantize_mx(out=hw[k][:, c0:c1].bitcast(FP8X4), scales=hs[k][:, c0:c1], in_=grouped[k][:, 4 * c0 : 4 * c1])
 
         def y_of(k, c0, c1):
-            b, first = Y_BANK[k]
+            b, first = Y_BANK[k][c0 // P]
             return banks[b][:, first + c0 : first + c1]
 
         def layer2(k, c0, c1):
@@ -209,140 +227,169 @@ def tile_moe_shr_mlp_relu2_kernel(
         def store(q, c0, c1):
             queue[q].dma_start(out=out[:, c0:c1], in_=res[:, c0:c1])
 
+        def warm_prepare():
+            nc.vector.memset(idle[:].bitcast(I32), 0)
+
+        def warm_quantize():
+            nc.vector.quantize_mx(out=idle_w[:].bitcast(FP8X4), scales=idle_s[:], in_=idle[:])
+
+        def warm2(n):
+            for j in range(n):
+                nc.tensor.matmul_mx(
+                    out=banks[WARM_BANK][:],
+                    lhsT=w2w[:, 0, :].bitcast(FP4X4),
+                    lhsT_scale=idle_s[:, 0:P],
+                    rhs=idle_w[:].bitcast(FP8X4),
+                    rhs_scale=idle_s[:],
+                    start=True,
+                    stop=True,
+                )
+
         def warm(n):
             for j in range(n):
-                nc.tensor.transpose(banks[7][:, (j % 4) * P : (j % 4 + 1) * P], ident[:], ident[:])
+                nc.tensor.matmul_mx(
+                    out=banks[WARM_BANK][:],
+                    lhsT=xw[0][:, 0:P].bitcast(FP8X4),
+                    lhsT_scale=xs[:, 0, 0:P],
+                    rhs=w1w[SHARED][:, 0, :].bitcast(FP4X4),
+                    rhs_scale=xs[:, 0, 0:H],
+                    start=True,
+                    stop=True,
+                )
 
-        zero_plane("V", w2s)
-        nc.sync.dma_start(offsets[:], offs)
         zero_plane("V", xs)
-        engine["V"].memset(ident[:], 0.0)
-        load_xs("Q", 2)
-        load_x("Q", 0, 0, 256)
-        load_xs("Q", 0)
-        load_xs("S", 3)
+        load_w1("Q", 2, 0, 1)
+        nc.sync.dma_start(offsets[:], offs)
         zero_plane("V", w1s[0])
-        load_w1s("Q", 0, 2, 3, 2)
-        load_xs("S", 1)
-        load_w1s("Q", 0, 2, 3, 0)
-        load_w1("S", 2, 0, 1)
-        gather_scales(0, 0, 256)
-        load_w1s("Q", 0, 2, 3, 1)
-        nc.vector.memset(zero[:], 0.0)
+        load_x("Q", 0, 0, 768)
+        load_xs("Q", 0)
         zero_plane("V", w1s[1])
-        gather_scales(2, 0, 256)
-        load_w1s("S", 0, 2, 3, 3)
-        load_x("Q", 1, 0, 256)
-        load_w1("Q", 2, 1, 3)
-        load_x("Q", 0, 256, 768)
-        load_x("S", 2, 0, 256)
-        load_w1s("S", 1, 0, 2, 2)
-        layer1(1, 0, 0)
+        load_xs("Q", 1)
+        gather_words(0, 0, 512)
+        load_xs("Q", 3)
+        engine["V"].memset(ident[:], 0.0)
+        load_w1s("Q", 0, 2, 3, 2)
+        load_xs("Q", 2)
         load_x("Q", 1, 256, 768)
-        layer1(0, 0, 0)
-        gather_scales(0, 256, 512)
-        load_w1("S", 1, 0, 3)
-        load_w2s("S", 2)
-        load_x("S", 2, 256, 768)
-        layer1(1, 0, 1)
-        load_w1s("S", 1, 0, 2, 0)
-        gather_words(1, 0, 256)
+        load_w1s("Q", 0, 2, 3, 3)
+        load_w1s("Q", 0, 2, 3, 0)
+        load_w1s("Q", 0, 2, 3, 1)
+        load_w1("Q", 2, 1, 3)
+        load_w1s("Q", 1, 0, 2, 2)
+        load_x("Q", 2, 256, 768)
+        load_xa("Q", 1, 3, 0, 256)
         load_w1s("Q", 1, 0, 2, 3)
-        layer1(0, 0, 1)
-        load_w2("Q")
-        load_w1("Q", 0, 0, 3)
+        load_w1s("Q", 1, 0, 2, 0)
+        gather_scales(0, 0, 512)
         layer1(0, 1, 0)
         load_w1s("Q", 1, 0, 2, 1)
-        layer1(1, 1, 0)
-        gather_scales(1, 0, 256)
+        load_w1("Q", 0, 0, 3)
+        gather_scales(1, 0, 512)
+        warm(3)
+        gather_scales(2, 0, 512)
+        gather_words(1, 0, 256)
         layer1(0, 1, 1)
-        load_w2s("Q", 3)
-        gather_words(0, 256, 512)
-        nc.scalar.activation(window[:], zero[:].to_broadcast([P, T]), ACT.Relu)
-        gather_words(2, 256, 512)
-        gather_words(0, 0, 256)
-        layer1(0, 0, 2)
-        load_w2s("S", 0)
-        load_w2s("Q", 1)
-        make_identity(nc, ident[:], nomemset=True)
-        layer1(1, 0, 2)
-        gather_scales(2, 256, 512)
-        gather_scales(1, 256, 512)
-        load_gate("S")
+        load_w1("Q", 1, 0, 3)
         layer1(0, 1, 2)
-        relu("S", 0, 0)
         gather_words(2, 0, 256)
-        turn2(0, 0)
-        relu("S", 0, 1)
-        relu("S", 1, 0)
-        layer1(1, 1, 1)
-        turn2(1, 0)
-        layer1(1, 1, 2)
-        turn2(0, 1)
-        layer1(2, 0, 0)
-        square2(1, 0)
-        relu("S", 1, 1)
-        layer1(2, 0, 1)
-        square2(0, 1)
-        square2(0, 0)
-        turn2(1, 1)
-        layer1(2, 0, 2)
-        layer1(2, 1, 0)
-        relu("V", 2, 0)
-        layer1(2, 1, 1)
-        layer1(2, 1, 2)
-        turn2(2, 0)
+        layer1(0, 0, 0)
+        layer1(1, 0, 0)
+        nc.vector.memset(zero[:], 0.0)
         gather_words(1, 256, 512)
-        relu("S", 2, 1)
-        turn2(2, 1)
+        load_w2("Q")
+        layer1(1, 0, 1)
+        layer1(2, 0, 0)
+        layer1(2, 1, 0)
+        layer1(2, 0, 1)
+        layer1(0, 0, 1)
+        layer1(0, 0, 2)
+        relu("S", 0, 0)
+        zero_plane("V", w2s)
+        layer1(2, 1, 1)
+        layer1(1, 1, 0)
+        layer1(2, 0, 2)
+        layer1(1, 1, 1)
+        square1("S", 0, 0)
         layer1(3, 0, 0)
+        make_identity(nc, ident[:], nomemset=True)
+        layer1(2, 1, 2)
+        relu("S", 2, 0)
+        layer1(1, 1, 2)
+        turn2(2, 0)
+        gather_words(2, 256, 512)
         square2(2, 0)
-        square2(2, 1)
-        square2(1, 1)
+        relu("V", 0, 1)
+        layer1(1, 0, 2)
+        relu("S", 2, 1)
+        relu("S", 1, 1)
+        turn1(0, 0)
+        load_w2s("Q", 3)
         layer1(3, 0, 1)
         layer1(3, 0, 2)
-        quantize(2, 0, 256)
-        layer1(4, 1, 0)
-        quantize(0, 0, 256)
-        relu("V", 3, 0)
+        square1("V", 0, 1)
+        turn2(2, 1)
+        quantize(2, 0, 128)
+        turn1(0, 1)
+        relu("S", 3, 0)
         turn2(3, 0)
-        square2(3, 0)
-        layer2(2, 0, 256)
-        quantize(3, 0, 128)
+        square2(2, 1)
+        relu("S", 1, 0)
+        nc.scalar.activation(window[:], zero[:].to_broadcast([P, T]), ACT.Relu)
         layer1(3, 1, 0)
-        leave_y("d", 2, 0, 256)
         layer1(3, 1, 1)
-        layer2(3, 0, 128)
-        scatter("d", 2, 0, 256)
+        quantize(2, 128, 256)
+        load_w2s("Q", 1)
         layer1(3, 1, 2)
-        relu("V", 3, 1)
-        turn2(3, 1)
+        square1("V", 1, 0)
+        load_w2s("Q", 2)
+        load_gate("Q")
+        load_w2s("Q", 0)
         layer1(4, 0, 0)
-        square2(3, 1)
+        layer2(2, 0, 128)
         layer1(4, 0, 1)
+        relu("V", 3, 1)
+        leave1("V", 0)
         layer1(4, 0, 2)
-        relu("S", 4, 0)
-        quantize(3, 128, 256)
-        turn2(4, 0)
-        leave_y("d", 3, 0, 128)
-        square2(4, 0)
-        quantize(4, 0, 128)
-        layer2(4, 0, 128)
-        scatter("d", 3, 0, 128)
+        square2(3, 0)
+        layer2(2, 128, 256)
+        quantize(0, 0, 256)
+        layer1(4, 1, 0)
         layer1(4, 1, 1)
-        layer2(3, 128, 256)
+        quantize(3, 0, 128)
+        leave_y("d", 2, 0, 128)
         layer1(4, 1, 2)
+        relu("S", 4, 0)
+        turn2(3, 1)
+        layer2(3, 0, 128)
+        leave_y("d", 2, 128, 256)
+        square2(3, 1)
+        turn1(1, 0)
+        turn2(4, 0)
+        square1("V", 1, 1)
+        leave_y("d", 3, 0, 128)
+        turn1(1, 1)
+        quantize(3, 128, 256)
+        layer2(3, 128, 256)
         relu("S", 4, 1)
+        leave_y("d", 3, 128, 256)
         turn2(4, 1)
         square2(4, 1)
+        leave1("S", 1)
+        scatter("d", 2, 0, 128)
+        scatter("d", 2, 128, 256)
+        scatter("d", 3, 0, 128)
+        scatter("d", 3, 128, 256)
+        square2(4, 0)
         quantize(4, 128, 256)
         quantize(1, 0, 256)
-        leave_y("d", 3, 128, 256)
+        quantize(4, 0, 128)
         layer2(0, 0, 256)
+        layer2(4, 0, 128)
         layer2(4, 128, 256)
         layer2(1, 0, 256)
-        scatter("d", 3, 128, 256)
-        add(3, 0, 0, 512)
-        add(0, 0, 512, 768)
-        store("Q", 512, 768)
-        store("S", 0, 512)
+        add(7, 0, 512, 640)
+        add(7, 128, 640, 768)
+        add(6, 0, 0, 512)
+        store("Q", 0, 512)
+        store("Q", 512, 640)
+        store("Q", 640, 768)

@@ -23,14 +23,14 @@ SHARED = E
 UNIT = 256
 BANK = 512
 UNITS = [(2, 0), (2, 256), (0, 0), (1, 256), (2, 512)]
-MODE = [1, 1, 2, 2, 2]
-L1_BANK = [[1, 5], [4, 3], [7, 6], [0, 4], [6, 7]]
-T_BANK = [[7, 7], [4, 4], [1, 2], [3, 3], [1, 3]]
-Y_BANK = [[(6, 0), (6, 0)], [(6, 256), (6, 256)], [(1, 0), (0, 0)], [(5, 0), (5, 0)], [(7, 0), (7, 0)]]
+MODE = [1, 1, 3, 3, 3]
+L1_BANK = [[0, 1], [3, 4], [2, 5], [7, 6], [5, 6]]
+T_BANK = [[2, 2], [0, 0], [4, 1], [0, 4], [7, 6]]
+Y_BANK = [[(4, 0), (4, 0)], [(4, 256), (4, 256)], [(3, 0), (3, 0)], [(5, 0), (5, 0)], [(2, 0), (2, 0)]]
 W1S_GROUPS = [1, 2]
 W1S_ORDER = [2, 0, 1]
 NBANKS = 8
-WARM_BANK = 6
+WARM_BANK = 2
 
 
 def tile_moe_shr_mlp_relu2_kernel(
@@ -257,139 +257,145 @@ def tile_moe_shr_mlp_relu2_kernel(
                     stop=True,
                 )
 
-        zero_plane("V", xs)
-        load_w1("Q", 2, 0, 1)
-        nc.sync.dma_start(offsets[:], offs)
         zero_plane("V", w1s[0])
-        load_x("Q", 0, 0, 768)
-        load_xs("Q", 0)
+        load_w1("Q", 2, 0, 1)
+        zero_plane("V", xs)
         zero_plane("V", w1s[1])
+        nc.sync.dma_start(offsets[:], offs)
+        load_x("Q", 0, 0, 768)
+        load_xs("Q", 2)
+        load_w1s("Q", 0, 2, 3, 3)
+        load_xs("Q", 0)
         load_xs("Q", 1)
-        gather_words(0, 0, 512)
         load_xs("Q", 3)
+        load_w1("Q", 2, 1, 3)
+        nc.vector.memset(zero[:], 0.0)
+        load_xa("Q", 1, 3, 0, 256)
+        load_w1s("Q", 0, 2, 3, 1)
+        load_w1s("Q", 0, 2, 3, 0)
         engine["V"].memset(ident[:], 0.0)
         load_w1s("Q", 0, 2, 3, 2)
-        load_xs("Q", 2)
-        load_x("Q", 1, 256, 768)
-        load_w1s("Q", 0, 2, 3, 3)
-        load_w1s("Q", 0, 2, 3, 0)
-        load_w1s("Q", 0, 2, 3, 1)
-        load_w1("Q", 2, 1, 3)
-        load_w1s("Q", 1, 0, 2, 2)
-        load_x("Q", 2, 256, 768)
-        load_xa("Q", 1, 3, 0, 256)
-        load_w1s("Q", 1, 0, 2, 3)
-        load_w1s("Q", 1, 0, 2, 0)
-        gather_scales(0, 0, 512)
-        layer1(0, 1, 0)
-        load_w1s("Q", 1, 0, 2, 1)
-        load_w1("Q", 0, 0, 3)
-        gather_scales(1, 0, 512)
-        warm(3)
-        gather_scales(2, 0, 512)
-        gather_words(1, 0, 256)
-        layer1(0, 1, 1)
-        load_w1("Q", 1, 0, 3)
-        layer1(0, 1, 2)
-        gather_words(2, 0, 256)
         layer1(0, 0, 0)
-        layer1(1, 0, 0)
-        nc.vector.memset(zero[:], 0.0)
-        gather_words(1, 256, 512)
-        load_w2("Q")
-        layer1(1, 0, 1)
-        layer1(2, 0, 0)
-        layer1(2, 1, 0)
-        layer1(2, 0, 1)
         layer1(0, 0, 1)
+        gather_scales(0, 0, 512)
+        load_x("Q", 1, 256, 768)
+        warm(3)
+        load_x("Q", 2, 256, 768)
+        gather_words(0, 0, 512)
+        gather_scales(2, 0, 512)
+        load_w1("Q", 0, 0, 3)
+        load_w1s("Q", 1, 0, 2, 1)
+        load_w1s("Q", 1, 0, 2, 0)
+        gather_words(2, 0, 256)
+        load_w1s("Q", 1, 0, 2, 3)
         layer1(0, 0, 2)
-        relu("S", 0, 0)
-        zero_plane("V", w2s)
-        layer1(2, 1, 1)
+        layer1(1, 0, 0)
         layer1(1, 1, 0)
-        layer1(2, 0, 2)
+        load_w1s("Q", 1, 0, 2, 2)
+        layer1(2, 0, 0)
+        zero_plane("V", w2s)
+        layer1(2, 1, 0)
         layer1(1, 1, 1)
-        square1("S", 0, 0)
-        layer1(3, 0, 0)
-        make_identity(nc, ident[:], nomemset=True)
-        layer1(2, 1, 2)
-        relu("S", 2, 0)
+        layer1(0, 1, 0)
+        relu("S", 0, 0)
+        gather_scales(1, 0, 512)
+        gather_words(1, 0, 256)
+        layer1(2, 0, 1)
         layer1(1, 1, 2)
-        turn2(2, 0)
-        gather_words(2, 256, 512)
-        square2(2, 0)
-        relu("V", 0, 1)
-        layer1(1, 0, 2)
-        relu("S", 2, 1)
-        relu("S", 1, 1)
-        turn1(0, 0)
-        load_w2s("Q", 3)
-        layer1(3, 0, 1)
-        layer1(3, 0, 2)
-        square1("V", 0, 1)
-        turn2(2, 1)
-        quantize(2, 0, 128)
-        turn1(0, 1)
-        relu("S", 3, 0)
-        turn2(3, 0)
-        square2(2, 1)
-        relu("S", 1, 0)
-        nc.scalar.activation(window[:], zero[:].to_broadcast([P, T]), ACT.Relu)
-        layer1(3, 1, 0)
-        layer1(3, 1, 1)
-        quantize(2, 128, 256)
-        load_w2s("Q", 1)
-        layer1(3, 1, 2)
-        square1("V", 1, 0)
-        load_w2s("Q", 2)
+        layer1(0, 1, 1)
+        layer1(2, 1, 1)
+        gather_words(1, 256, 512)
+        layer1(2, 0, 2)
+        layer1(0, 1, 2)
+        square1("S", 0, 0)
+        load_w1("Q", 1, 0, 3)
         load_gate("Q")
-        load_w2s("Q", 0)
+        relu("S", 2, 0)
+        layer1(2, 1, 2)
+        relu("S", 0, 1)
+        layer1(3, 0, 0)
+        gather_words(2, 256, 512)
+        relu("S", 2, 1)
+        load_w2s("Q", 1)
+        square1("V", 2, 1)
+        layer1(1, 0, 1)
+        layer1(3, 0, 1)
+        load_w2("Q")
+        load_w2s("Q", 3)
+        layer1(1, 0, 2)
+        layer1(3, 0, 2)
+        load_w2s("Q", 2)
+        layer1(3, 1, 0)
         layer1(4, 0, 0)
-        layer2(2, 0, 128)
+        layer1(3, 1, 1)
+        relu("S", 1, 0)
         layer1(4, 0, 1)
+        layer1(3, 1, 2)
+        square1("V", 0, 1)
+        square1("V", 2, 0)
+        make_identity(nc, ident[:], nomemset=True)
+        relu("S", 1, 1)
+        load_w2s("Q", 0)
+        turn1(2, 0)
+        turn1(0, 0)
+        turn1(2, 1)
+        relu("S", 3, 0)
+        square1("S", 1, 1)
+        leave3("S", 2, 1)
+        square1("S", 3, 0)
+        leave3("V", 2, 0)
         relu("V", 3, 1)
-        leave1("V", 0)
-        layer1(4, 0, 2)
-        square2(3, 0)
-        layer2(2, 128, 256)
-        quantize(0, 0, 256)
+        turn1(3, 0)
+        turn1(0, 1)
         layer1(4, 1, 0)
+        square1("V", 1, 0)
+        square1("S", 3, 1)
+        layer1(4, 0, 2)
+        quantize(2, 0, 128)
+        layer2(2, 0, 128)
         layer1(4, 1, 1)
-        quantize(3, 0, 128)
-        leave_y("d", 2, 0, 128)
+        quantize(2, 128, 256)
         layer1(4, 1, 2)
         relu("S", 4, 0)
-        turn2(3, 1)
-        layer2(3, 0, 128)
-        leave_y("d", 2, 128, 256)
-        square2(3, 1)
+        leave1("S", 0)
+        leave3("V", 3, 0)
+        quantize(3, 0, 128)
         turn1(1, 0)
-        turn2(4, 0)
-        square1("V", 1, 1)
-        leave_y("d", 3, 0, 128)
-        turn1(1, 1)
-        quantize(3, 128, 256)
-        layer2(3, 128, 256)
         relu("S", 4, 1)
-        leave_y("d", 3, 128, 256)
-        turn2(4, 1)
-        square2(4, 1)
+        turn1(3, 1)
+        leave_y("e", 2, 0, 128)
+        quantize(0, 0, 256)
+        layer2(2, 128, 256)
+        nc.scalar.activation(window[:], zero[:].to_broadcast([P, T]), ACT.Relu)
+        leave3("S", 3, 1)
+        square1("S", 4, 1)
+        scatter("e", 2, 0, 128)
+        quantize(3, 128, 256)
+        layer2(3, 0, 128)
+        leave_y("e", 2, 128, 256)
+        turn1(1, 1)
+        leave_y("e", 3, 0, 128)
+        square1("S", 4, 0)
+        scatter("e", 2, 128, 256)
         leave1("S", 1)
-        scatter("d", 2, 0, 128)
-        scatter("d", 2, 128, 256)
-        scatter("d", 3, 0, 128)
-        scatter("d", 3, 128, 256)
-        square2(4, 0)
-        quantize(4, 128, 256)
+        turn1(4, 0)
+        layer2(3, 128, 256)
+        turn1(4, 1)
         quantize(1, 0, 256)
-        quantize(4, 0, 128)
         layer2(0, 0, 256)
+        leave3("S", 4, 0)
+        leave_y("e", 3, 128, 256)
+        leave3("S", 4, 1)
+        layer2(1, 0, 256)
+        scatter("e", 3, 0, 128)
+        scatter("e", 3, 128, 256)
+        quantize(4, 0, 128)
+        quantize(4, 128, 256)
         layer2(4, 0, 128)
         layer2(4, 128, 256)
-        layer2(1, 0, 256)
-        add(7, 0, 512, 640)
-        add(7, 128, 640, 768)
-        add(6, 0, 0, 512)
-        store("Q", 0, 512)
+        add(2, 0, 512, 640)
         store("Q", 512, 640)
+        add(4, 0, 0, 512)
+        add(2, 128, 640, 768)
         store("Q", 640, 768)
+        store("Q", 0, 512)

@@ -20,17 +20,20 @@ ALU = mybir.AluOpType
 P = 128
 PASSES = K // 512
 SHARED = E
-UNIT = 256
 BANK = 512
-UNITS = [(2, 0), (2, 256), (0, 0), (1, 256), (2, 512)]
-MODE = [1, 1, 3, 3, 3]
-L1_BANK = [[0, 1], [3, 4], [2, 5], [7, 6], [5, 6]]
-T_BANK = [[2, 2], [0, 0], [4, 1], [0, 4], [7, 6]]
-Y_BANK = [[(4, 0), (4, 0)], [(4, 256), (4, 256)], [(3, 0), (3, 0)], [(5, 0), (5, 0)], [(2, 0), (2, 0)]]
-W1S_GROUPS = [1, 2]
-W1S_ORDER = [2, 0, 1]
-NBANKS = 8
-WARM_BANK = 2
+WARM_PASSES = 3
+SCALAR, VECTOR = "scalar", "vector"
+
+S0, S1, R0, R1, S2 = range(5)
+UNIT = 2 * P
+UNITS = [(SHARED, 0), (SHARED, UNIT), (0, 0), (1, C), (SHARED, 2 * UNIT)]
+PAIR_UNITS = (S0, S1)
+
+LAYER1_BANK = [[1, 2], [5, 3], [6, 0], [1, 4], [7, 0]]
+TURN_BANK = [[6, 6], [0, 0], [7, 2], [5, 1], [2, 6]]
+LAYER2_BANK = [[2, 2], [2, 2], [3, 2], [3, 1], [4, 4]]
+LAYER2_FIRST = [0, UNIT, 0, 0, 0]
+WARM_BANK = 3
 
 
 def tile_moe_shr_mlp_relu2_kernel(
@@ -40,362 +43,308 @@ def tile_moe_shr_mlp_relu2_kernel(
     with ExitStack() as ctx:
         keep = ctx.enter_context(tc.tile_pool(name="keep", bufs=1))
         psum = ctx.enter_context(tc.psum_pool(name="psum", bufs=1))
-        queue = {"Q": nc.sync, "S": nc.scalar, "G": nc.gpsimd}
-        engine = {"V": nc.vector, "G": nc.gpsimd}
 
         offsets = keep.tile([P, E * C // 16], U16, name="offsets")
-        xw_all = keep.tile([P, PASSES, T], I32, name="xw", align_bytes=64)
-        xw = [xw_all[:, o, :] for o in range(PASSES)]
-        xs = keep.tile([P, PASSES, T], U8, name="xs", align_bytes=64)
-        w1w = [keep.tile([P, PASSES, 2 * H], U8, name="w1w%d" % e, align_bytes=64) for e in range(E + 1)]
-        w1s = [keep.tile([P, n * PASSES, H], U8, name="w1s%d" % j, align_bytes=64) for j, n in enumerate(W1S_GROUPS)]
-        w2w = keep.tile([P, E + 1, 2 * N], U8, name="w2w", align_bytes=64)
-        w2s = keep.tile([P, E + 1, N], U8, name="w2s", align_bytes=64)
+        x_codes = keep.tile([P, PASSES, T], I32, name="x_codes", align_bytes=64)
+        x_plane = keep.tile([P, PASSES, T], U8, name="x_plane", align_bytes=64)
+        w1_codes = [keep.tile([P, PASSES, 2 * H], U8, name="w1_codes%d" % e, align_bytes=64) for e in range(E + 1)]
+        w1_plane_shared = keep.tile([P, PASSES, H], U8, name="w1_plane_shared", align_bytes=64)
+        w1_plane_routed = keep.tile([P, E * PASSES, H], U8, name="w1_plane_routed", align_bytes=64)
+        w2_codes = keep.tile([P, E + 1, 2 * N], U8, name="w2_codes", align_bytes=64)
+        w2_plane = keep.tile([P, E + 1, N], U8, name="w2_plane", align_bytes=64)
         gates = keep.tile([P, E * C], F32, name="gates")
         ident = keep.tile([P, P], F32, name="ident")
         zero = keep.tile([P, 1], F32, name="zero")
         window = keep.tile([P, T], F32, name="window")
-        gw = [keep.tile([P, E * C], U32, name="gw%d" % o, align_bytes=64) for o in range(PASSES)]
-        gs = [keep.tile([P, E * C], U8, name="gs%d" % o, align_bytes=64) for o in range(PASSES)]
-        banks = [psum.tile([P, BANK], F32, name="bank%d" % b) for b in range(NBANKS)]
-        relus = [[keep.tile([P, H], F32, name="r%d_%d" % (k, a)) for a in range(2)] for k in range(5)]
-        hidden = [keep.tile([P, 2, H], BF16, name="h%d" % k, align_bytes=64) for k in range(5)]
-        grouped = [keep.tile([P, 4 * UNIT], BF16, name="g%d" % k, align_bytes=64) for k in range(5)]
-        hw = [keep.tile([P, UNIT], U32, name="hw%d" % k, align_bytes=64) for k in range(5)]
-        hs = [keep.tile([P, UNIT], U8, name="hs%d" % k, align_bytes=64) for k in range(5)]
-        yv = [keep.tile([P, C], F32, name="yv%d" % e) for e in range(E)]
-        idle = keep.tile([P, 4 * BANK], BF16, name="idle", align_bytes=64)
-        idle_w = keep.tile([P, BANK], U32, name="idle_w", align_bytes=64)
-        idle_s = keep.tile([P, BANK], U8, name="idle_s", align_bytes=64)
-        res = keep.tile([P, T], F32, name="res")
+        slot_codes = [keep.tile([P, E * C], U32, name="slot_codes%d" % o, align_bytes=64) for o in range(PASSES)]
+        slot_plane = [keep.tile([P, E * C], U8, name="slot_plane%d" % o, align_bytes=64) for o in range(PASSES)]
+        banks = [psum.tile([P, BANK], F32, name="bank%d" % b) for b in range(8)]
+        relus = [[keep.tile([P, H], F32, name="relu%d_%d" % (u, half)) for half in range(2)] for u in range(5)]
+        squares = {u: keep.tile([P, 2, H], BF16, name="squares%d" % u, align_bytes=64) for u in PAIR_UNITS}
+        h_values = [keep.tile([P, 4 * UNIT], BF16, name="h_values%d" % u, align_bytes=64) for u in range(5)]
+        h_codes = [keep.tile([P, UNIT], U32, name="h_codes%d" % u, align_bytes=64) for u in range(5)]
+        h_plane = [keep.tile([P, UNIT], U8, name="h_plane%d" % u, align_bytes=64) for u in range(5)]
+        slot_y = [keep.tile([P, C], F32, name="slot_y%d" % e) for e in range(E)]
+        result = keep.tile([P, T], F32, name="result")
 
-        def w1_plane(e, o):
-            first = 0
-            for j, n in enumerate(W1S_GROUPS):
-                if W1S_ORDER.index(e) < first + n:
-                    return w1s[j][:, (W1S_ORDER.index(e) - first) * PASSES + o, :]
-                first += n
+        routed_scales = w1_scales[0:E].rearrange("e s q i -> (e s) q i")
+        w2_scale_rows = w2_scales.rearrange("e s q n -> (e s) q n")
 
-        def zero_plane(eng, tile):
-            engine[eng].memset(tile[:].rearrange("p a b -> p (a b)").bitcast(I32), 0)
+        def zero_plane(plane):
+            nc.vector.memset(plane[:].rearrange("p a b -> p (a b)").bitcast(I32), 0)
 
-        def load_scales(q, plane, rows, r):
+        def load_scale_rows(plane, rows, r):
             by_row = rows.rearrange("a (q r) w -> r q a w", r=4)
-            queue[q].dma_start(out=plane[r:P:32, :, :].bitcast(I32), in_=by_row[r].bitcast(I32))
+            nc.sync.dma_start(out=plane[r:P:32, :, :].bitcast(I32), in_=by_row[r].bitcast(I32))
 
-        def load_xs(q, r):
-            load_scales(q, xs, x_scales, r)
-
-        def load_w1s(q, j, e0, e1, r):
-            load_scales(q, w1s[j], w1_scales[e0:e1].rearrange("e s q i -> (e s) q i"), r)
-
-        def load_w2s(q, r):
-            load_scales(q, w2s, w2_scales.rearrange("e s q n -> (e s) q n"), r)
-
-        def load_x(q, o, c0, c1):
+        def load_token_pass(o, cols):
             words = x_words[o].rearrange("p t r -> p (t r)").bitcast(I32)
-            queue[q].dma_start(out=xw[o][:, c0:c1], in_=words[:, c0:c1])
+            nc.sync.dma_start(out=x_codes[:, o, :][:, cols], in_=words[:, cols])
 
-        def load_xa(q, o0, o1, c0, c1):
-            words = x_words[o0:o1].rearrange("o p t r -> p o (t r)").bitcast(I32)
-            queue[q].dma_start(out=xw_all[:, o0:o1, c0:c1], in_=words[:, :, c0:c1])
+        def load_tokens(passes, cols):
+            words = x_words[passes].rearrange("o p t r -> p o (t r)").bitcast(I32)
+            nc.sync.dma_start(out=x_codes[:, passes, cols], in_=words[:, :, cols])
 
-        def load_w1(q, e, s0, s1):
-            queue[q].dma_start(
-                out=w1w[e][:, s0:s1, :].bitcast(I32),
-                in_=w1_words[e, s0:s1].rearrange("s p b -> p s b").bitcast(I32),
+        def load_w1(e, passes):
+            nc.sync.dma_start(
+                out=w1_codes[e][:, passes, :].bitcast(I32),
+                in_=w1_words[e, passes].rearrange("s p b -> p s b").bitcast(I32),
             )
 
-        def load_w2(q):
-            queue[q].dma_start(out=w2w[:].bitcast(I32), in_=w2_words.rearrange("e s p b -> p (e s) b").bitcast(I32))
+        def slots(cols):
+            return offsets[:, cols.start // 16 : cols.stop // 16]
 
-        def load_gate(q):
-            queue[q].dma_start(out=gates[:], in_=gate)
+        def gather_scales(o):
+            nc.vector.tensor_copy(slot_plane[o][:], x_plane[:, o, :].indirect(offsets[:]))
 
-        def slots(j0, j1):
-            return offsets[:, j0 // 16 : j1 // 16]
+        def gather_words(o, cols):
+            nc.vector.tensor_copy(slot_codes[o][:, cols], x_codes[:, o, :].bitcast(U32).indirect(slots(cols)))
 
-        def gather_scales(o, j0, j1):
-            nc.vector.tensor_copy(gs[o][:, j0:j1], xs[:, o, :].indirect(slots(j0, j1)))
+        def warm_up():
+            for repeat in range(WARM_PASSES):
+                nc.tensor.matmul_mx(
+                    out=banks[WARM_BANK][:],
+                    lhsT=x_codes[:, 0, :][:, 0:P].bitcast(FP8X4),
+                    lhsT_scale=x_plane[:, 0, 0:P],
+                    rhs=w1_codes[SHARED][:, 0, :].bitcast(FP4X4),
+                    rhs_scale=x_plane[:, 0, 0:H],
+                    start=True,
+                    stop=True,
+                )
 
-        def gather_words(o, j0, j1):
-            nc.vector.tensor_copy(gw[o][:, j0:j1], xw[o].bitcast(U32).indirect(slots(j0, j1)))
-
-        def layer1(k, a, o):
-            e, c0 = UNITS[k]
-            cols = slice(c0 + a * P, c0 + (a + 1) * P)
+        def layer1(u, half, o):
+            e, first = UNITS[u]
+            cols = slice(first + half * P, first + (half + 1) * P)
             if e == SHARED:
-                tok, tok_s = xw[o][:, cols], xs[:, o, cols]
+                codes, plane, w1_plane = x_codes[:, o, :][:, cols], x_plane[:, o, cols], w1_plane_shared[:, o, :]
             else:
-                tok, tok_s = gw[o][:, cols], gs[o][:, cols]
+                codes, plane, w1_plane = slot_codes[o][:, cols], slot_plane[o][:, cols], w1_plane_routed[:, e * PASSES + o, :]
             nc.tensor.matmul_mx(
-                out=banks[L1_BANK[k][a]][:],
-                lhsT=tok.bitcast(FP8X4),
-                lhsT_scale=tok_s,
-                rhs=w1w[e][:, o, :].bitcast(FP4X4),
-                rhs_scale=w1_plane(e, o),
+                out=banks[LAYER1_BANK[u][half]][:],
+                lhsT=codes.bitcast(FP8X4),
+                lhsT_scale=plane,
+                rhs=w1_codes[e][:, o, :].bitcast(FP4X4),
+                rhs_scale=w1_plane,
                 start=(o == 0),
                 stop=(o == PASSES - 1),
             )
 
-        def relu(eng, k, a):
-            if MODE[k] != 2:
-                src = banks[L1_BANK[k][a]][:].rearrange("t (p u e) -> t u p e", u=2, e=2)
-                dst = relus[k][a][:].rearrange("t (u p e) -> t u p e", u=2, e=2)
+        def relu(engine, u, half):
+            bank, relu_tile = banks[LAYER1_BANK[u][half]], relus[u][half]
+            if u in PAIR_UNITS:
+                src = bank[:].rearrange("t (p w e) -> t w p e", w=2, e=2)
+                dst = relu_tile[:].rearrange("t (w p e) -> t w p e", w=2, e=2)
             else:
-                src = banks[L1_BANK[k][a]][:].rearrange("t (p j) -> t j p", j=4)
-                dst = relus[k][a][:].rearrange("t (j p) -> t j p", j=4)
-            if eng == "S":
+                src = bank[:].rearrange("t (p r) -> t r p", r=4)
+                dst = relu_tile[:].rearrange("t (r p) -> t r p", r=4)
+            if engine == SCALAR:
                 nc.scalar.activation(dst, src, ACT.Relu)
             else:
                 nc.vector.tensor_scalar_max(dst, src, 0.0)
 
-        def square1(eng, k, a):
-            r = relus[k][a][:]
-            if eng == "S":
-                nc.scalar.activation(hidden[k][:, a, :], r, ACT.Square)
+        def square_pairs(engine, u, half):
+            values = relus[u][half][:]
+            if engine == SCALAR:
+                nc.scalar.activation(squares[u][:, half, :], values, ACT.Square)
             else:
-                engine[eng].tensor_tensor(hidden[k][:, a, :], r, r, ALU.mult)
+                nc.vector.tensor_tensor(squares[u][:, half, :], values, values, ALU.mult)
 
-        def turn1(k, a):
-            words = hidden[k][:, a, :].bitcast(F32)
-            for u in range(2):
-                j = 2 * a + u
-                nc.tensor.transpose(banks[T_BANK[k][a]][:, j * P : (j + 1) * P], words[:, u * P : (u + 1) * P], ident[:])
+        def turn_pairs(u, half):
+            words = squares[u][:, half, :].bitcast(F32)
+            for w in range(2):
+                j = 2 * half + w
+                nc.tensor.transpose(banks[TURN_BANK[u][half]][:, j * P : (j + 1) * P], words[:, w * P : (w + 1) * P], ident[:])
 
-        def leave1(eng, k):
-            src = banks[T_BANK[k][0]][:].rearrange("p (a u t) -> p a t u", a=2, u=2)
-            dst = grouped[k][:].bitcast(F32).rearrange("p (a t u) -> p a t u", a=2, u=2)
-            if eng == "S":
+        def interleave_pairs(engine, u):
+            src = banks[TURN_BANK[u][0]][:].rearrange("p (half w t) -> p half t w", half=2, w=2)
+            dst = h_values[u][:].bitcast(F32).rearrange("p (half t w) -> p half t w", half=2, w=2)
+            if engine == SCALAR:
                 nc.scalar.copy(dst, src)
             else:
                 nc.vector.tensor_copy(dst, src)
 
-        def leave3(eng, k, a):
-            src = banks[T_BANK[k][a]][:, 2 * a * P : 2 * (a + 1) * P].rearrange("p (u t) -> p t u", u=2)
-            dst = grouped[k][:, a * H : (a + 1) * H].bitcast(F32).rearrange("p (t u) -> p t u", u=2)
-            if eng == "S":
-                nc.scalar.copy(dst, src)
-            else:
-                nc.vector.tensor_copy(dst, src)
+        def turn_floats(u, half):
+            for r in range(4):
+                cols = slice(r * P, (r + 1) * P)
+                nc.tensor.transpose(banks[TURN_BANK[u][half]][:, cols], relus[u][half][:, cols], ident[:])
 
-        def turn2(k, a):
-            for j in range(4):
-                nc.tensor.transpose(banks[T_BANK[k][a]][:, j * P : (j + 1) * P], relus[k][a][:, j * P : (j + 1) * P], ident[:])
-
-        def square2(k, a):
-            src = banks[T_BANK[k][a]][:].rearrange("p (j t) -> p t j", j=4)
-            dst = grouped[k][:, a * H : (a + 1) * H].rearrange("p (t j) -> p t j", j=4)
+        def square_turned(u, half):
+            src = banks[TURN_BANK[u][half]][:].rearrange("p (r t) -> p t r", r=4)
+            dst = h_values[u][:, half * H : (half + 1) * H].rearrange("p (t r) -> p t r", r=4)
             nc.scalar.activation(dst, src, ACT.Square)
 
-        def quantize(k, c0, c1):
-            nc.vector.quantize_mx(out=hw[k][:, c0:c1].bitcast(FP8X4), scales=hs[k][:, c0:c1], in_=grouped[k][:, 4 * c0 : 4 * c1])
+        def quantize(u, cols):
+            nc.vector.quantize_mx(
+                out=h_codes[u][:, cols].bitcast(FP8X4),
+                scales=h_plane[u][:, cols],
+                in_=h_values[u][:, 4 * cols.start : 4 * cols.stop],
+            )
 
-        def y_of(k, c0, c1):
-            b, first = Y_BANK[k][c0 // P]
-            return banks[b][:, first + c0 : first + c1]
+        def layer2_sums(u, cols):
+            first = LAYER2_FIRST[u]
+            return banks[LAYER2_BANK[u][cols.start // P]][:, first + cols.start : first + cols.stop]
 
-        def layer2(k, c0, c1):
-            e = UNITS[k][0]
+        def layer2(u, cols):
+            e = UNITS[u][0]
             nc.tensor.matmul_mx(
-                out=y_of(k, c0, c1),
-                lhsT=w2w[:, e, :].bitcast(FP4X4),
-                lhsT_scale=w2s[:, e, :],
-                rhs=hw[k][:, c0:c1].bitcast(FP8X4),
-                rhs_scale=hs[k][:, c0:c1],
+                out=layer2_sums(u, cols),
+                lhsT=w2_codes[:, e, :].bitcast(FP4X4),
+                lhsT_scale=w2_plane[:, e, :],
+                rhs=h_codes[u][:, cols].bitcast(FP8X4),
+                rhs_scale=h_plane[u][:, cols],
                 start=True,
                 stop=True,
             )
 
-        def leave_y(form, k, j0, j1):
-            e, c0 = UNITS[k]
-            if form == "d":
-                nc.scalar.copy(yv[e][:, j0:j1], y_of(k, j0, j1))
-            else:
-                nc.vector.tensor_tensor(yv[e][:, j0:j1], y_of(k, j0, j1), gates[:, c0 + j0 : c0 + j1], ALU.mult)
+        def apply_gate(u, cols):
+            e, first = UNITS[u]
+            nc.vector.tensor_tensor(slot_y[e][:, cols], layer2_sums(u, cols), gates[:, first + cols.start : first + cols.stop], ALU.mult)
 
-        def scatter(form, k, j0, j1):
-            e, c0 = UNITS[k]
-            if form == "d":
-                nc.vector.tensor_tensor(window[:].indirect(slots(c0 + j0, c0 + j1)), yv[e][:, j0:j1], gates[:, c0 + j0 : c0 + j1], ALU.mult)
-            else:
-                nc.vector.tensor_copy(window[:].indirect(slots(c0 + j0, c0 + j1)), yv[e][:, j0:j1])
+        def scatter(u, cols):
+            e, first = UNITS[u]
+            nc.vector.tensor_copy(window[:].indirect(slots(slice(first + cols.start, first + cols.stop))), slot_y[e][:, cols])
 
-        def add(b, b0, c0, c1):
-            nc.vector.tensor_tensor(res[:, c0:c1], banks[b][:, b0 : b0 + c1 - c0], window[:, c0:c1], ALU.add)
+        def add_shared(u, cols):
+            first = UNITS[u][1]
+            sums = banks[LAYER2_BANK[u][0]][:, cols.start - first : cols.stop - first]
+            nc.vector.tensor_tensor(result[:, cols], sums, window[:, cols], ALU.add)
 
-        def store(q, c0, c1):
-            queue[q].dma_start(out=out[:, c0:c1], in_=res[:, c0:c1])
+        def store(cols):
+            nc.sync.dma_start(out=out[:, cols], in_=result[:, cols])
 
-        def warm_prepare():
-            nc.vector.memset(idle[:].bitcast(I32), 0)
-
-        def warm_quantize():
-            nc.vector.quantize_mx(out=idle_w[:].bitcast(FP8X4), scales=idle_s[:], in_=idle[:])
-
-        def warm2(n):
-            for j in range(n):
-                nc.tensor.matmul_mx(
-                    out=banks[WARM_BANK][:],
-                    lhsT=w2w[:, 0, :].bitcast(FP4X4),
-                    lhsT_scale=idle_s[:, 0:P],
-                    rhs=idle_w[:].bitcast(FP8X4),
-                    rhs_scale=idle_s[:],
-                    start=True,
-                    stop=True,
-                )
-
-        def warm(n):
-            for j in range(n):
-                nc.tensor.matmul_mx(
-                    out=banks[WARM_BANK][:],
-                    lhsT=xw[0][:, 0:P].bitcast(FP8X4),
-                    lhsT_scale=xs[:, 0, 0:P],
-                    rhs=w1w[SHARED][:, 0, :].bitcast(FP4X4),
-                    rhs_scale=xs[:, 0, 0:H],
-                    start=True,
-                    stop=True,
-                )
-
-        zero_plane("V", w1s[0])
-        load_w1("Q", 2, 0, 1)
-        zero_plane("V", xs)
-        zero_plane("V", w1s[1])
+        zero_plane(x_plane)
+        load_token_pass(0, slice(0, 768))
         nc.sync.dma_start(offsets[:], offs)
-        load_x("Q", 0, 0, 768)
-        load_xs("Q", 2)
-        load_w1s("Q", 0, 2, 3, 3)
-        load_xs("Q", 0)
-        load_xs("Q", 1)
-        load_xs("Q", 3)
-        load_w1("Q", 2, 1, 3)
+        zero_plane(w1_plane_routed)
+        load_scale_rows(x_plane, x_scales, 0)
+        load_scale_rows(x_plane, x_scales, 1)
+        load_scale_rows(x_plane, x_scales, 3)
+        load_w1(SHARED, slice(0, 1))
+        load_scale_rows(x_plane, x_scales, 2)
+        load_w1(SHARED, slice(1, 3))
+        zero_plane(w1_plane_shared)
+        nc.vector.memset(ident[:], 0.0)
+        zero_plane(w2_plane)
         nc.vector.memset(zero[:], 0.0)
-        load_xa("Q", 1, 3, 0, 256)
-        load_w1s("Q", 0, 2, 3, 1)
-        load_w1s("Q", 0, 2, 3, 0)
-        engine["V"].memset(ident[:], 0.0)
-        load_w1s("Q", 0, 2, 3, 2)
-        layer1(0, 0, 0)
-        layer1(0, 0, 1)
-        gather_scales(0, 0, 512)
-        load_x("Q", 1, 256, 768)
-        warm(3)
-        load_x("Q", 2, 256, 768)
-        gather_words(0, 0, 512)
-        gather_scales(2, 0, 512)
-        load_w1("Q", 0, 0, 3)
-        load_w1s("Q", 1, 0, 2, 1)
-        load_w1s("Q", 1, 0, 2, 0)
-        gather_words(2, 0, 256)
-        load_w1s("Q", 1, 0, 2, 3)
-        layer1(0, 0, 2)
-        layer1(1, 0, 0)
-        layer1(1, 1, 0)
-        load_w1s("Q", 1, 0, 2, 2)
-        layer1(2, 0, 0)
-        zero_plane("V", w2s)
-        layer1(2, 1, 0)
-        layer1(1, 1, 1)
-        layer1(0, 1, 0)
-        relu("S", 0, 0)
-        gather_scales(1, 0, 512)
-        gather_words(1, 0, 256)
-        layer1(2, 0, 1)
-        layer1(1, 1, 2)
-        layer1(0, 1, 1)
-        layer1(2, 1, 1)
-        gather_words(1, 256, 512)
-        layer1(2, 0, 2)
-        layer1(0, 1, 2)
-        square1("S", 0, 0)
-        load_w1("Q", 1, 0, 3)
-        load_gate("Q")
-        relu("S", 2, 0)
-        layer1(2, 1, 2)
-        relu("S", 0, 1)
-        layer1(3, 0, 0)
-        gather_words(2, 256, 512)
-        relu("S", 2, 1)
-        load_w2s("Q", 1)
-        square1("V", 2, 1)
-        layer1(1, 0, 1)
-        layer1(3, 0, 1)
-        load_w2("Q")
-        load_w2s("Q", 3)
-        layer1(1, 0, 2)
-        layer1(3, 0, 2)
-        load_w2s("Q", 2)
-        layer1(3, 1, 0)
-        layer1(4, 0, 0)
-        layer1(3, 1, 1)
-        relu("S", 1, 0)
-        layer1(4, 0, 1)
-        layer1(3, 1, 2)
-        square1("V", 0, 1)
-        square1("V", 2, 0)
         make_identity(nc, ident[:], nomemset=True)
-        relu("S", 1, 1)
-        load_w2s("Q", 0)
-        turn1(2, 0)
-        turn1(0, 0)
-        turn1(2, 1)
-        relu("S", 3, 0)
-        square1("S", 1, 1)
-        leave3("S", 2, 1)
-        square1("S", 3, 0)
-        leave3("V", 2, 0)
-        relu("V", 3, 1)
-        turn1(3, 0)
-        turn1(0, 1)
-        layer1(4, 1, 0)
-        square1("V", 1, 0)
-        square1("S", 3, 1)
-        layer1(4, 0, 2)
-        quantize(2, 0, 128)
-        layer2(2, 0, 128)
-        layer1(4, 1, 1)
-        quantize(2, 128, 256)
-        layer1(4, 1, 2)
-        relu("S", 4, 0)
-        leave1("S", 0)
-        leave3("V", 3, 0)
-        quantize(3, 0, 128)
-        turn1(1, 0)
-        relu("S", 4, 1)
-        turn1(3, 1)
-        leave_y("e", 2, 0, 128)
-        quantize(0, 0, 256)
-        layer2(2, 128, 256)
         nc.scalar.activation(window[:], zero[:].to_broadcast([P, T]), ACT.Relu)
-        leave3("S", 3, 1)
-        square1("S", 4, 1)
-        scatter("e", 2, 0, 128)
-        quantize(3, 128, 256)
-        layer2(3, 0, 128)
-        leave_y("e", 2, 128, 256)
-        turn1(1, 1)
-        leave_y("e", 3, 0, 128)
-        square1("S", 4, 0)
-        scatter("e", 2, 128, 256)
-        leave1("S", 1)
-        turn1(4, 0)
-        layer2(3, 128, 256)
-        turn1(4, 1)
-        quantize(1, 0, 256)
-        layer2(0, 0, 256)
-        leave3("S", 4, 0)
-        leave_y("e", 3, 128, 256)
-        leave3("S", 4, 1)
-        layer2(1, 0, 256)
-        scatter("e", 3, 0, 128)
-        scatter("e", 3, 128, 256)
-        quantize(4, 0, 128)
-        quantize(4, 128, 256)
-        layer2(4, 0, 128)
-        layer2(4, 128, 256)
-        add(2, 0, 512, 640)
-        store("Q", 512, 640)
-        add(4, 0, 0, 512)
-        add(2, 128, 640, 768)
-        store("Q", 640, 768)
-        store("Q", 0, 512)
+        load_scale_rows(w1_plane_shared, w1_scales[SHARED], 3)
+        gather_words(0, slice(0, 512))
+        load_scale_rows(w1_plane_shared, w1_scales[SHARED], 1)
+        load_scale_rows(w1_plane_shared, w1_scales[SHARED], 0)
+        load_scale_rows(w1_plane_shared, w1_scales[SHARED], 2)
+        load_tokens(slice(1, 3), slice(0, 256))
+        load_w1(0, slice(0, 3))
+        load_token_pass(1, slice(256, 768))
+        warm_up()
+        gather_scales(0)
+        load_token_pass(2, slice(256, 768))
+        load_scale_rows(w1_plane_routed, routed_scales, 0)
+        load_scale_rows(w1_plane_routed, routed_scales, 2)
+        load_scale_rows(w1_plane_routed, routed_scales, 3)
+        load_scale_rows(w1_plane_routed, routed_scales, 1)
+        gather_scales(1)
+        layer1(S0, 0, 0)
+        nc.sync.dma_start(out=gates[:], in_=gate)
+        layer1(S0, 1, 0)
+        layer1(S1, 0, 0)
+        gather_scales(2)
+        load_scale_rows(w2_plane, w2_scale_rows, 3)
+        layer1(S0, 0, 1)
+        layer1(S0, 0, 2)
+        load_w1(1, slice(0, 3))
+        layer1(S0, 1, 1)
+        layer1(S0, 1, 2)
+        relu(SCALAR, S0, 0)
+        load_scale_rows(w2_plane, w2_scale_rows, 2)
+        gather_words(1, slice(0, 256))
+        layer1(S1, 1, 0)
+        load_scale_rows(w2_plane, w2_scale_rows, 0)
+        nc.sync.dma_start(out=w2_codes[:].bitcast(I32), in_=w2_words.rearrange("e s p b -> p (e s) b").bitcast(I32))
+        layer1(S1, 0, 1)
+        load_scale_rows(w2_plane, w2_scale_rows, 1)
+        relu(SCALAR, S0, 1)
+        layer1(S1, 1, 1)
+        gather_words(1, slice(256, 512))
+        layer1(S1, 0, 2)
+        square_pairs(SCALAR, S0, 0)
+        layer1(S1, 1, 2)
+        gather_words(2, slice(0, 256))
+        layer1(R0, 1, 0)
+        square_pairs(SCALAR, S0, 1)
+        layer1(R0, 0, 0)
+        gather_words(2, slice(256, 512))
+        layer1(R0, 1, 1)
+        relu(SCALAR, S1, 0)
+        layer1(R0, 0, 1)
+        relu(VECTOR, S1, 1)
+        layer1(R0, 0, 2)
+        layer1(R0, 1, 2)
+        layer1(R1, 0, 0)
+        square_pairs(VECTOR, S1, 0)
+        relu(SCALAR, R0, 0)
+        layer1(R1, 0, 1)
+        layer1(R1, 0, 2)
+        square_pairs(VECTOR, S1, 1)
+        relu(SCALAR, R0, 1)
+        layer1(R1, 1, 0)
+        turn_floats(R0, 0)
+        relu(SCALAR, R1, 0)
+        turn_pairs(S0, 0)
+        turn_pairs(S0, 1)
+        square_turned(R0, 0)
+        turn_floats(R0, 1)
+        interleave_pairs(VECTOR, S0)
+        turn_floats(R1, 0)
+        square_turned(R0, 1)
+        layer1(R1, 1, 1)
+        quantize(R0, slice(0, 128))
+        quantize(S0, slice(0, 256))
+        layer1(S2, 1, 0)
+        square_turned(R1, 0)
+        layer1(R1, 1, 2)
+        quantize(R0, slice(128, 256))
+        layer2(R0, slice(0, 128))
+        layer1(S2, 1, 1)
+        relu(SCALAR, R1, 1)
+        layer1(S2, 1, 2)
+        quantize(R1, slice(0, 128))
+        layer1(S2, 0, 0)
+        apply_gate(R0, slice(0, 128))
+        layer1(S2, 0, 1)
+        relu(SCALAR, S2, 1)
+        scatter(R0, slice(0, 128))
+        layer1(S2, 0, 2)
+        layer2(R0, slice(128, 256))
+        turn_floats(R1, 1)
+        relu(SCALAR, S2, 0)
+        apply_gate(R0, slice(128, 256))
+        turn_pairs(S1, 0)
+        turn_pairs(S1, 1)
+        scatter(R0, slice(128, 256))
+        square_turned(R1, 1)
+        layer2(R1, slice(0, 128))
+        turn_floats(S2, 0)
+        interleave_pairs(SCALAR, S1)
+        apply_gate(R1, slice(0, 128))
+        turn_floats(S2, 1)
+        quantize(R1, slice(128, 256))
+        scatter(R1, slice(0, 128))
+        square_turned(S2, 0)
+        layer2(R1, slice(128, 256))
+        square_turned(S2, 1)
+        quantize(S1, slice(0, 256))
+        layer2(S0, slice(0, 256))
+        apply_gate(R1, slice(128, 256))
+        quantize(S2, slice(0, 128))
+        scatter(R1, slice(128, 256))
+        layer2(S1, slice(0, 256))
+        layer2(S2, slice(0, 128))
+        quantize(S2, slice(128, 256))
+        add_shared(S0, slice(0, 512))
+        layer2(S2, slice(128, 256))
+        store(slice(0, 512))
+        add_shared(S2, slice(512, 640))
+        add_shared(S2, slice(640, 768))
+        store(slice(512, 640))
+        store(slice(640, 768))

@@ -21,19 +21,12 @@ P = 128
 PASSES = K // 512
 SHARED = E
 BANK = 512
+SLOTS = E * C
 WARM_PASSES = 3
 SCALAR, VECTOR = "scalar", "vector"
-
-S0, S1, R0, R1, S2 = range(5)
-UNIT = 2 * P
-UNITS = [(SHARED, 0), (SHARED, UNIT), (0, 0), (1, C), (SHARED, 2 * UNIT)]
-PAIR_UNITS = (S0, S1)
-
-LAYER1_BANK = [[1, 2], [5, 3], [6, 0], [1, 4], [7, 0]]
-TURN_BANK = [[6, 6], [0, 0], [7, 2], [5, 1], [2, 6]]
-LAYER2_BANK = [[2, 2], [2, 2], [3, 2], [3, 1], [4, 4]]
-LAYER2_FIRST = [0, UNIT, 0, 0, 0]
-WARM_BANK = 3
+S0, S1, S2, S3, S4, S5, R0, R1, R2, R3 = range(10)
+SHARED_BLOCKS = T // P
+PAIR_BLOCKS = (S0, S1, S2, S3)
 
 
 def tile_moe_shr_mlp_relu2_kernel(
@@ -44,7 +37,7 @@ def tile_moe_shr_mlp_relu2_kernel(
         keep = ctx.enter_context(tc.tile_pool(name="keep", bufs=1))
         psum = ctx.enter_context(tc.psum_pool(name="psum", bufs=1))
 
-        offsets = keep.tile([P, E * C // 16], U16, name="offsets")
+        offsets = keep.tile([P, SLOTS // 16], U16, name="offsets")
         x_codes = keep.tile([P, PASSES, T], I32, name="x_codes", align_bytes=64)
         x_plane = keep.tile([P, PASSES, T], U8, name="x_plane", align_bytes=64)
         w1_codes = [keep.tile([P, PASSES, 2 * H], U8, name="w1_codes%d" % e, align_bytes=64) for e in range(E + 1)]
@@ -52,20 +45,26 @@ def tile_moe_shr_mlp_relu2_kernel(
         w1_plane_routed = keep.tile([P, E * PASSES, H], U8, name="w1_plane_routed", align_bytes=64)
         w2_codes = keep.tile([P, E + 1, 2 * N], U8, name="w2_codes", align_bytes=64)
         w2_plane = keep.tile([P, E + 1, N], U8, name="w2_plane", align_bytes=64)
-        gates = keep.tile([P, E * C], F32, name="gates")
+        gates = keep.tile([P, SLOTS], F32, name="gates")
         ident = keep.tile([P, P], F32, name="ident")
         zero = keep.tile([P, 1], F32, name="zero")
         window = keep.tile([P, T], F32, name="window")
-        slot_codes = [keep.tile([P, E * C], U32, name="slot_codes%d" % o, align_bytes=64) for o in range(PASSES)]
-        slot_plane = [keep.tile([P, E * C], U8, name="slot_plane%d" % o, align_bytes=64) for o in range(PASSES)]
+        slot_codes = [keep.tile([P, SLOTS], U32, name="slot_codes%d" % o, align_bytes=64) for o in range(PASSES)]
+        slot_plane = [keep.tile([P, SLOTS], U8, name="slot_plane%d" % o, align_bytes=64) for o in range(PASSES)]
         banks = [psum.tile([P, BANK], F32, name="bank%d" % b) for b in range(8)]
-        relus = [[keep.tile([P, H], F32, name="relu%d_%d" % (u, half)) for half in range(2)] for u in range(5)]
-        squares = {u: keep.tile([P, 2, H], BF16, name="squares%d" % u, align_bytes=64) for u in PAIR_UNITS}
-        h_values = [keep.tile([P, 4 * UNIT], BF16, name="h_values%d" % u, align_bytes=64) for u in range(5)]
-        h_codes = [keep.tile([P, UNIT], U32, name="h_codes%d" % u, align_bytes=64) for u in range(5)]
-        h_plane = [keep.tile([P, UNIT], U8, name="h_plane%d" % u, align_bytes=64) for u in range(5)]
-        slot_y = [keep.tile([P, C], F32, name="slot_y%d" % e) for e in range(E)]
-        result = keep.tile([P, T], F32, name="result")
+        relus = [keep.tile([P, H], F32, name="relu%d" % b) for b in range(10)]
+        squares = {b: keep.tile([P, H], BF16, name="squares%d" % b, align_bytes=64) for b in PAIR_BLOCKS}
+        h_values = keep.tile([P, 4 * (T + SLOTS)], BF16, name="h_values", align_bytes=64)
+        h_codes = keep.tile([P, T + SLOTS], U32, name="h_codes", align_bytes=64)
+        h_plane = keep.tile([P, T + SLOTS], U8, name="h_plane", align_bytes=64)
+        slot_y = keep.tile([P, SLOTS], F32, name="slot_y")
+        result_head = h_values[:, S4 * H : (S5 + 1) * H].bitcast(F32)
+        result_tail = keep.tile([P, 2 * P], F32, name="result_tail")
+
+        def result(b, count):
+            if b < S4:
+                return result_head[:, b * P : (b + count) * P]
+            return result_tail[:, (b - S4) * P : (b - S4 + count) * P]
 
         routed_scales = w1_scales[0:E].rearrange("e s q i -> (e s) q i")
         w2_scale_rows = w2_scales.rearrange("e s q n -> (e s) q n")
@@ -73,9 +72,10 @@ def tile_moe_shr_mlp_relu2_kernel(
         def zero_plane(plane):
             nc.vector.memset(plane[:].rearrange("p a b -> p (a b)").bitcast(I32), 0)
 
-        def load_scale_rows(plane, rows, r):
+        def load_scales(queue, plane, rows):
             by_row = rows.rearrange("a (q r) w -> r q a w", r=4)
-            nc.sync.dma_start(out=plane[r:P:32, :, :].bitcast(I32), in_=by_row[r].bitcast(I32))
+            for r in range(4):
+                queue.dma_start(out=plane[r:P:32, :, :].bitcast(I32), in_=by_row[r].bitcast(I32))
 
         def load_token_pass(o, cols):
             words = x_words[o].rearrange("p t r -> p (t r)").bitcast(I32)
@@ -91,36 +91,43 @@ def tile_moe_shr_mlp_relu2_kernel(
                 in_=w1_words[e, passes].rearrange("s p b -> p s b").bitcast(I32),
             )
 
+        def load_w2():
+            nc.sync.dma_start(out=w2_codes[:].bitcast(I32), in_=w2_words.rearrange("e s p b -> p (e s) b").bitcast(I32))
+
         def slots(cols):
             return offsets[:, cols.start // 16 : cols.stop // 16]
 
-        def gather_scales(o):
-            nc.vector.tensor_copy(slot_plane[o][:], x_plane[:, o, :].indirect(offsets[:]))
+        def gather_scales(o, cols):
+            nc.vector.tensor_copy(slot_plane[o][:, cols], x_plane[:, o, :].indirect(slots(cols)))
 
         def gather_words(o, cols):
             nc.vector.tensor_copy(slot_codes[o][:, cols], x_codes[:, o, :].bitcast(U32).indirect(slots(cols)))
 
-        def warm_up():
+        def warm_up(bank):
             for repeat in range(WARM_PASSES):
                 nc.tensor.matmul_mx(
-                    out=banks[WARM_BANK][:],
+                    out=banks[bank][:],
                     lhsT=x_codes[:, 0, :][:, 0:P].bitcast(FP8X4),
                     lhsT_scale=x_plane[:, 0, 0:P],
-                    rhs=w1_codes[SHARED][:, 0, :].bitcast(FP4X4),
+                    rhs=x_codes[:, 0, :][:, 0 : 2 * P].bitcast(FP4X4),
                     rhs_scale=x_plane[:, 0, 0:H],
                     start=True,
                     stop=True,
                 )
 
-        def layer1(u, half, o):
-            e, first = UNITS[u]
-            cols = slice(first + half * P, first + (half + 1) * P)
+        def expert_of(b):
+            return SHARED if b < SHARED_BLOCKS else (b - SHARED_BLOCKS) * P // C
+
+        def layer1_pass(b, bank, o):
+            e = expert_of(b)
             if e == SHARED:
+                cols = slice(b * P, (b + 1) * P)
                 codes, plane, w1_plane = x_codes[:, o, :][:, cols], x_plane[:, o, cols], w1_plane_shared[:, o, :]
             else:
+                cols = slice(b * P - T, (b + 1) * P - T)
                 codes, plane, w1_plane = slot_codes[o][:, cols], slot_plane[o][:, cols], w1_plane_routed[:, e * PASSES + o, :]
             nc.tensor.matmul_mx(
-                out=banks[LAYER1_BANK[u][half]][:],
+                out=banks[bank][:],
                 lhsT=codes.bitcast(FP8X4),
                 lhsT_scale=plane,
                 rhs=w1_codes[e][:, o, :].bitcast(FP4X4),
@@ -129,222 +136,172 @@ def tile_moe_shr_mlp_relu2_kernel(
                 stop=(o == PASSES - 1),
             )
 
-        def relu(engine, u, half):
-            bank, relu_tile = banks[LAYER1_BANK[u][half]], relus[u][half]
-            if u in PAIR_UNITS:
-                src = bank[:].rearrange("t (p w e) -> t w p e", w=2, e=2)
-                dst = relu_tile[:].rearrange("t (w p e) -> t w p e", w=2, e=2)
+        def layer1(b, bank):
+            for o in range(PASSES):
+                layer1_pass(b, bank, o)
+
+        def relu(engine, b, bank):
+            if b in PAIR_BLOCKS:
+                src = banks[bank][:].rearrange("t (p w e) -> t w p e", w=2, e=2)
+                dst = relus[b][:].rearrange("t (w p e) -> t w p e", w=2, e=2)
             else:
-                src = bank[:].rearrange("t (p r) -> t r p", r=4)
-                dst = relu_tile[:].rearrange("t (r p) -> t r p", r=4)
+                src = banks[bank][:].rearrange("t (p r) -> t r p", r=4)
+                dst = relus[b][:].rearrange("t (r p) -> t r p", r=4)
             if engine == SCALAR:
                 nc.scalar.activation(dst, src, ACT.Relu)
             else:
                 nc.vector.tensor_scalar_max(dst, src, 0.0)
 
-        def square_pairs(engine, u, half):
-            values = relus[u][half][:]
-            if engine == SCALAR:
-                nc.scalar.activation(squares[u][:, half, :], values, ACT.Square)
-            else:
-                nc.vector.tensor_tensor(squares[u][:, half, :], values, values, ALU.mult)
+        def turn(b, bank):
+            for r in range(4):
+                cols = slice(r * P, (r + 1) * P)
+                nc.tensor.transpose(banks[bank][:, cols], relus[b][:, cols], ident[:])
 
-        def turn_pairs(u, half):
-            words = squares[u][:, half, :].bitcast(F32)
+        def square(b, bank):
+            src = banks[bank][:].rearrange("p (r t) -> p t r", r=4)
+            dst = h_values[:, b * H : (b + 1) * H].rearrange("p (t r) -> p t r", r=4)
+            nc.scalar.activation(dst, src, ACT.Square)
+
+        def square_pairs(engine, b):
+            if engine == SCALAR:
+                nc.scalar.activation(squares[b][:], relus[b][:], ACT.Square)
+            else:
+                nc.vector.tensor_tensor(squares[b][:], relus[b][:], relus[b][:], ALU.mult)
+
+        def turn_pairs(b, bank, half):
+            words = squares[b][:].bitcast(F32)
             for w in range(2):
                 j = 2 * half + w
-                nc.tensor.transpose(banks[TURN_BANK[u][half]][:, j * P : (j + 1) * P], words[:, w * P : (w + 1) * P], ident[:])
+                nc.tensor.transpose(banks[bank][:, j * P : (j + 1) * P], words[:, w * P : (w + 1) * P], ident[:])
 
-        def interleave_pairs(engine, u):
-            src = banks[TURN_BANK[u][0]][:].rearrange("p (half w t) -> p half t w", half=2, w=2)
-            dst = h_values[u][:].bitcast(F32).rearrange("p (half t w) -> p half t w", half=2, w=2)
+        def interleave_pairs(engine, b, count, bank, half):
+            src = banks[bank][:, half * 2 * P : (half + count) * 2 * P].rearrange("p (h w t) -> p h t w", h=count, w=2)
+            dst = h_values[:, b * H : (b + count) * H].bitcast(F32).rearrange("p (h t w) -> p h t w", h=count, w=2)
             if engine == SCALAR:
                 nc.scalar.copy(dst, src)
             else:
                 nc.vector.tensor_copy(dst, src)
 
-        def turn_floats(u, half):
-            for r in range(4):
-                cols = slice(r * P, (r + 1) * P)
-                nc.tensor.transpose(banks[TURN_BANK[u][half]][:, cols], relus[u][half][:, cols], ident[:])
-
-        def square_turned(u, half):
-            src = banks[TURN_BANK[u][half]][:].rearrange("p (r t) -> p t r", r=4)
-            dst = h_values[u][:, half * H : (half + 1) * H].rearrange("p (t r) -> p t r", r=4)
-            nc.scalar.activation(dst, src, ACT.Square)
-
-        def quantize(u, cols):
+        def quantize(b, count):
+            cols = slice(b * P, (b + count) * P)
             nc.vector.quantize_mx(
-                out=h_codes[u][:, cols].bitcast(FP8X4),
-                scales=h_plane[u][:, cols],
-                in_=h_values[u][:, 4 * cols.start : 4 * cols.stop],
+                out=h_codes[:, cols].bitcast(FP8X4), scales=h_plane[:, cols], in_=h_values[:, b * H : (b + count) * H]
             )
 
-        def layer2_sums(u, cols):
-            first = LAYER2_FIRST[u]
-            return banks[LAYER2_BANK[u][cols.start // P]][:, first + cols.start : first + cols.stop]
-
-        def layer2(u, cols):
-            e = UNITS[u][0]
+        def layer2(b, count, bank, first):
+            e = expert_of(b)
+            cols = slice(b * P, (b + count) * P)
             nc.tensor.matmul_mx(
-                out=layer2_sums(u, cols),
+                out=banks[bank][:, first : first + count * P],
                 lhsT=w2_codes[:, e, :].bitcast(FP4X4),
                 lhsT_scale=w2_plane[:, e, :],
-                rhs=h_codes[u][:, cols].bitcast(FP8X4),
-                rhs_scale=h_plane[u][:, cols],
+                rhs=h_codes[:, cols].bitcast(FP8X4),
+                rhs_scale=h_plane[:, cols],
                 start=True,
                 stop=True,
             )
 
-        def apply_gate(u, cols):
-            e, first = UNITS[u]
-            nc.vector.tensor_tensor(slot_y[e][:, cols], layer2_sums(u, cols), gates[:, first + cols.start : first + cols.stop], ALU.mult)
+        def slot_cols(b, count):
+            return slice(b * P - T, (b + count) * P - T)
 
-        def scatter(u, cols):
-            e, first = UNITS[u]
-            nc.vector.tensor_copy(window[:].indirect(slots(slice(first + cols.start, first + cols.stop))), slot_y[e][:, cols])
+        def empty_y(b, count, bank, first):
+            nc.scalar.copy(slot_y[:, slot_cols(b, count)], banks[bank][:, first : first + count * P])
 
-        def add_shared(u, cols):
-            first = UNITS[u][1]
-            sums = banks[LAYER2_BANK[u][0]][:, cols.start - first : cols.stop - first]
-            nc.vector.tensor_tensor(result[:, cols], sums, window[:, cols], ALU.add)
+        def scatter(b, count):
+            cols = slot_cols(b, count)
+            nc.vector.tensor_tensor(window[:].indirect(slots(cols)), slot_y[:, cols], gates[:, cols], ALU.mult)
 
-        def store(cols):
-            nc.sync.dma_start(out=out[:, cols], in_=result[:, cols])
+        def add_shared(b, count, bank, first):
+            cols = slice(b * P, (b + count) * P)
+            nc.vector.tensor_tensor(result(b, count), banks[bank][:, first : first + count * P], window[:, cols], ALU.add)
 
-        zero_plane(x_plane)
-        load_token_pass(0, slice(0, 768))
+        def store(b, count):
+            cols = slice(b * P, (b + count) * P)
+            nc.sync.dma_start(out=out[:, cols], in_=result(b, count))
+
         nc.sync.dma_start(offsets[:], offs)
-        zero_plane(w1_plane_routed)
-        load_scale_rows(x_plane, x_scales, 0)
-        load_scale_rows(x_plane, x_scales, 1)
-        load_scale_rows(x_plane, x_scales, 3)
-        load_w1(SHARED, slice(0, 1))
-        load_scale_rows(x_plane, x_scales, 2)
-        load_w1(SHARED, slice(1, 3))
+        load_tokens(slice(0, PASSES), slice(0, 2 * P))
+        zero_plane(x_plane)
+        load_scales(nc.sync, x_plane, x_scales)
+        load_w1(SHARED, slice(0, PASSES))
         zero_plane(w1_plane_shared)
-        nc.vector.memset(ident[:], 0.0)
-        zero_plane(w2_plane)
+        load_scales(nc.sync, w1_plane_shared, w1_scales[SHARED])
+        load_tokens(slice(0, PASSES), slice(2 * P, T))
+        load_w1(0, slice(0, PASSES))
         nc.vector.memset(zero[:], 0.0)
-        make_identity(nc, ident[:], nomemset=True)
-        nc.scalar.activation(window[:], zero[:].to_broadcast([P, T]), ACT.Relu)
-        load_scale_rows(w1_plane_shared, w1_scales[SHARED], 3)
-        gather_words(0, slice(0, 512))
-        load_scale_rows(w1_plane_shared, w1_scales[SHARED], 1)
-        load_scale_rows(w1_plane_shared, w1_scales[SHARED], 0)
-        load_scale_rows(w1_plane_shared, w1_scales[SHARED], 2)
-        load_tokens(slice(1, 3), slice(0, 256))
-        load_w1(0, slice(0, 3))
-        load_token_pass(1, slice(256, 768))
-        warm_up()
-        gather_scales(0)
-        load_token_pass(2, slice(256, 768))
-        load_scale_rows(w1_plane_routed, routed_scales, 0)
-        load_scale_rows(w1_plane_routed, routed_scales, 2)
-        load_scale_rows(w1_plane_routed, routed_scales, 3)
-        load_scale_rows(w1_plane_routed, routed_scales, 1)
-        gather_scales(1)
-        layer1(S0, 0, 0)
+        zero_plane(w1_plane_routed)
+        load_scales(nc.sync, w1_plane_routed, routed_scales)
+        load_w1(1, slice(0, PASSES))
+        load_w2()
+        zero_plane(w2_plane)
+        load_scales(nc.sync, w2_plane, w2_scale_rows)
         nc.sync.dma_start(out=gates[:], in_=gate)
-        layer1(S0, 1, 0)
-        layer1(S1, 0, 0)
-        gather_scales(2)
-        load_scale_rows(w2_plane, w2_scale_rows, 3)
-        layer1(S0, 0, 1)
-        layer1(S0, 0, 2)
-        load_w1(1, slice(0, 3))
-        layer1(S0, 1, 1)
-        layer1(S0, 1, 2)
-        relu(SCALAR, S0, 0)
-        load_scale_rows(w2_plane, w2_scale_rows, 2)
-        gather_words(1, slice(0, 256))
-        layer1(S1, 1, 0)
-        load_scale_rows(w2_plane, w2_scale_rows, 0)
-        nc.sync.dma_start(out=w2_codes[:].bitcast(I32), in_=w2_words.rearrange("e s p b -> p (e s) b").bitcast(I32))
-        layer1(S1, 0, 1)
-        load_scale_rows(w2_plane, w2_scale_rows, 1)
-        relu(SCALAR, S0, 1)
-        layer1(S1, 1, 1)
-        gather_words(1, slice(256, 512))
-        layer1(S1, 0, 2)
-        square_pairs(SCALAR, S0, 0)
-        layer1(S1, 1, 2)
-        gather_words(2, slice(0, 256))
-        layer1(R0, 1, 0)
-        square_pairs(SCALAR, S0, 1)
-        layer1(R0, 0, 0)
-        gather_words(2, slice(256, 512))
-        layer1(R0, 1, 1)
-        relu(SCALAR, S1, 0)
-        layer1(R0, 0, 1)
-        relu(VECTOR, S1, 1)
-        layer1(R0, 0, 2)
-        layer1(R0, 1, 2)
-        layer1(R1, 0, 0)
-        square_pairs(VECTOR, S1, 0)
-        relu(SCALAR, R0, 0)
-        layer1(R1, 0, 1)
-        layer1(R1, 0, 2)
-        square_pairs(VECTOR, S1, 1)
-        relu(SCALAR, R0, 1)
-        layer1(R1, 1, 0)
-        turn_floats(R0, 0)
-        relu(SCALAR, R1, 0)
-        turn_pairs(S0, 0)
-        turn_pairs(S0, 1)
-        square_turned(R0, 0)
-        turn_floats(R0, 1)
-        interleave_pairs(VECTOR, S0)
-        turn_floats(R1, 0)
-        square_turned(R0, 1)
-        layer1(R1, 1, 1)
-        quantize(R0, slice(0, 128))
-        quantize(S0, slice(0, 256))
-        layer1(S2, 1, 0)
-        square_turned(R1, 0)
-        layer1(R1, 1, 2)
-        quantize(R0, slice(128, 256))
-        layer2(R0, slice(0, 128))
-        layer1(S2, 1, 1)
-        relu(SCALAR, R1, 1)
-        layer1(S2, 1, 2)
-        quantize(R1, slice(0, 128))
-        layer1(S2, 0, 0)
-        apply_gate(R0, slice(0, 128))
-        layer1(S2, 0, 1)
-        relu(SCALAR, S2, 1)
-        scatter(R0, slice(0, 128))
-        layer1(S2, 0, 2)
-        layer2(R0, slice(128, 256))
-        turn_floats(R1, 1)
-        relu(SCALAR, S2, 0)
-        apply_gate(R0, slice(128, 256))
-        turn_pairs(S1, 0)
-        turn_pairs(S1, 1)
-        scatter(R0, slice(128, 256))
-        square_turned(R1, 1)
-        layer2(R1, slice(0, 128))
-        turn_floats(S2, 0)
-        interleave_pairs(SCALAR, S1)
-        apply_gate(R1, slice(0, 128))
-        turn_floats(S2, 1)
-        quantize(R1, slice(128, 256))
-        scatter(R1, slice(0, 128))
-        square_turned(S2, 0)
-        layer2(R1, slice(128, 256))
-        square_turned(S2, 1)
-        quantize(S1, slice(0, 256))
-        layer2(S0, slice(0, 256))
-        apply_gate(R1, slice(128, 256))
-        quantize(S2, slice(0, 128))
-        scatter(R1, slice(128, 256))
-        layer2(S1, slice(0, 256))
-        layer2(S2, slice(0, 128))
-        quantize(S2, slice(128, 256))
-        add_shared(S0, slice(0, 512))
-        layer2(S2, slice(128, 256))
-        store(slice(0, 512))
-        add_shared(S2, slice(512, 640))
-        add_shared(S2, slice(640, 768))
-        store(slice(512, 640))
-        store(slice(640, 768))
+        make_identity(nc, ident[:])
+        nc.scalar.activation(window[:], zero[:].to_broadcast([P, T]), ACT.Relu)
+
+        first, second = slice(0, C), slice(C, SLOTS)
+        warm_up(7)
+        for o in range(PASSES):
+            gather_scales(o, slice(0, SLOTS))
+        for o in range(PASSES):
+            gather_words(o, first)
+        for o in range(PASSES):
+            gather_words(o, second)
+        for b in (S0, S1, S2, S3):
+            layer1(b, b)
+            relu(SCALAR, b, b)
+            square_pairs(SCALAR if b < S2 else VECTOR, b)
+        layer1(R0, 4)
+        layer1(R1, 5)
+        relu(SCALAR, R0, 4)
+        layer1(R2, 6)
+        relu(SCALAR, R1, 5)
+        turn(R0, 0)
+        turn_pairs(S0, 4, 0)
+        turn_pairs(S1, 4, 1)
+        turn(R1, 1)
+        turn_pairs(S2, 5, 0)
+        turn_pairs(S3, 5, 1)
+        relu(VECTOR, R2, 6)
+        square(R0, 0)
+        quantize(R0, 1)
+        layer2(R0, 1, 0, 0)
+        empty_y(R0, 1, 0, 0)
+        layer1(R3, 7)
+        square(R1, 1)
+        interleave_pairs(VECTOR, S0, 2, 4, 0)
+        turn(R2, 2)
+        quantize(R1, 1)
+        layer2(R1, 1, 1, 0)
+        interleave_pairs(VECTOR, S2, 2, 5, 0)
+        layer1(S4, 6)
+        relu(SCALAR, R3, 7)
+        square(R2, 2)
+        turn(R3, 3)
+        empty_y(R1, 1, 1, 0)
+        square(R3, 3)
+        quantize(R2, 1)
+        layer2(R2, 1, 0, 0)
+        empty_y(R2, 1, 0, 0)
+        quantize(R3, 1)
+        layer2(R3, 1, 1, 0)
+        empty_y(R3, 1, 1, 0)
+        layer1(S5, 7)
+        relu(SCALAR, S4, 6)
+        turn(S4, 2)
+        relu(SCALAR, S5, 7)
+        turn(S5, 3)
+        square(S4, 2)
+        square(S5, 3)
+        quantize(S0, 4)
+        quantize(S4, 1)
+        quantize(S5, 1)
+        for b in (R0, R1, R2, R3):
+            scatter(b, 1)
+        layer2(S4, 1, 6, 0)
+        layer2(S5, 1, 6, P)
+        layer2(S0, 4, 4, 0)
+        add_shared(S0, 4, 4, 0)
+        store(S0, 4)
+        add_shared(S4, 2, 6, 0)
+        store(S4, 2)

@@ -152,6 +152,11 @@ def tile_moe_shr_mlp_relu2_kernel(
             else:
                 nc.vector.tensor_scalar_max(dst, src, 0.0)
 
+        def relu_half(b, bank, half):
+            src = banks[bank][:].rearrange("t (p r) -> t r p", r=4)[:, 2 * half : 2 * half + 2, :]
+            dst = relus[b][:].rearrange("t (r p) -> t r p", r=4)[:, 2 * half : 2 * half + 2, :]
+            nc.scalar.activation(dst, src, ACT.Relu)
+
         def turn(b, bank):
             for r in range(4):
                 cols = slice(r * P, (r + 1) * P)
@@ -220,13 +225,14 @@ def tile_moe_shr_mlp_relu2_kernel(
             nc.sync.dma_start(out=out[:, cols], in_=result(b, count))
 
         nc.sync.dma_start(offsets[:], offs)
-        load_tokens(slice(0, PASSES), slice(0, 2 * P))
+        load_token_pass(0, slice(0, T))
         zero_plane(x_plane)
         load_scales(nc.sync, x_plane, x_scales)
         load_w1(SHARED, slice(0, PASSES))
         zero_plane(w1_plane_shared)
         load_scales(nc.sync, w1_plane_shared, w1_scales[SHARED])
-        load_tokens(slice(0, PASSES), slice(2 * P, T))
+        load_tokens(slice(1, PASSES), slice(0, 2 * P))
+        load_tokens(slice(1, PASSES), slice(2 * P, T))
         load_w1(0, slice(0, PASSES))
         nc.vector.memset(zero[:], 0.0)
         zero_plane(w1_plane_routed)
@@ -241,66 +247,69 @@ def tile_moe_shr_mlp_relu2_kernel(
 
         first, second = slice(0, C), slice(C, SLOTS)
         warm_up(7)
+        gather_words(0, slice(0, SLOTS))
         for o in range(PASSES):
             gather_scales(o, slice(0, SLOTS))
-        for o in range(PASSES):
-            gather_words(o, first)
-        for o in range(PASSES):
-            gather_words(o, second)
+        for cols in (first, second):
+            for o in range(1, PASSES):
+                gather_words(o, cols)
         for b in (S0, S1, S2, S3):
             layer1(b, b)
             relu(SCALAR, b, b)
-            square_pairs(SCALAR if b < S2 else VECTOR, b)
+            square_pairs(SCALAR, b)
         layer1(R0, 4)
         layer1(R1, 5)
-        relu(SCALAR, R0, 4)
+        relu(VECTOR, R0, 4)
         layer1(R2, 6)
-        relu(SCALAR, R1, 5)
+        relu(VECTOR, R1, 5)
         turn(R0, 0)
         turn_pairs(S0, 4, 0)
+        relu(VECTOR, R2, 6)
         turn_pairs(S1, 4, 1)
         turn(R1, 1)
+        square(R0, 0)
         turn_pairs(S2, 5, 0)
         turn_pairs(S3, 5, 1)
-        relu(VECTOR, R2, 6)
-        square(R0, 0)
-        quantize(R0, 1)
-        layer2(R0, 1, 0, 0)
-        empty_y(R0, 1, 0, 0)
+        interleave_pairs(VECTOR, S0, 2, 4, 0)
         layer1(R3, 7)
         square(R1, 1)
-        interleave_pairs(VECTOR, S0, 2, 4, 0)
-        turn(R2, 2)
+        quantize(R0, 1)
+        interleave_pairs(SCALAR, S2, 2, 5, 0)
+        layer2(R0, 1, 0, 0)
         quantize(R1, 1)
-        layer2(R1, 1, 1, 0)
-        interleave_pairs(VECTOR, S2, 2, 5, 0)
-        layer1(S4, 6)
+        turn(R2, 2)
         relu(SCALAR, R3, 7)
+        empty_y(R0, 1, 0, 0)
+        quantize(S0, 4)
+        layer2(R1, 1, 1, 0)
+        layer1(S4, 6)
         square(R2, 2)
+        scatter(R0, 1)
         turn(R3, 3)
         empty_y(R1, 1, 1, 0)
-        square(R3, 3)
+        relu(SCALAR, S4, 6)
         quantize(R2, 1)
+        layer1(S5, 7)
         layer2(R2, 1, 0, 0)
+        square(R3, 3)
+        scatter(R1, 1)
+        turn(S4, 2)
         empty_y(R2, 1, 0, 0)
         quantize(R3, 1)
+        relu_half(S5, 7, 0)
+        relu_half(S5, 7, 1)
         layer2(R3, 1, 1, 0)
-        empty_y(R3, 1, 1, 0)
-        layer1(S5, 7)
-        relu(SCALAR, S4, 6)
-        turn(S4, 2)
-        relu(SCALAR, S5, 7)
-        turn(S5, 3)
-        square(S4, 2)
-        square(S5, 3)
-        quantize(S0, 4)
-        quantize(S4, 1)
-        quantize(S5, 1)
-        for b in (R0, R1, R2, R3):
-            scatter(b, 1)
-        layer2(S4, 1, 6, 0)
-        layer2(S5, 1, 6, P)
         layer2(S0, 4, 4, 0)
+        scatter(R2, 1)
+        turn(S5, 3)
+        empty_y(R3, 1, 1, 0)
+        square(S4, 2)
+        scatter(R3, 1)
+        square(S5, 3)
+        quantize(S4, 1)
+        layer2(S4, 1, 6, 0)
+        quantize(S5, 1)
+        layer2(S5, 1, 6, P)
         add_shared(S0, 4, 4, 0)
         store(S0, 4)
         add_shared(S4, 2, 6, 0)

@@ -216,6 +216,14 @@ def tile_moe_shr_mlp_relu2_kernel(
             cols = slot_cols(b, count)
             nc.vector.tensor_tensor(window[:].indirect(slots(cols)), slot_y[:, cols], gates[:, cols], ALU.mult)
 
+        def apply_gate(b, count, bank, first):
+            cols = slot_cols(b, count)
+            nc.vector.tensor_tensor(slot_y[:, cols], banks[bank][:, first : first + count * P], gates[:, cols], ALU.mult)
+
+        def scatter_copy(b, count):
+            cols = slot_cols(b, count)
+            nc.vector.tensor_copy(window[:].indirect(slots(cols)), slot_y[:, cols])
+
         def add_shared(b, count, bank, first):
             cols = slice(b * P, (b + count) * P)
             nc.vector.tensor_tensor(result(b, count), banks[bank][:, first : first + count * P], window[:, cols], ALU.add)
@@ -256,12 +264,12 @@ def tile_moe_shr_mlp_relu2_kernel(
         for b in (S0, S1, S2, S3):
             layer1(b, b)
             relu(SCALAR, b, b)
-            square_pairs(SCALAR, b)
+            square_pairs(SCALAR if b < S2 else VECTOR, b)
         layer1(R0, 4)
         layer1(R1, 5)
-        relu(VECTOR, R0, 4)
+        relu(SCALAR, R0, 4)
         layer1(R2, 6)
-        relu(VECTOR, R1, 5)
+        relu(SCALAR, R1, 5)
         turn(R0, 0)
         turn_pairs(S0, 4, 0)
         relu(VECTOR, R2, 6)

@@ -23,7 +23,7 @@ SHARED = E
 BANK = 512
 SLOTS = E * C
 WARM_PASSES = 3
-SCALAR, VECTOR = "scalar", "vector"
+SCALAR, VECTOR, GPSIMD = "scalar", "vector", "gpsimd"
 S0, S1, S2, S3, S4, S5, R0, R1, R2, R3 = range(10)
 SHARED_BLOCKS = T // P
 PAIR_BLOCKS = (S0, S1, S2, S3)
@@ -58,19 +58,25 @@ def tile_moe_shr_mlp_relu2_kernel(
         h_codes = keep.tile([P, T + SLOTS], U32, name="h_codes", align_bytes=64)
         h_plane = keep.tile([P, T + SLOTS], U8, name="h_plane", align_bytes=64)
         slot_y = keep.tile([P, SLOTS], F32, name="slot_y")
-        result_head = h_values[:, S4 * H : (S5 + 1) * H].bitcast(F32)
+        h_last = keep.tile([P, 2 * H], BF16, name="h_last", tag="last", align_bytes=64)
+        late = {}
         result_tail = keep.tile([P, 2 * P], F32, name="result_tail")
+
+        def h_of(b, count):
+            return h_last[:, 0:H] if b == S5 else h_values[:, b * H : (b + count) * H]
 
         def result(b, count):
             if b < S4:
-                return result_head[:, b * P : (b + count) * P]
+                if "head" not in late:
+                    late.setdefault("head", keep.tile([P, 4 * P], F32, name="result_head", tag="last", align_bytes=64))
+                return late["head"][:, b * P : (b + count) * P]
             return result_tail[:, (b - S4) * P : (b - S4 + count) * P]
 
         routed_scales = w1_scales[0:E].rearrange("e s q i -> (e s) q i")
         w2_scale_rows = w2_scales.rearrange("e s q n -> (e s) q n")
 
-        def zero_plane(plane):
-            nc.vector.memset(plane[:].rearrange("p a b -> p (a b)").bitcast(I32), 0)
+        def zero_plane(plane, engine=nc.vector):
+            engine.memset(plane[:].rearrange("p a b -> p (a b)").bitcast(I32), 0)
 
         def load_scales(queue, plane, rows):
             by_row = rows.rearrange("a (q r) w -> r q a w", r=4)
@@ -164,12 +170,20 @@ def tile_moe_shr_mlp_relu2_kernel(
 
         def square(b, bank):
             src = banks[bank][:].rearrange("p (r t) -> p t r", r=4)
-            dst = h_values[:, b * H : (b + 1) * H].rearrange("p (t r) -> p t r", r=4)
+            dst = h_of(b, 1).rearrange("p (t r) -> p t r", r=4)
+            nc.scalar.activation(dst, src, ACT.Square)
+
+        def square_half(b, bank, half):
+            cols = slice(half * P // 2, (half + 1) * P // 2)
+            src = banks[bank][:].rearrange("p (r t) -> p t r", r=4)[:, cols, :]
+            dst = h_of(b, 1).rearrange("p (t r) -> p t r", r=4)[:, cols, :]
             nc.scalar.activation(dst, src, ACT.Square)
 
         def square_pairs(engine, b):
             if engine == SCALAR:
                 nc.scalar.activation(squares[b][:], relus[b][:], ACT.Square)
+            elif engine == GPSIMD:
+                nc.gpsimd.tensor_tensor(squares[b][:], relus[b][:], relus[b][:], ALU.mult)
             else:
                 nc.vector.tensor_tensor(squares[b][:], relus[b][:], relus[b][:], ALU.mult)
 
@@ -190,7 +204,7 @@ def tile_moe_shr_mlp_relu2_kernel(
         def quantize(b, count):
             cols = slice(b * P, (b + count) * P)
             nc.vector.quantize_mx(
-                out=h_codes[:, cols].bitcast(FP8X4), scales=h_plane[:, cols], in_=h_values[:, b * H : (b + count) * H]
+                out=h_codes[:, cols].bitcast(FP8X4), scales=h_plane[:, cols], in_=h_of(b, count)
             )
 
         def layer2(b, count, bank, first):
@@ -286,8 +300,9 @@ def tile_moe_shr_mlp_relu2_kernel(
         layer2(R0, 1, 0, 0)
         quantize(R1, 1)
         turn(R2, 2)
-        relu(SCALAR, R3, 7)
+        relu_half(R3, 7, 0)
         empty_y(R0, 1, 0, 0)
+        relu_half(R3, 7, 1)
         quantize(S0, 4)
         layer2(R1, 1, 1, 0)
         layer1(S4, 6)
@@ -297,8 +312,8 @@ def tile_moe_shr_mlp_relu2_kernel(
         empty_y(R1, 1, 1, 0)
         relu(SCALAR, S4, 6)
         quantize(R2, 1)
-        layer1(S5, 7)
         layer2(R2, 1, 0, 0)
+        layer1(S5, 7)
         square(R3, 3)
         scatter(R1, 1)
         turn(S4, 2)
@@ -310,15 +325,18 @@ def tile_moe_shr_mlp_relu2_kernel(
         layer2(S0, 4, 4, 0)
         scatter(R2, 1)
         turn(S5, 3)
+        square_half(S4, 2, 0)
         empty_y(R3, 1, 1, 0)
-        square(S4, 2)
+        square_half(S4, 2, 1)
         scatter(R3, 1)
         square(S5, 3)
         quantize(S4, 1)
         layer2(S4, 1, 6, 0)
         quantize(S5, 1)
         layer2(S5, 1, 6, P)
-        add_shared(S0, 4, 4, 0)
-        store(S0, 4)
+        add_shared(S0, 2, 4, 0)
+        store(S0, 2)
+        add_shared(S2, 2, 4, 2 * P)
+        store(S2, 2)
         add_shared(S4, 2, 6, 0)
         store(S4, 2)

@@ -254,11 +254,11 @@ def tile_moe_shr_mlp_relu2_kernel(
         zero_plane(w1_plane_shared)
         load_scales(nc.sync, w1_plane_shared, w1_scales[SHARED])
         load_tokens(slice(1, PASSES), slice(0, 2 * P))
-        load_tokens(slice(1, PASSES), slice(2 * P, T))
-        load_w1(0, slice(0, PASSES))
         nc.vector.memset(zero[:], 0.0)
         zero_plane(w1_plane_routed)
         load_scales(nc.sync, w1_plane_routed, routed_scales)
+        load_tokens(slice(1, PASSES), slice(2 * P, T))
+        load_w1(0, slice(0, PASSES))
         load_w1(1, slice(0, PASSES))
         load_w2()
         zero_plane(w2_plane)

@@ -22,11 +22,13 @@ PASSES = K // 512
 SHARED = E
 BANK = 512
 SLOTS = E * C
-WARM_PASSES = 3
+CHUNK = 256
+WARM_PASSES = 2
 SCALAR, VECTOR, GPSIMD = "scalar", "vector", "gpsimd"
-S0, S1, S2, S3, S4, S5, R0, R1, R2, R3 = range(10)
-SHARED_BLOCKS = T // P
-PAIR_BLOCKS = (S0, S1, S2, S3)
+A, B, D = range(3)
+R0, R1, R2, R3 = range(4)
+TOKEN_H_TAGS = ("token_h0", "token_h1", "token_h2")
+FIRST_CODES_TAG = "slot_codes2"
 
 
 def tile_moe_shr_mlp_relu2_kernel(
@@ -40,303 +42,318 @@ def tile_moe_shr_mlp_relu2_kernel(
         offsets = keep.tile([P, SLOTS // 16], U16, name="offsets")
         x_codes = keep.tile([P, PASSES, T], I32, name="x_codes", align_bytes=64)
         x_plane = keep.tile([P, PASSES, T], U8, name="x_plane", align_bytes=64)
-        w1_codes = [keep.tile([P, PASSES, 2 * H], U8, name="w1_codes%d" % e, align_bytes=64) for e in range(E + 1)]
-        w1_plane_shared = keep.tile([P, PASSES, H], U8, name="w1_plane_shared", align_bytes=64)
-        w1_plane_routed = keep.tile([P, E * PASSES, H], U8, name="w1_plane_routed", align_bytes=64)
+        ws_words = keep.tile([P, PASSES, 2 * H], U8, name="ws_words", align_bytes=64)
+        ws_codes = [keep.tile([P, 2 * H], U8, name="ws_codes%d" % o, align_bytes=64) for o in range(PASSES)]
+        ws_rows = keep.tile([P, PASSES, H], U8, name="ws_rows", align_bytes=64)
+        ws_plane = [keep.tile([P, H], U8, name="ws_plane%d" % o, align_bytes=64) for o in range(PASSES)]
+        w1_codes = [keep.tile([P, PASSES, 2 * H], U8, name="w1_codes%d" % e, tag="w1_codes%d" % e, align_bytes=64) for e in range(E)]
+        w1_plane = keep.tile([P, E * PASSES, H], U8, name="w1_plane", align_bytes=64)
         w2_codes = keep.tile([P, E + 1, 2 * N], U8, name="w2_codes", align_bytes=64)
         w2_plane = keep.tile([P, E + 1, N], U8, name="w2_plane", align_bytes=64)
         gates = keep.tile([P, SLOTS], F32, name="gates")
         ident = keep.tile([P, P], F32, name="ident")
         zero = keep.tile([P, 1], F32, name="zero")
         window = keep.tile([P, T], F32, name="window")
-        slot_codes = [keep.tile([P, SLOTS], U32, name="slot_codes%d" % o, align_bytes=64) for o in range(PASSES)]
-        slot_plane = [keep.tile([P, SLOTS], U8, name="slot_plane%d" % o, align_bytes=64) for o in range(PASSES)]
+        slot_codes = [keep.tile([P, SLOTS], U32, name="slot_codes%d" % o, tag="slot_codes%d" % o, align_bytes=64) for o in range(PASSES)]
+        slot_plane = {}
         banks = [psum.tile([P, BANK], F32, name="bank%d" % b) for b in range(8)]
-        relus = [keep.tile([P, H], F32, name="relu%d" % b) for b in range(10)]
-        squares = {b: keep.tile([P, H], BF16, name="squares%d" % b, align_bytes=64) for b in PAIR_BLOCKS}
-        h_values = keep.tile([P, 4 * (T + SLOTS)], BF16, name="h_values", align_bytes=64)
-        h_codes = keep.tile([P, T + SLOTS], U32, name="h_codes", align_bytes=64)
+        token_relu = [keep.tile([P, 4 * CHUNK], F32, name="token_relu%d" % c) for c in range(T // CHUNK)]
+        slot_relu = [keep.tile([P, H], F32, name="slot_relu%d" % b) for b in range(SLOTS // P)]
         h_plane = keep.tile([P, T + SLOTS], U8, name="h_plane", align_bytes=64)
-        slot_y = keep.tile([P, SLOTS], F32, name="slot_y")
-        h_last = keep.tile([P, 2 * H], BF16, name="h_last", tag="last", align_bytes=64)
         late = {}
-        result_tail = keep.tile([P, 2 * P], F32, name="result_tail")
 
-        def h_of(b, count):
-            return h_last[:, 0:H] if b == S5 else h_values[:, b * H : (b + count) * H]
+        def late_tile(name, shape, dtype, tag):
+            if name not in late:
+                late.setdefault(name, keep.tile(shape, dtype, name=name, tag=tag, align_bytes=64))
+            return late[name]
 
-        def result(b, count):
-            if b < S4:
-                if "head" not in late:
-                    late.setdefault("head", keep.tile([P, 4 * P], F32, name="result_head", tag="last", align_bytes=64))
-                return late["head"][:, b * P : (b + count) * P]
-            return result_tail[:, (b - S4) * P : (b - S4 + count) * P]
+        def h_values(cols):
+            if cols.start >= T:
+                return late_tile("slot_h", [P, 4 * SLOTS], BF16, "slot_h")[:, 4 * (cols.start - T) : 4 * (cols.stop - T)]
+            c = cols.start // CHUNK
+            tile = late_tile("token_h%d" % c, [P, 4 * CHUNK], BF16, TOKEN_H_TAGS[c])
+            return tile[:, 4 * (cols.start - c * CHUNK) : 4 * (cols.stop - c * CHUNK)]
+
+        def h_codes(cols):
+            if cols.start >= 2 * CHUNK:
+                tile = late_tile("last_codes", [P, CHUNK + SLOTS], U32, "last_codes")
+                return tile[:, cols.start - 2 * CHUNK : cols.stop - 2 * CHUNK]
+            return late_tile("first_codes", [P, 2 * CHUNK], U32, FIRST_CODES_TAG)[:, cols]
+
+        slot_y = keep.tile([P, SLOTS], F32, name="slot_y")
+        result = keep.tile([P, T], F32, name="result")
 
         routed_scales = w1_scales[0:E].rearrange("e s q i -> (e s) q i")
         w2_scale_rows = w2_scales.rearrange("e s q n -> (e s) q n")
 
-        def zero_plane(plane, engine=nc.vector):
-            engine.memset(plane[:].rearrange("p a b -> p (a b)").bitcast(I32), 0)
+        def zero_plane(plane):
+            nc.vector.memset(plane[:].rearrange("p a b -> p (a b)").bitcast(I32), 0)
 
-        def load_scales(queue, plane, rows):
+        def load_scales(plane, rows):
             by_row = rows.rearrange("a (q r) w -> r q a w", r=4)
             for r in range(4):
-                queue.dma_start(out=plane[r:P:32, :, :].bitcast(I32), in_=by_row[r].bitcast(I32))
-
-        def load_token_pass(o, cols):
-            words = x_words[o].rearrange("p t r -> p (t r)").bitcast(I32)
-            nc.sync.dma_start(out=x_codes[:, o, :][:, cols], in_=words[:, cols])
+                nc.sync.dma_start(out=plane[r:P:32, :, :].bitcast(I32), in_=by_row[r].bitcast(I32))
 
         def load_tokens(passes, cols):
             words = x_words[passes].rearrange("o p t r -> p o (t r)").bitcast(I32)
             nc.sync.dma_start(out=x_codes[:, passes, cols], in_=words[:, :, cols])
 
-        def load_w1(e, passes):
-            nc.sync.dma_start(
-                out=w1_codes[e][:, passes, :].bitcast(I32),
-                in_=w1_words[e, passes].rearrange("s p b -> p s b").bitcast(I32),
-            )
+        def load_w1(dst, e, passes):
+            nc.sync.dma_start(out=dst[:].bitcast(I32), in_=w1_words[e, passes].rearrange("s p b -> p s b").bitcast(I32))
 
         def load_w2():
             nc.sync.dma_start(out=w2_codes[:].bitcast(I32), in_=w2_words.rearrange("e s p b -> p (e s) b").bitcast(I32))
 
+        def permute_words(o, u):
+            nc.scalar.copy(
+                ws_codes[o][:].bitcast(U16).rearrange("p (t m) -> p t m", t=4)[:, 2 * u : 2 * u + 2, :],
+                ws_words[:, o, :].bitcast(U16).rearrange("p (m t) -> p t m", t=4)[:, 2 * u : 2 * u + 2, :],
+            )
+
+        def permute_scales(o):
+            nc.vector.tensor_copy(
+                ws_plane[o][:].rearrange("p (t m) -> p t m", t=4),
+                ws_rows[:, o, :].rearrange("p (m t) -> p t m", t=4),
+            )
+
         def slots(cols):
             return offsets[:, cols.start // 16 : cols.stop // 16]
 
-        def gather_scales(o, cols):
-            nc.vector.tensor_copy(slot_plane[o][:, cols], x_plane[:, o, :].indirect(slots(cols)))
+        def gather_scales(b, o):
+            plane = keep.tile([P, P], U8, name="slot_plane%d_%d" % (b, o), tag="slot_plane%d_%d" % (b % 2, o), align_bytes=64)
+            slot_plane.setdefault((b, o), plane)
+            nc.vector.tensor_copy(plane[:], x_plane[:, o, :].indirect(slots(block(b))))
 
         def gather_words(o, cols):
             nc.vector.tensor_copy(slot_codes[o][:, cols], x_codes[:, o, :].bitcast(U32).indirect(slots(cols)))
+
+        def token_pass(c, bank, t, o):
+            cols = slice(c * CHUNK, (c + 1) * CHUNK)
+            nc.tensor.matmul_mx(
+                out=banks[bank + t // 2][:, (t % 2) * CHUNK : (t % 2 + 1) * CHUNK],
+                lhsT=ws_codes[o][:, 2 * t * P : 2 * (t + 1) * P].bitcast(FP4X4),
+                lhsT_scale=ws_plane[o][:, t * P : (t + 1) * P],
+                rhs=x_codes[:, o, :][:, cols].bitcast(FP8X4),
+                rhs_scale=x_plane[:, o, cols],
+                start=(o == 0 and t % 2 == 0),
+                stop=(o == PASSES - 1 and t % 2 == 1),
+            )
+
+        def token_half(c, bank, u):
+            for o in range(PASSES):
+                for t in (2 * u, 2 * u + 1):
+                    token_pass(c, bank, t, o)
+
+        def token_passes(c, bank, o):
+            for t in range(4):
+                token_pass(c, bank, t, o)
+
+        def token_rest(c, bank, u):
+            for o in range(1, PASSES):
+                for t in (2 * u, 2 * u + 1):
+                    token_pass(c, bank, t, o)
+
+        def token_relu_half(engine, c, bank, u):
+            src = banks[bank + u][:].rearrange("p (e c) -> p c e", e=2)
+            dst = token_relu[c][:, u * BANK : (u + 1) * BANK].rearrange("p (c e) -> p c e", e=2)
+            if engine == SCALAR:
+                nc.scalar.activation(dst, src, ACT.Relu)
+            else:
+                nc.vector.tensor_scalar_max(dst, src, 0.0)
+
+        def token_square(engine, c, cols):
+            src = token_relu[c][:].rearrange("p (u c e) -> p c u e", u=2, e=2)[:, cols]
+            dst = h_values(chunk(c)).rearrange("p (c u e) -> p c u e", u=2, e=2)[:, cols]
+            if engine == SCALAR:
+                nc.scalar.activation(dst, src, ACT.Square)
+            elif engine == GPSIMD:
+                nc.gpsimd.tensor_tensor(dst, src, src, ALU.mult)
+            else:
+                nc.vector.tensor_tensor(dst, src, src, ALU.mult)
+
+        def slot_pass(b, bank, o):
+            e = b * P // C
+            nc.tensor.matmul_mx(
+                out=banks[bank][:],
+                lhsT=slot_codes[o][:, b * P : (b + 1) * P].bitcast(FP8X4),
+                lhsT_scale=slot_plane[(b, o)][:],
+                rhs=w1_codes[e][:, o, :].bitcast(FP4X4),
+                rhs_scale=w1_plane[:, e * PASSES + o, :],
+                start=(o == 0),
+                stop=(o == PASSES - 1),
+            )
+
+        def slot_passes(b, bank):
+            for o in range(PASSES):
+                slot_pass(b, bank, o)
+
+        def relu(engine, b, bank):
+            src = banks[bank][:].rearrange("t (p r) -> t r p", r=4)
+            dst = slot_relu[b][:].rearrange("t (r p) -> t r p", r=4)
+            if engine == SCALAR:
+                nc.scalar.activation(dst, src, ACT.Relu)
+            else:
+                nc.vector.tensor_scalar_max(dst, src, 0.0)
+
+        def turn(b, bank):
+            for r in range(4):
+                cols = slice(r * P, (r + 1) * P)
+                nc.tensor.transpose(banks[bank][:, cols], slot_relu[b][:, cols], ident[:])
+
+        def square(b, bank):
+            src = banks[bank][:].rearrange("p (r t) -> p t r", r=4)
+            dst = h_values(slot_block(b)).rearrange("p (t r) -> p t r", r=4)
+            nc.scalar.activation(dst, src, ACT.Square)
+
+        def quantize(cols):
+            nc.vector.quantize_mx(
+                out=h_codes(cols).bitcast(FP8X4),
+                scales=h_plane[:, cols],
+                in_=h_values(cols),
+            )
+
+        def layer2(e, cols, bank, first):
+            nc.tensor.matmul_mx(
+                out=banks[bank][:, first : first + cols.stop - cols.start],
+                lhsT=w2_codes[:, e, :].bitcast(FP4X4),
+                lhsT_scale=w2_plane[:, e, :],
+                rhs=h_codes(cols).bitcast(FP8X4),
+                rhs_scale=h_plane[:, cols],
+                start=True,
+                stop=True,
+            )
+
+        def block(b):
+            return slice(b * P, (b + 1) * P)
+
+        def slot_block(b):
+            return slice(T + b * P, T + (b + 1) * P)
+
+        def slot_layer2(b, bank):
+            layer2(b * P // C, slot_block(b), bank, 0)
+
+        def empty_y(b, bank):
+            nc.scalar.copy(slot_y[:, block(b)], banks[bank][:, 0:P])
+
+        def scatter(b):
+            cols = block(b)
+            nc.vector.tensor_tensor(window[:].indirect(slots(cols)), slot_y[:, cols], gates[:, cols], ALU.mult)
+
+        def add_shared(cols, bank, first):
+            nc.vector.tensor_tensor(
+                result[:, cols], banks[bank][:, first : first + cols.stop - cols.start], window[:, cols], ALU.add
+            )
+
+        def store(cols):
+            nc.sync.dma_start(out=out[:, cols], in_=result[:, cols])
+
+        def chunk(c):
+            return slice(c * CHUNK, (c + 1) * CHUNK)
 
         def warm_up(bank):
             for repeat in range(WARM_PASSES):
                 nc.tensor.matmul_mx(
                     out=banks[bank][:],
                     lhsT=x_codes[:, 0, :][:, 0:P].bitcast(FP8X4),
-                    lhsT_scale=x_plane[:, 0, 0:P],
-                    rhs=x_codes[:, 0, :][:, 0 : 2 * P].bitcast(FP4X4),
-                    rhs_scale=x_plane[:, 0, 0:H],
+                    lhsT_scale=ws_rows[:, 1, 0:P],
+                    rhs=ws_words[:, 0, :].bitcast(FP4X4),
+                    rhs_scale=ws_rows[:, 0, :],
                     start=True,
                     stop=True,
                 )
 
-        def expert_of(b):
-            return SHARED if b < SHARED_BLOCKS else (b - SHARED_BLOCKS) * P // C
-
-        def layer1_pass(b, bank, o):
-            e = expert_of(b)
-            if e == SHARED:
-                cols = slice(b * P, (b + 1) * P)
-                codes, plane, w1_plane = x_codes[:, o, :][:, cols], x_plane[:, o, cols], w1_plane_shared[:, o, :]
-            else:
-                cols = slice(b * P - T, (b + 1) * P - T)
-                codes, plane, w1_plane = slot_codes[o][:, cols], slot_plane[o][:, cols], w1_plane_routed[:, e * PASSES + o, :]
-            nc.tensor.matmul_mx(
-                out=banks[bank][:],
-                lhsT=codes.bitcast(FP8X4),
-                lhsT_scale=plane,
-                rhs=w1_codes[e][:, o, :].bitcast(FP4X4),
-                rhs_scale=w1_plane,
-                start=(o == 0),
-                stop=(o == PASSES - 1),
-            )
-
-        def layer1(b, bank):
-            for o in range(PASSES):
-                layer1_pass(b, bank, o)
-
-        def relu(engine, b, bank):
-            if b in PAIR_BLOCKS:
-                src = banks[bank][:].rearrange("t (p w e) -> t w p e", w=2, e=2)
-                dst = relus[b][:].rearrange("t (w p e) -> t w p e", w=2, e=2)
-            else:
-                src = banks[bank][:].rearrange("t (p r) -> t r p", r=4)
-                dst = relus[b][:].rearrange("t (r p) -> t r p", r=4)
-            if engine == SCALAR:
-                nc.scalar.activation(dst, src, ACT.Relu)
-            else:
-                nc.vector.tensor_scalar_max(dst, src, 0.0)
-
-        def relu_half(b, bank, half):
-            src = banks[bank][:].rearrange("t (p r) -> t r p", r=4)[:, 2 * half : 2 * half + 2, :]
-            dst = relus[b][:].rearrange("t (r p) -> t r p", r=4)[:, 2 * half : 2 * half + 2, :]
-            nc.scalar.activation(dst, src, ACT.Relu)
-
-        def turn(b, bank):
-            for r in range(4):
-                cols = slice(r * P, (r + 1) * P)
-                nc.tensor.transpose(banks[bank][:, cols], relus[b][:, cols], ident[:])
-
-        def square(b, bank):
-            src = banks[bank][:].rearrange("p (r t) -> p t r", r=4)
-            dst = h_of(b, 1).rearrange("p (t r) -> p t r", r=4)
-            nc.scalar.activation(dst, src, ACT.Square)
-
-        def square_half(b, bank, half):
-            cols = slice(half * P // 2, (half + 1) * P // 2)
-            src = banks[bank][:].rearrange("p (r t) -> p t r", r=4)[:, cols, :]
-            dst = h_of(b, 1).rearrange("p (t r) -> p t r", r=4)[:, cols, :]
-            nc.scalar.activation(dst, src, ACT.Square)
-
-        def square_pairs(engine, b):
-            if engine == SCALAR:
-                nc.scalar.activation(squares[b][:], relus[b][:], ACT.Square)
-            elif engine == GPSIMD:
-                nc.gpsimd.tensor_tensor(squares[b][:], relus[b][:], relus[b][:], ALU.mult)
-            else:
-                nc.vector.tensor_tensor(squares[b][:], relus[b][:], relus[b][:], ALU.mult)
-
-        def turn_pairs(b, bank, half):
-            words = squares[b][:].bitcast(F32)
-            for w in range(2):
-                j = 2 * half + w
-                nc.tensor.transpose(banks[bank][:, j * P : (j + 1) * P], words[:, w * P : (w + 1) * P], ident[:])
-
-        def interleave_pairs(engine, b, count, bank, half):
-            src = banks[bank][:, half * 2 * P : (half + count) * 2 * P].rearrange("p (h w t) -> p h t w", h=count, w=2)
-            dst = h_values[:, b * H : (b + count) * H].bitcast(F32).rearrange("p (h t w) -> p h t w", h=count, w=2)
-            if engine == SCALAR:
-                nc.scalar.copy(dst, src)
-            else:
-                nc.vector.tensor_copy(dst, src)
-
-        def quantize(b, count):
-            cols = slice(b * P, (b + count) * P)
-            nc.vector.quantize_mx(
-                out=h_codes[:, cols].bitcast(FP8X4), scales=h_plane[:, cols], in_=h_of(b, count)
-            )
-
-        def layer2(b, count, bank, first):
-            e = expert_of(b)
-            cols = slice(b * P, (b + count) * P)
-            nc.tensor.matmul_mx(
-                out=banks[bank][:, first : first + count * P],
-                lhsT=w2_codes[:, e, :].bitcast(FP4X4),
-                lhsT_scale=w2_plane[:, e, :],
-                rhs=h_codes[:, cols].bitcast(FP8X4),
-                rhs_scale=h_plane[:, cols],
-                start=True,
-                stop=True,
-            )
-
-        def slot_cols(b, count):
-            return slice(b * P - T, (b + count) * P - T)
-
-        def empty_y(b, count, bank, first):
-            nc.scalar.copy(slot_y[:, slot_cols(b, count)], banks[bank][:, first : first + count * P])
-
-        def scatter(b, count):
-            cols = slot_cols(b, count)
-            nc.vector.tensor_tensor(window[:].indirect(slots(cols)), slot_y[:, cols], gates[:, cols], ALU.mult)
-
-        def apply_gate(b, count, bank, first):
-            cols = slot_cols(b, count)
-            nc.vector.tensor_tensor(slot_y[:, cols], banks[bank][:, first : first + count * P], gates[:, cols], ALU.mult)
-
-        def scatter_copy(b, count):
-            cols = slot_cols(b, count)
-            nc.vector.tensor_copy(window[:].indirect(slots(cols)), slot_y[:, cols])
-
-        def add_shared(b, count, bank, first):
-            cols = slice(b * P, (b + count) * P)
-            nc.vector.tensor_tensor(result(b, count), banks[bank][:, first : first + count * P], window[:, cols], ALU.add)
-
-        def store(b, count):
-            cols = slice(b * P, (b + count) * P)
-            nc.sync.dma_start(out=out[:, cols], in_=result(b, count))
-
         nc.sync.dma_start(offsets[:], offs)
-        load_token_pass(0, slice(0, T))
+        load_w1(ws_words, SHARED, slice(0, PASSES))
+        zero_plane(ws_rows)
+        load_scales(ws_rows, w1_scales[SHARED])
+        load_tokens(slice(0, 1), slice(0, T))
+        load_tokens(slice(1, PASSES), slice(0, CHUNK))
         zero_plane(x_plane)
-        load_scales(nc.sync, x_plane, x_scales)
-        load_w1(SHARED, slice(0, PASSES))
-        zero_plane(w1_plane_shared)
-        load_scales(nc.sync, w1_plane_shared, w1_scales[SHARED])
-        load_tokens(slice(1, PASSES), slice(0, 2 * P))
-        nc.vector.memset(zero[:], 0.0)
-        zero_plane(w1_plane_routed)
-        load_scales(nc.sync, w1_plane_routed, routed_scales)
-        load_tokens(slice(1, PASSES), slice(2 * P, T))
-        load_w1(0, slice(0, PASSES))
-        load_w1(1, slice(0, PASSES))
+        load_scales(x_plane, x_scales)
+        load_tokens(slice(1, PASSES), slice(CHUNK, T))
+        load_w1(w1_codes[0], 0, slice(0, PASSES))
+        load_w1(w1_codes[1], 1, slice(0, PASSES))
         load_w2()
+        nc.vector.memset(zero[:], 0.0)
+        zero_plane(w1_plane)
+        load_scales(w1_plane, routed_scales)
         zero_plane(w2_plane)
-        load_scales(nc.sync, w2_plane, w2_scale_rows)
+        load_scales(w2_plane, w2_scale_rows)
         nc.sync.dma_start(out=gates[:], in_=gate)
         make_identity(nc, ident[:])
         nc.scalar.activation(window[:], zero[:].to_broadcast([P, T]), ACT.Relu)
 
         first, second = slice(0, C), slice(C, SLOTS)
+        low, high = slice(0, P), slice(P, CHUNK)
         warm_up(7)
-        gather_words(0, slice(0, SLOTS))
         for o in range(PASSES):
-            gather_scales(o, slice(0, SLOTS))
+            permute_scales(o)
+        for u in range(2):
+            for o in range(PASSES):
+                permute_words(o, u)
+        gather_words(0, slice(0, SLOTS))
+        for b in (R0, R1):
+            for o in range(PASSES):
+                gather_scales(b, o)
         for cols in (first, second):
             for o in range(1, PASSES):
                 gather_words(o, cols)
-        for b in (S0, S1, S2, S3):
-            layer1(b, b)
-            relu(SCALAR, b, b)
-            square_pairs(SCALAR if b < S2 else VECTOR, b)
-        layer1(R0, 4)
-        layer1(R1, 5)
+        for c, bank in ((A, 0), (B, 2)):
+            for u in range(2):
+                token_half(c, bank, u)
+                token_relu_half(SCALAR, c, bank, u)
+            token_square(GPSIMD, c, low)
+            token_square(GPSIMD, c, high)
+        slot_passes(R0, 4)
+        for o in range(PASSES):
+            gather_scales(R2, o)
         relu(SCALAR, R0, 4)
-        layer1(R2, 6)
+        slot_passes(R1, 5)
+        for o in range(PASSES):
+            gather_scales(R3, o)
         relu(SCALAR, R1, 5)
         turn(R0, 0)
-        turn_pairs(S0, 4, 0)
-        relu(VECTOR, R2, 6)
-        turn_pairs(S1, 4, 1)
-        turn(R1, 1)
         square(R0, 0)
-        turn_pairs(S2, 5, 0)
-        turn_pairs(S3, 5, 1)
-        interleave_pairs(VECTOR, S0, 2, 4, 0)
-        layer1(R3, 7)
+        slot_passes(R2, 6)
+        turn(R1, 1)
+        quantize(slot_block(R0))
+        slot_layer2(R0, 0)
+        empty_y(R0, 0)
         square(R1, 1)
-        quantize(R0, 1)
-        interleave_pairs(SCALAR, S2, 2, 5, 0)
-        layer2(R0, 1, 0, 0)
-        quantize(R1, 1)
+        relu(VECTOR, R2, 6)
+        scatter(R0)
+        slot_passes(R3, 7)
+        quantize(slot_block(R1))
         turn(R2, 2)
-        relu_half(R3, 7, 0)
-        empty_y(R0, 1, 0, 0)
-        relu_half(R3, 7, 1)
-        quantize(S0, 4)
-        layer2(R1, 1, 1, 0)
-        layer1(S4, 6)
+        slot_layer2(R1, 1)
+        empty_y(R1, 1)
+        relu(SCALAR, R3, 7)
         square(R2, 2)
-        scatter(R0, 1)
+        scatter(R1)
         turn(R3, 3)
-        empty_y(R1, 1, 1, 0)
-        relu(SCALAR, S4, 6)
-        quantize(R2, 1)
-        layer2(R2, 1, 0, 0)
-        layer1(S5, 7)
+        quantize(slot_block(R2))
+        slot_layer2(R2, 2)
+        empty_y(R2, 2)
         square(R3, 3)
-        scatter(R1, 1)
-        turn(S4, 2)
-        empty_y(R2, 1, 0, 0)
-        quantize(R3, 1)
-        relu_half(S5, 7, 0)
-        relu_half(S5, 7, 1)
-        layer2(R3, 1, 1, 0)
-        layer2(S0, 4, 4, 0)
-        scatter(R2, 1)
-        turn(S5, 3)
-        square_half(S4, 2, 0)
-        empty_y(R3, 1, 1, 0)
-        square_half(S4, 2, 1)
-        scatter(R3, 1)
-        square(S5, 3)
-        quantize(S4, 1)
-        layer2(S4, 1, 6, 0)
-        quantize(S5, 1)
-        layer2(S5, 1, 6, P)
-        add_shared(S0, 2, 4, 0)
-        store(S0, 2)
-        add_shared(S2, 2, 4, 2 * P)
-        store(S2, 2)
-        add_shared(S4, 2, 6, 0)
-        store(S4, 2)
+        quantize(slot_block(R3))
+        scatter(R2)
+        slot_layer2(R3, 3)
+        empty_y(R3, 3)
+        scatter(R3)
+        token_half(D, 6, 0)
+        token_half(D, 6, 1)
+        token_relu_half(SCALAR, D, 6, 0)
+        token_relu_half(SCALAR, D, 6, 1)
+        token_square(SCALAR, D, low)
+        token_square(SCALAR, D, high)
+        quantize(chunk(A))
+        quantize(chunk(B))
+        layer2(SHARED, slice(0, 2 * CHUNK), 4, 0)
+        quantize(chunk(D))
+        layer2(SHARED, chunk(D), 5, 0)
+        add_shared(chunk(A), 4, 0)
+        store(chunk(A))
+        add_shared(chunk(B), 4, CHUNK)
+        store(chunk(B))
+        add_shared(chunk(D), 5, 0)
+        store(chunk(D))

@@ -23,12 +23,12 @@ SHARED = E
 BANK = 512
 SLOTS = E * C
 CHUNK = 256
-WARM_PASSES = 2
+WARM_PASSES = 3
 SCALAR, VECTOR, GPSIMD = "scalar", "vector", "gpsimd"
 A, B, D = range(3)
 R0, R1, R2, R3 = range(4)
-TOKEN_H_TAGS = ("token_h0", "token_h1", "token_h2")
-FIRST_CODES_TAG = "slot_codes2"
+TOKEN_CODES_TAGS = ("slot_plane1_0", "second_codes")
+D0, D1 = 4, 5
 
 
 def tile_moe_shr_mlp_relu2_kernel(
@@ -57,8 +57,8 @@ def tile_moe_shr_mlp_relu2_kernel(
         slot_codes = [keep.tile([P, SLOTS], U32, name="slot_codes%d" % o, tag="slot_codes%d" % o, align_bytes=64) for o in range(PASSES)]
         slot_plane = {}
         banks = [psum.tile([P, BANK], F32, name="bank%d" % b) for b in range(8)]
-        token_relu = [keep.tile([P, 4 * CHUNK], F32, name="token_relu%d" % c) for c in range(T // CHUNK)]
-        slot_relu = [keep.tile([P, H], F32, name="slot_relu%d" % b) for b in range(SLOTS // P)]
+        token_relu = [keep.tile([P, 4 * CHUNK], F32, name="token_relu%d" % c, tag="token_relu%d" % c, align_bytes=64) for c in range(T // CHUNK)]
+        slot_relu = [keep.tile([P, H], F32, name="slot_relu%d" % b, tag="slot_relu%d" % b, align_bytes=64) for b in range(SLOTS // P)]
         h_plane = keep.tile([P, T + SLOTS], U8, name="h_plane", align_bytes=64)
         late = {}
 
@@ -67,21 +67,34 @@ def tile_moe_shr_mlp_relu2_kernel(
                 late.setdefault(name, keep.tile(shape, dtype, name=name, tag=tag, align_bytes=64))
             return late[name]
 
+        h_all = keep.tile([P, 4 * (T + SLOTS)], BF16, name="h_all", align_bytes=64)
+        h_last = keep.tile([P, 4 * CHUNK], BF16, name="h_last", tag="last", align_bytes=64)
+        codes_all = keep.tile([P, T + SLOTS], U32, name="codes_all", align_bytes=64)
+
         def h_values(cols):
-            if cols.start >= T:
-                return late_tile("slot_h", [P, 4 * SLOTS], BF16, "slot_h")[:, 4 * (cols.start - T) : 4 * (cols.stop - T)]
-            c = cols.start // CHUNK
-            tile = late_tile("token_h%d" % c, [P, 4 * CHUNK], BF16, TOKEN_H_TAGS[c])
-            return tile[:, 4 * (cols.start - c * CHUNK) : 4 * (cols.stop - c * CHUNK)]
+            if cols.start == P:
+                return late_tile("h_early", [P, H], BF16, "w1_codes0")[:]
+            if B * CHUNK <= cols.start < D * CHUNK:
+                tile = late_tile("h_second", [P, 4 * CHUNK], BF16, "slot_plane0_2")
+                return tile[:, 4 * (cols.start - B * CHUNK) : 4 * (cols.stop - B * CHUNK)]
+            if D * CHUNK <= cols.start < T:
+                return h_last[:, 4 * (cols.start - D * CHUNK) : 4 * (cols.stop - D * CHUNK)]
+            return h_all[:, 4 * cols.start : 4 * cols.stop]
 
         def h_codes(cols):
-            if cols.start >= 2 * CHUNK:
-                tile = late_tile("last_codes", [P, CHUNK + SLOTS], U32, "last_codes")
-                return tile[:, cols.start - 2 * CHUNK : cols.stop - 2 * CHUNK]
-            return late_tile("first_codes", [P, 2 * CHUNK], U32, FIRST_CODES_TAG)[:, cols]
+            if cols.start < D * CHUNK:
+                c = cols.start // CHUNK
+                tile = late_tile("token_codes%d" % c, [P, CHUNK], U32, TOKEN_CODES_TAGS[c])
+                return tile[:, cols.start - c * CHUNK : cols.stop - c * CHUNK]
+            return codes_all[:, cols]
 
         slot_y = keep.tile([P, SLOTS], F32, name="slot_y")
-        result = keep.tile([P, T], F32, name="result")
+        result_tail = keep.tile([P, CHUNK], F32, name="result_tail")
+
+        def result(cols):
+            if cols.start < D * CHUNK:
+                return late_tile("result_head", [P, D * CHUNK], F32, "token_relu2")[:, cols]
+            return result_tail[:]
 
         routed_scales = w1_scales[0:E].rearrange("e s q i -> (e s) q i")
         w2_scale_rows = w2_scales.rearrange("e s q n -> (e s) q n")
@@ -163,7 +176,40 @@ def tile_moe_shr_mlp_relu2_kernel(
 
         def token_square(engine, c, cols):
             src = token_relu[c][:].rearrange("p (u c e) -> p c u e", u=2, e=2)[:, cols]
-            dst = h_values(chunk(c)).rearrange("p (c u e) -> p c u e", u=2, e=2)[:, cols]
+            tokens = slice(c * CHUNK + cols.start, c * CHUNK + cols.stop)
+            dst = h_values(tokens).rearrange("p (c u e) -> p c u e", u=2, e=2)
+            if engine == SCALAR:
+                nc.scalar.activation(dst, src, ACT.Square)
+            elif engine == GPSIMD:
+                nc.gpsimd.tensor_tensor(dst, src, src, ALU.mult)
+            else:
+                nc.vector.tensor_tensor(dst, src, src, ALU.mult)
+
+        def token_block(s, bank):
+            cols = slice(s * P, (s + 1) * P)
+            for t in range(4):
+                for o in range(PASSES):
+                    nc.tensor.matmul_mx(
+                        out=banks[bank][:, t * P : (t + 1) * P],
+                        lhsT=ws_codes[o][:, 2 * t * P : 2 * (t + 1) * P].bitcast(FP4X4),
+                        lhsT_scale=ws_plane[o][:, t * P : (t + 1) * P],
+                        rhs=x_codes[:, o, :][:, cols].bitcast(FP8X4),
+                        rhs_scale=x_plane[:, o, cols],
+                        start=(o == 0),
+                        stop=(o == PASSES - 1),
+                    )
+
+        def block_relu(engine, s, bank):
+            src = banks[bank][:].rearrange("p (t c) -> p c t", t=4)
+            dst = token_relu[D][:, (s - D0) * H : (s - D0 + 1) * H].rearrange("p (c t) -> p c t", t=4)
+            if engine == SCALAR:
+                nc.scalar.activation(dst, src, ACT.Relu)
+            else:
+                nc.vector.tensor_scalar_max(dst, src, 0.0)
+
+        def block_square(engine, s):
+            src = token_relu[D][:, (s - D0) * H : (s - D0 + 1) * H]
+            dst = h_values(slice(s * P, (s + 1) * P))
             if engine == SCALAR:
                 nc.scalar.activation(dst, src, ACT.Square)
             elif engine == GPSIMD:
@@ -239,13 +285,29 @@ def tile_moe_shr_mlp_relu2_kernel(
             cols = block(b)
             nc.vector.tensor_tensor(window[:].indirect(slots(cols)), slot_y[:, cols], gates[:, cols], ALU.mult)
 
+        def apply_gate(b, bank):
+            cols = block(b)
+            nc.vector.tensor_tensor(slot_y[:, cols], banks[bank][:, 0:P], gates[:, cols], ALU.mult)
+
+        def scatter_copy(b):
+            cols = block(b)
+            nc.vector.tensor_copy(window[:].indirect(slots(cols)), slot_y[:, cols])
+
+        def relu_half(engine, b, bank, u):
+            src = banks[bank][:].rearrange("t (p r) -> t r p", r=4)[:, 2 * u : 2 * u + 2, :]
+            dst = slot_relu[b][:].rearrange("t (r p) -> t r p", r=4)[:, 2 * u : 2 * u + 2, :]
+            if engine == SCALAR:
+                nc.scalar.activation(dst, src, ACT.Relu)
+            else:
+                nc.vector.tensor_scalar_max(dst, src, 0.0)
+
         def add_shared(cols, bank, first):
             nc.vector.tensor_tensor(
-                result[:, cols], banks[bank][:, first : first + cols.stop - cols.start], window[:, cols], ALU.add
+                result(cols), banks[bank][:, first : first + cols.stop - cols.start], window[:, cols], ALU.add
             )
 
         def store(cols):
-            nc.sync.dma_start(out=out[:, cols], in_=result[:, cols])
+            nc.sync.dma_start(out=out[:, cols], in_=result(cols))
 
         def chunk(c):
             return slice(c * CHUNK, (c + 1) * CHUNK)
@@ -256,27 +318,27 @@ def tile_moe_shr_mlp_relu2_kernel(
                     out=banks[bank][:],
                     lhsT=x_codes[:, 0, :][:, 0:P].bitcast(FP8X4),
                     lhsT_scale=ws_rows[:, 1, 0:P],
-                    rhs=ws_words[:, 0, :].bitcast(FP4X4),
+                    rhs=x_codes[:, 0, :][:, 0 : 2 * P].bitcast(FP4X4),
                     rhs_scale=ws_rows[:, 0, :],
                     start=True,
                     stop=True,
                 )
 
         nc.sync.dma_start(offsets[:], offs)
-        load_w1(ws_words, SHARED, slice(0, PASSES))
+        load_tokens(slice(0, 1), slice(0, T))
         zero_plane(ws_rows)
         load_scales(ws_rows, w1_scales[SHARED])
-        load_tokens(slice(0, 1), slice(0, T))
-        load_tokens(slice(1, PASSES), slice(0, CHUNK))
+        load_w1(ws_words, SHARED, slice(0, PASSES))
         zero_plane(x_plane)
         load_scales(x_plane, x_scales)
+        load_tokens(slice(1, PASSES), slice(0, CHUNK))
         load_tokens(slice(1, PASSES), slice(CHUNK, T))
-        load_w1(w1_codes[0], 0, slice(0, PASSES))
-        load_w1(w1_codes[1], 1, slice(0, PASSES))
-        load_w2()
         nc.vector.memset(zero[:], 0.0)
         zero_plane(w1_plane)
         load_scales(w1_plane, routed_scales)
+        load_w1(w1_codes[0], 0, slice(0, PASSES))
+        load_w1(w1_codes[1], 1, slice(0, PASSES))
+        load_w2()
         zero_plane(w2_plane)
         load_scales(w2_plane, w2_scale_rows)
         nc.sync.dma_start(out=gates[:], in_=gate)
@@ -286,74 +348,93 @@ def tile_moe_shr_mlp_relu2_kernel(
         first, second = slice(0, C), slice(C, SLOTS)
         low, high = slice(0, P), slice(P, CHUNK)
         warm_up(7)
+        gather_words(0, slice(0, SLOTS))
         for o in range(PASSES):
             permute_scales(o)
-        for u in range(2):
-            for o in range(PASSES):
-                permute_words(o, u)
-        gather_words(0, slice(0, SLOTS))
+        for o, u in ((0, 0), (0, 1), (1, 0), (2, 0), (1, 1), (2, 1)):
+            permute_words(o, u)
         for b in (R0, R1):
             for o in range(PASSES):
                 gather_scales(b, o)
         for cols in (first, second):
             for o in range(1, PASSES):
                 gather_words(o, cols)
-        for c, bank in ((A, 0), (B, 2)):
-            for u in range(2):
-                token_half(c, bank, u)
-                token_relu_half(SCALAR, c, bank, u)
-            token_square(GPSIMD, c, low)
-            token_square(GPSIMD, c, high)
+        token_passes(A, 0, 0)
+        for u in range(2):
+            token_rest(A, 0, u)
+            token_relu_half(SCALAR, A, 0, u)
+        token_square(SCALAR, A, low)
+        token_half(B, 2, 0)
+        token_half(B, 2, 1)
+        token_relu_half(SCALAR, B, 2, 0)
+        token_relu_half(SCALAR, B, 2, 1)
         slot_passes(R0, 4)
         for o in range(PASSES):
             gather_scales(R2, o)
-        relu(SCALAR, R0, 4)
         slot_passes(R1, 5)
+        relu(SCALAR, R0, 4)
         for o in range(PASSES):
             gather_scales(R3, o)
         relu(SCALAR, R1, 5)
-        turn(R0, 0)
-        square(R0, 0)
+        token_square(SCALAR, A, high)
         slot_passes(R2, 6)
+        turn(R0, 0)
         turn(R1, 1)
-        quantize(slot_block(R0))
-        slot_layer2(R0, 0)
-        empty_y(R0, 0)
+        square(R0, 0)
         square(R1, 1)
         relu(VECTOR, R2, 6)
-        scatter(R0)
+        token_square(VECTOR, B, low)
+        quantize(slot_block(R0))
         slot_passes(R3, 7)
+        token_pass(D, 4, 0, 0)
+        token_pass(D, 4, 1, 0)
+        token_pass(D, 4, 0, 1)
+        slot_layer2(R0, 0)
+        token_pass(D, 4, 1, 1)
+        relu_half(SCALAR, R3, 7, 0)
+        relu_half(SCALAR, R3, 7, 1)
+        token_square(VECTOR, B, high)
         quantize(slot_block(R1))
+        empty_y(R0, 0)
         turn(R2, 2)
-        slot_layer2(R1, 1)
-        empty_y(R1, 1)
-        relu(SCALAR, R3, 7)
-        square(R2, 2)
-        scatter(R1)
         turn(R3, 3)
-        quantize(slot_block(R2))
-        slot_layer2(R2, 2)
-        empty_y(R2, 2)
+        quantize(low)
+        quantize(high)
+        quantize(chunk(B))
+        scatter(R0)
+        slot_layer2(R1, 1)
+        square(R2, 2)
+        empty_y(R1, 1)
         square(R3, 3)
+        token_pass(D, 4, 0, 2)
+        token_pass(D, 4, 1, 2)
+        quantize(slot_block(R2))
+        scatter(R1)
+        token_pass(D, 4, 2, 0)
+        token_pass(D, 4, 3, 0)
+        token_pass(D, 4, 2, 1)
+        token_pass(D, 4, 3, 1)
+        token_pass(D, 4, 2, 2)
+        slot_layer2(R2, 2)
+        token_pass(D, 4, 3, 2)
+        token_relu_half(SCALAR, D, 4, 0)
+        empty_y(R2, 2)
         quantize(slot_block(R3))
-        scatter(R2)
         slot_layer2(R3, 3)
+        layer2(SHARED, chunk(A), 6, 0)
+        layer2(SHARED, chunk(B), 6, CHUNK)
+        scatter(R2)
+        token_relu_half(SCALAR, D, 4, 1)
         empty_y(R3, 3)
-        scatter(R3)
-        token_half(D, 6, 0)
-        token_half(D, 6, 1)
-        token_relu_half(SCALAR, D, 6, 0)
-        token_relu_half(SCALAR, D, 6, 1)
         token_square(SCALAR, D, low)
         token_square(SCALAR, D, high)
-        quantize(chunk(A))
-        quantize(chunk(B))
-        layer2(SHARED, slice(0, 2 * CHUNK), 4, 0)
-        quantize(chunk(D))
-        layer2(SHARED, chunk(D), 5, 0)
-        add_shared(chunk(A), 4, 0)
+        scatter(R3)
+        quantize(slice(D0 * P, D1 * P))
+        quantize(slice(D1 * P, T))
+        layer2(SHARED, chunk(D), 7, 0)
+        add_shared(chunk(A), 6, 0)
         store(chunk(A))
-        add_shared(chunk(B), 4, CHUNK)
+        add_shared(chunk(B), 6, CHUNK)
         store(chunk(B))
-        add_shared(chunk(D), 5, 0)
+        add_shared(chunk(D), 7, 0)
         store(chunk(D))

@@ -119,14 +119,14 @@ def tile_moe_shr_mlp_relu2_kernel(
 
         def permute_words(o, u):
             nc.scalar.copy(
-                ws_codes[o][:].bitcast(U16).rearrange("p (t m) -> p t m", t=4)[:, 2 * u : 2 * u + 2, :],
-                ws_words[:, o, :].bitcast(U16).rearrange("p (m t) -> p t m", t=4)[:, 2 * u : 2 * u + 2, :],
+                ws_codes[o][:].bitcast(U16).rearrange("p (t c i) -> p c t i", t=4, i=8)[:, :, 2 * u : 2 * u + 2, :],
+                ws_words[:, o, :].bitcast(U16).rearrange("p (c i t) -> p c t i", t=4, i=8)[:, :, 2 * u : 2 * u + 2, :],
             )
 
         def permute_scales(o):
             nc.vector.tensor_copy(
-                ws_plane[o][:].rearrange("p (t m) -> p t m", t=4),
-                ws_rows[:, o, :].rearrange("p (m t) -> p t m", t=4),
+                ws_plane[o][:].rearrange("p (t c i) -> p c t i", t=4, i=16),
+                ws_rows[:, o, :].rearrange("p (c i t) -> p c t i", t=4, i=16),
             )
 
         def slots(cols):

@@ -27,8 +27,10 @@ WARM_PASSES = 3
 SCALAR, VECTOR, GPSIMD = "scalar", "vector", "gpsimd"
 A, B, D = range(3)
 R0, R1, R2, R3 = range(4)
-TOKEN_CODES_TAGS = ("slot_plane1_0", "second_codes")
+TOKEN_CODES_TAGS = ("slot_relu1", "h_first_slots")
 D0, D1 = 4, 5
+SLOT_Y_TAGS = ("slot_y0", "slot_y1", "slot_y2", "slot_y3")
+PLANE_BUFFER = (0, 1, 2, 0)
 
 
 def tile_moe_shr_mlp_relu2_kernel(
@@ -72,28 +74,35 @@ def tile_moe_shr_mlp_relu2_kernel(
         codes_all = keep.tile([P, T + SLOTS], U32, name="codes_all", align_bytes=64)
 
         def h_values(cols):
+            if cols.start == T:
+                return late_tile("h_first_slots", [P, H], BF16, "h_first_slots")[:]
             if cols.start == P:
-                return late_tile("h_early", [P, H], BF16, "w1_codes0")[:]
+                return late_tile("h_early", [P, H], BF16, "slot_plane2_1")[:]
             if B * CHUNK <= cols.start < D * CHUNK:
-                tile = late_tile("h_second", [P, 4 * CHUNK], BF16, "slot_plane0_2")
+                tile = late_tile("h_second", [P, 4 * CHUNK], BF16, "h_second")
                 return tile[:, 4 * (cols.start - B * CHUNK) : 4 * (cols.stop - B * CHUNK)]
             if D * CHUNK <= cols.start < T:
                 return h_last[:, 4 * (cols.start - D * CHUNK) : 4 * (cols.stop - D * CHUNK)]
             return h_all[:, 4 * cols.start : 4 * cols.stop]
 
         def h_codes(cols):
+            if cols.start >= T + R2 * P:
+                return late_tile("late_slot_codes%d" % cols.start, [P, P], U32, "late_slot_codes")[:]
             if cols.start < D * CHUNK:
                 c = cols.start // CHUNK
                 tile = late_tile("token_codes%d" % c, [P, CHUNK], U32, TOKEN_CODES_TAGS[c])
                 return tile[:, cols.start - c * CHUNK : cols.stop - c * CHUNK]
             return codes_all[:, cols]
 
-        slot_y = keep.tile([P, SLOTS], F32, name="slot_y")
+
+        def slot_y(b):
+            return late_tile("slot_y%d" % b, [P, P], F32, SLOT_Y_TAGS[b])[:]
+
         result_tail = keep.tile([P, CHUNK], F32, name="result_tail")
 
         def result(cols):
             if cols.start < D * CHUNK:
-                return late_tile("result_head", [P, D * CHUNK], F32, "token_relu2")[:, cols]
+                return late_tile("result_head", [P, D * CHUNK], F32, "last")[:, cols]
             return result_tail[:]
 
         routed_scales = w1_scales[0:E].rearrange("e s q i -> (e s) q i")
@@ -133,7 +142,7 @@ def tile_moe_shr_mlp_relu2_kernel(
             return offsets[:, cols.start // 16 : cols.stop // 16]
 
         def gather_scales(b, o):
-            plane = keep.tile([P, P], U8, name="slot_plane%d_%d" % (b, o), tag="slot_plane%d_%d" % (b % 2, o), align_bytes=64)
+            plane = keep.tile([P, P], U8, name="slot_plane%d_%d" % (b, o), tag="slot_plane%d_%d" % (PLANE_BUFFER[b], o), align_bytes=64)
             slot_plane.setdefault((b, o), plane)
             nc.vector.tensor_copy(plane[:], x_plane[:, o, :].indirect(slots(block(b))))
 
@@ -279,19 +288,19 @@ def tile_moe_shr_mlp_relu2_kernel(
             layer2(b * P // C, slot_block(b), bank, 0)
 
         def empty_y(b, bank):
-            nc.scalar.copy(slot_y[:, block(b)], banks[bank][:, 0:P])
+            nc.scalar.copy(slot_y(b), banks[bank][:, 0:P])
 
         def scatter(b):
             cols = block(b)
-            nc.vector.tensor_tensor(window[:].indirect(slots(cols)), slot_y[:, cols], gates[:, cols], ALU.mult)
+            nc.vector.tensor_tensor(window[:].indirect(slots(cols)), slot_y(b), gates[:, cols], ALU.mult)
 
         def apply_gate(b, bank):
             cols = block(b)
-            nc.vector.tensor_tensor(slot_y[:, cols], banks[bank][:, 0:P], gates[:, cols], ALU.mult)
+            nc.vector.tensor_tensor(slot_y(b), banks[bank][:, 0:P], gates[:, cols], ALU.mult)
 
         def scatter_copy(b):
             cols = block(b)
-            nc.vector.tensor_copy(window[:].indirect(slots(cols)), slot_y[:, cols])
+            nc.vector.tensor_copy(window[:].indirect(slots(cols)), slot_y(b))
 
         def relu_half(engine, b, bank, u):
             src = banks[bank][:].rearrange("t (p r) -> t r p", r=4)[:, 2 * u : 2 * u + 2, :]
@@ -332,10 +341,10 @@ def tile_moe_shr_mlp_relu2_kernel(
         zero_plane(x_plane)
         load_scales(x_plane, x_scales)
         load_tokens(slice(1, PASSES), slice(0, CHUNK))
-        load_tokens(slice(1, PASSES), slice(CHUNK, T))
         nc.vector.memset(zero[:], 0.0)
         zero_plane(w1_plane)
         load_scales(w1_plane, routed_scales)
+        load_tokens(slice(1, PASSES), slice(CHUNK, T))
         load_w1(w1_codes[0], 0, slice(0, PASSES))
         load_w1(w1_codes[1], 1, slice(0, PASSES))
         load_w2()
@@ -353,7 +362,7 @@ def tile_moe_shr_mlp_relu2_kernel(
             permute_scales(o)
         for o, u in ((0, 0), (0, 1), (1, 0), (2, 0), (1, 1), (2, 1)):
             permute_words(o, u)
-        for b in (R0, R1):
+        for b in (R0, R1, R2):
             for o in range(PASSES):
                 gather_scales(b, o)
         for cols in (first, second):
@@ -370,43 +379,41 @@ def tile_moe_shr_mlp_relu2_kernel(
         token_relu_half(SCALAR, B, 2, 1)
         slot_passes(R0, 4)
         for o in range(PASSES):
-            gather_scales(R2, o)
+            gather_scales(R3, o)
         slot_passes(R1, 5)
         relu(SCALAR, R0, 4)
-        for o in range(PASSES):
-            gather_scales(R3, o)
         relu(SCALAR, R1, 5)
-        token_square(SCALAR, A, high)
         slot_passes(R2, 6)
+        token_square(SCALAR, A, high)
         turn(R0, 0)
         turn(R1, 1)
         square(R0, 0)
         square(R1, 1)
         relu(VECTOR, R2, 6)
         token_square(VECTOR, B, low)
+        token_square(VECTOR, B, high)
         quantize(slot_block(R0))
+        quantize(low)
+        quantize(high)
+        quantize(chunk(B))
         slot_passes(R3, 7)
         token_pass(D, 4, 0, 0)
         token_pass(D, 4, 1, 0)
         token_pass(D, 4, 0, 1)
         slot_layer2(R0, 0)
         token_pass(D, 4, 1, 1)
+        token_pass(D, 4, 0, 2)
         relu_half(SCALAR, R3, 7, 0)
         relu_half(SCALAR, R3, 7, 1)
-        token_square(VECTOR, B, high)
         quantize(slot_block(R1))
         empty_y(R0, 0)
         turn(R2, 2)
         turn(R3, 3)
-        quantize(low)
-        quantize(high)
-        quantize(chunk(B))
-        scatter(R0)
         slot_layer2(R1, 1)
+        scatter(R0)
         square(R2, 2)
         empty_y(R1, 1)
         square(R3, 3)
-        token_pass(D, 4, 0, 2)
         token_pass(D, 4, 1, 2)
         quantize(slot_block(R2))
         scatter(R1)

@@ -27,8 +27,9 @@ WARM_PASSES = 3
 SCALAR, VECTOR, GPSIMD = "scalar", "vector", "gpsimd"
 A, B, D = range(3)
 R0, R1, R2, R3 = range(4)
-TOKEN_CODES_TAGS = ("slot_relu1", "h_first_slots")
+TOKEN_CODES_TAGS = ("first_slot_codes", "h_first_slots")
 D0, D1 = 4, 5
+TOKEN_BANKS = ((0, 1), (2, 3), (7, 5))
 SLOT_Y_TAGS = ("slot_y0", "slot_y1", "slot_y2", "slot_y3")
 PLANE_BUFFER = (0, 1, 2, 0)
 
@@ -86,6 +87,8 @@ def tile_moe_shr_mlp_relu2_kernel(
             return h_all[:, 4 * cols.start : 4 * cols.stop]
 
         def h_codes(cols):
+            if cols.start == T:
+                return late_tile("first_slot_codes", [P, P], U32, "first_slot_codes")[:]
             if cols.start >= T + R2 * P:
                 return late_tile("late_slot_codes%d" % cols.start, [P, P], U32, "late_slot_codes")[:]
             if cols.start < D * CHUNK:
@@ -98,12 +101,9 @@ def tile_moe_shr_mlp_relu2_kernel(
         def slot_y(b):
             return late_tile("slot_y%d" % b, [P, P], F32, SLOT_Y_TAGS[b])[:]
 
-        result_tail = keep.tile([P, CHUNK], F32, name="result_tail")
 
         def result(cols):
-            if cols.start < D * CHUNK:
-                return late_tile("result_head", [P, D * CHUNK], F32, "last")[:, cols]
-            return result_tail[:]
+            return late_tile("result", [P, T], F32, "last")[:, cols]
 
         routed_scales = w1_scales[0:E].rearrange("e s q i -> (e s) q i")
         w2_scale_rows = w2_scales.rearrange("e s q n -> (e s) q n")
@@ -152,7 +152,7 @@ def tile_moe_shr_mlp_relu2_kernel(
         def token_pass(c, bank, t, o):
             cols = slice(c * CHUNK, (c + 1) * CHUNK)
             nc.tensor.matmul_mx(
-                out=banks[bank + t // 2][:, (t % 2) * CHUNK : (t % 2 + 1) * CHUNK],
+                out=banks[TOKEN_BANKS[c][t // 2]][:, (t % 2) * CHUNK : (t % 2 + 1) * CHUNK],
                 lhsT=ws_codes[o][:, 2 * t * P : 2 * (t + 1) * P].bitcast(FP4X4),
                 lhsT_scale=ws_plane[o][:, t * P : (t + 1) * P],
                 rhs=x_codes[:, o, :][:, cols].bitcast(FP8X4),
@@ -176,12 +176,17 @@ def tile_moe_shr_mlp_relu2_kernel(
                     token_pass(c, bank, t, o)
 
         def token_relu_half(engine, c, bank, u):
-            src = banks[bank + u][:].rearrange("p (e c) -> p c e", e=2)
+            src = banks[TOKEN_BANKS[c][u]][:].rearrange("p (e c) -> p c e", e=2)
             dst = token_relu[c][:, u * BANK : (u + 1) * BANK].rearrange("p (c e) -> p c e", e=2)
             if engine == SCALAR:
                 nc.scalar.activation(dst, src, ACT.Relu)
             else:
                 nc.vector.tensor_scalar_max(dst, src, 0.0)
+
+        def token_relu_part(c, u, cols):
+            src = banks[TOKEN_BANKS[c][u]][:].rearrange("p (e c) -> p c e", e=2)[:, cols]
+            dst = token_relu[c][:, u * BANK : (u + 1) * BANK].rearrange("p (c e) -> p c e", e=2)[:, cols]
+            nc.scalar.activation(dst, src, ACT.Relu)
 
         def token_square(engine, c, cols):
             src = token_relu[c][:].rearrange("p (u c e) -> p c u e", u=2, e=2)[:, cols]
@@ -393,28 +398,29 @@ def tile_moe_shr_mlp_relu2_kernel(
         token_square(VECTOR, B, low)
         token_square(VECTOR, B, high)
         quantize(slot_block(R0))
-        quantize(low)
-        quantize(high)
         quantize(chunk(B))
-        slot_passes(R3, 7)
+        slot_passes(R3, 4)
         token_pass(D, 4, 0, 0)
         token_pass(D, 4, 1, 0)
         token_pass(D, 4, 0, 1)
-        slot_layer2(R0, 0)
         token_pass(D, 4, 1, 1)
         token_pass(D, 4, 0, 2)
-        relu_half(SCALAR, R3, 7, 0)
-        relu_half(SCALAR, R3, 7, 1)
+        slot_layer2(R0, 0)
+        token_pass(D, 4, 1, 2)
+        relu_half(SCALAR, R3, 4, 0)
+        relu_half(SCALAR, R3, 4, 1)
         quantize(slot_block(R1))
+        quantize(low)
+        quantize(high)
         empty_y(R0, 0)
+        token_relu_half(SCALAR, D, 4, 0)
         turn(R2, 2)
-        turn(R3, 3)
         slot_layer2(R1, 1)
+        turn(R3, 3)
         scatter(R0)
         square(R2, 2)
         empty_y(R1, 1)
         square(R3, 3)
-        token_pass(D, 4, 1, 2)
         quantize(slot_block(R2))
         scatter(R1)
         token_pass(D, 4, 2, 0)
@@ -424,24 +430,26 @@ def tile_moe_shr_mlp_relu2_kernel(
         token_pass(D, 4, 2, 2)
         slot_layer2(R2, 2)
         token_pass(D, 4, 3, 2)
-        token_relu_half(SCALAR, D, 4, 0)
+        token_relu_part(D, 1, low)
         empty_y(R2, 2)
         quantize(slot_block(R3))
-        slot_layer2(R3, 3)
         layer2(SHARED, chunk(A), 6, 0)
         layer2(SHARED, chunk(B), 6, CHUNK)
         scatter(R2)
-        token_relu_half(SCALAR, D, 4, 1)
-        empty_y(R3, 3)
+        token_relu_part(D, 1, high)
+        slot_layer2(R3, 2)
         token_square(SCALAR, D, low)
+        empty_y(R3, 2)
         token_square(SCALAR, D, high)
-        scatter(R3)
         quantize(slice(D0 * P, D1 * P))
+        scatter(R3)
         quantize(slice(D1 * P, T))
-        layer2(SHARED, chunk(D), 7, 0)
+        layer2(SHARED, block(D0), 0, 0)
+        layer2(SHARED, block(D1), 1, 0)
         add_shared(chunk(A), 6, 0)
         store(chunk(A))
         add_shared(chunk(B), 6, CHUNK)
         store(chunk(B))
-        add_shared(chunk(D), 7, 0)
+        add_shared(block(D0), 0, 0)
+        add_shared(block(D1), 1, 0)
         store(chunk(D))

@@ -338,8 +338,8 @@ def tile_moe_shr_mlp_relu2_kernel(
                     stop=True,
                 )
 
-        nc.sync.dma_start(offsets[:], offs)
         load_tokens(slice(0, 1), slice(0, T))
+        nc.sync.dma_start(offsets[:], offs)
         zero_plane(ws_rows)
         load_scales(ws_rows, w1_scales[SHARED])
         load_w1(ws_words, SHARED, slice(0, PASSES))

from contextlib import ExitStack

import concourse.mybir as mybir
from concourse.masks import make_identity

K, T, E, C, H, N = 1536, 768, 2, 256, 512, 128
FLOPS = 2 * (T + E * C) * (K * H + H * N)

F32 = mybir.dt.float32
BF16 = mybir.dt.bfloat16
I32 = mybir.dt.int32
U32 = mybir.dt.uint32
U16 = mybir.dt.uint16
U8 = mybir.dt.uint8
FP8X4 = mybir.dt.float8_e4m3fn_x4
FP4X4 = mybir.dt.float4_e2m1fn_x4
ACT = mybir.ActivationFunctionType
ALU = mybir.AluOpType

P = 128
PASSES = K // 512
SHARED = E
BANK = 512
SLOTS = E * C
CHUNK = 256
WARM_PASSES = 3
SCALAR, VECTOR, GPSIMD = "scalar", "vector", "gpsimd"
A, B, D = range(3)
R0, R1, R2, R3 = range(4)
TOKEN_CODES_TAGS = ("first_slot_codes", "h_first_slots")
D0, D1 = 4, 5
TOKEN_BANKS = ((0, 1), (2, 3), (7, 5))
SLOT_Y_TAGS = ("slot_y0", "slot_y1", "slot_y2", "slot_y3")
PLANE_BUFFER = (0, 1, 2, 0)


def tile_moe_shr_mlp_relu2_kernel(
    tc, x_words, x_scales, w1_words, w1_scales, w2_words, w2_scales, gate, offs, out
):
    nc = tc.nc
    with ExitStack() as ctx:
        keep = ctx.enter_context(tc.tile_pool(name="keep", bufs=1))
        psum = ctx.enter_context(tc.psum_pool(name="psum", bufs=1))

        offsets = keep.tile([P, SLOTS // 16], U16, name="offsets")
        x_codes = keep.tile([P, PASSES, T], I32, name="x_codes", align_bytes=64)
        x_plane = keep.tile([P, PASSES, T], U8, name="x_plane", align_bytes=64)
        ws_words = keep.tile([P, PASSES, 2 * H], U8, name="ws_words", align_bytes=64)
        ws_codes = [keep.tile([P, 2 * H], U8, name="ws_codes%d" % o, align_bytes=64) for o in range(PASSES)]
        ws_rows = keep.tile([P, PASSES, H], U8, name="ws_rows", align_bytes=64)
        ws_plane = [keep.tile([P, H], U8, name="ws_plane%d" % o, align_bytes=64) for o in range(PASSES)]
        w1_codes = [keep.tile([P, PASSES, 2 * H], U8, name="w1_codes%d" % e, tag="w1_codes%d" % e, align_bytes=64) for e in range(E)]
        w1_plane = keep.tile([P, E * PASSES, H], U8, name="w1_plane", align_bytes=64)
        w2_codes = keep.tile([P, E + 1, 2 * N], U8, name="w2_codes", align_bytes=64)
        w2_plane = keep.tile([P, E + 1, N], U8, name="w2_plane", align_bytes=64)
        gates = keep.tile([P, SLOTS], F32, name="gates")
        ident = keep.tile([P, P], F32, name="ident")
        zero = keep.tile([P, 1], F32, name="zero")
        window = keep.tile([P, T], F32, name="window")
        slot_codes = [keep.tile([P, SLOTS], U32, name="slot_codes%d" % o, tag="slot_codes%d" % o, align_bytes=64) for o in range(PASSES)]
        slot_plane = {}
        banks = [psum.tile([P, BANK], F32, name="bank%d" % b) for b in range(8)]
        token_relu = [keep.tile([P, 4 * CHUNK], F32, name="token_relu%d" % c, tag="token_relu%d" % c, align_bytes=64) for c in range(T // CHUNK)]
        slot_relu = [keep.tile([P, H], F32, name="slot_relu%d" % b, tag="slot_relu%d" % b, align_bytes=64) for b in range(SLOTS // P)]
        h_plane = keep.tile([P, T + SLOTS], U8, name="h_plane", align_bytes=64)
        late = {}

        def late_tile(name, shape, dtype, tag):
            if name not in late:
                late.setdefault(name, keep.tile(shape, dtype, name=name, tag=tag, align_bytes=64))
            return late[name]

        h_all = keep.tile([P, 4 * (T + SLOTS)], BF16, name="h_all", align_bytes=64)
        h_last = keep.tile([P, 4 * CHUNK], BF16, name="h_last", tag="last", align_bytes=64)
        codes_all = keep.tile([P, T + SLOTS], U32, name="codes_all", align_bytes=64)

        def h_values(cols):
            if cols.start == T:
                return late_tile("h_first_slots", [P, H], BF16, "h_first_slots")[:]
            if cols.start == P:
                return late_tile("h_early", [P, H], BF16, "slot_plane2_1")[:]
            if B * CHUNK <= cols.start < D * CHUNK:
                tile = late_tile("h_second", [P, 4 * CHUNK], BF16, "h_second")
                return tile[:, 4 * (cols.start - B * CHUNK) : 4 * (cols.stop - B * CHUNK)]
            if D * CHUNK <= cols.start < T:
                return h_last[:, 4 * (cols.start - D * CHUNK) : 4 * (cols.stop - D * CHUNK)]
            return h_all[:, 4 * cols.start : 4 * cols.stop]

        def h_codes(cols):
            if cols.start == T:
                return late_tile("first_slot_codes", [P, P], U32, "first_slot_codes")[:]
            if cols.start >= T + R2 * P:
                return late_tile("late_slot_codes%d" % cols.start, [P, P], U32, "late_slot_codes")[:]
            if cols.start < D * CHUNK:
                c = cols.start // CHUNK
                tile = late_tile("token_codes%d" % c, [P, CHUNK], U32, TOKEN_CODES_TAGS[c])
                return tile[:, cols.start - c * CHUNK : cols.stop - c * CHUNK]
            return codes_all[:, cols]


        def slot_y(b):
            return late_tile("slot_y%d" % b, [P, P], F32, SLOT_Y_TAGS[b])[:]


        def result(cols):
            return late_tile("result", [P, T], F32, "last")[:, cols]

        routed_scales = w1_scales[0:E].rearrange("e s q i -> (e s) q i")
        w2_scale_rows = w2_scales.rearrange("e s q n -> (e s) q n")

        def zero_plane(plane):
            nc.vector.memset(plane[:].rearrange("p a b -> p (a b)").bitcast(I32), 0)

        def load_scales(plane, rows):
            by_row = rows.rearrange("a (q r) w -> r q a w", r=4)
            for r in range(4):
                nc.sync.dma_start(out=plane[r:P:32, :, :].bitcast(I32), in_=by_row[r].bitcast(I32))

        def load_tokens(passes, cols):
            words = x_words[passes].rearrange("o p t r -> p o (t r)").bitcast(I32)
            nc.sync.dma_start(out=x_codes[:, passes, cols], in_=words[:, :, cols])

        def load_w1(dst, e, passes):
            nc.sync.dma_start(out=dst[:].bitcast(I32), in_=w1_words[e, passes].rearrange("s p b -> p s b").bitcast(I32))

        def load_w2():
            nc.sync.dma_start(out=w2_codes[:].bitcast(I32), in_=w2_words.rearrange("e s p b -> p (e s) b").bitcast(I32))

        def permute_words(o, u):
            nc.scalar.copy(
                ws_codes[o][:].bitcast(U16).rearrange("p (t c i) -> p c t i", t=4, i=8)[:, :, 2 * u : 2 * u + 2, :],
                ws_words[:, o, :].bitcast(U16).rearrange("p (c i t) -> p c t i", t=4, i=8)[:, :, 2 * u : 2 * u + 2, :],
            )

        def permute_scales(o):
            nc.vector.tensor_copy(
                ws_plane[o][:].rearrange("p (t c i) -> p c t i", t=4, i=16),
                ws_rows[:, o, :].rearrange("p (c i t) -> p c t i", t=4, i=16),
            )

        def slots(cols):
            return offsets[:, cols.start // 16 : cols.stop // 16]

        def gather_scales(b, o):
            plane = keep.tile([P, P], U8, name="slot_plane%d_%d" % (b, o), tag="slot_plane%d_%d" % (PLANE_BUFFER[b], o), align_bytes=64)
            slot_plane.setdefault((b, o), plane)
            nc.vector.tensor_copy(plane[:], x_plane[:, o, :].indirect(slots(block(b))))

        def gather_words(o, cols):
            nc.vector.tensor_copy(slot_codes[o][:, cols], x_codes[:, o, :].bitcast(U32).indirect(slots(cols)))

        def token_pass(c, bank, t, o):
            cols = slice(c * CHUNK, (c + 1) * CHUNK)
            nc.tensor.matmul_mx(
                out=banks[TOKEN_BANKS[c][t // 2]][:, (t % 2) * CHUNK : (t % 2 + 1) * CHUNK],
                lhsT=ws_codes[o][:, 2 * t * P : 2 * (t + 1) * P].bitcast(FP4X4),
                lhsT_scale=ws_plane[o][:, t * P : (t + 1) * P],
                rhs=x_codes[:, o, :][:, cols].bitcast(FP8X4),
                rhs_scale=x_plane[:, o, cols],
                start=(o == 0 and t % 2 == 0),
                stop=(o == PASSES - 1 and t % 2 == 1),
            )

        def token_half(c, bank, u):
            for o in range(PASSES):
                for t in (2 * u, 2 * u + 1):
                    token_pass(c, bank, t, o)

        def token_passes(c, bank, o):
            for t in range(4):
                token_pass(c, bank, t, o)

        def token_rest(c, bank, u):
            for o in range(1, PASSES):
                for t in (2 * u, 2 * u + 1):
                    token_pass(c, bank, t, o)

        def token_relu_half(engine, c, bank, u):
            src = banks[TOKEN_BANKS[c][u]][:].rearrange("p (e c) -> p c e", e=2)
            dst = token_relu[c][:, u * BANK : (u + 1) * BANK].rearrange("p (c e) -> p c e", e=2)
            if engine == SCALAR:
                nc.scalar.activation(dst, src, ACT.Relu)
            else:
                nc.vector.tensor_scalar_max(dst, src, 0.0)

        def token_relu_part(c, u, cols):
            src = banks[TOKEN_BANKS[c][u]][:].rearrange("p (e c) -> p c e", e=2)[:, cols]
            dst = token_relu[c][:, u * BANK : (u + 1) * BANK].rearrange("p (c e) -> p c e", e=2)[:, cols]
            nc.scalar.activation(dst, src, ACT.Relu)

        def token_square(engine, c, cols):
            src = token_relu[c][:].rearrange("p (u c e) -> p c u e", u=2, e=2)[:, cols]
            tokens = slice(c * CHUNK + cols.start, c * CHUNK + cols.stop)
            dst = h_values(tokens).rearrange("p (c u e) -> p c u e", u=2, e=2)
            if engine == SCALAR:
                nc.scalar.activation(dst, src, ACT.Square)
            elif engine == GPSIMD:
                nc.gpsimd.tensor_tensor(dst, src, src, ALU.mult)
            else:
                nc.vector.tensor_tensor(dst, src, src, ALU.mult)

        def token_block(s, bank):
            cols = slice(s * P, (s + 1) * P)
            for t in range(4):
                for o in range(PASSES):
                    nc.tensor.matmul_mx(
                        out=banks[bank][:, t * P : (t + 1) * P],
                        lhsT=ws_codes[o][:, 2 * t * P : 2 * (t + 1) * P].bitcast(FP4X4),
                        lhsT_scale=ws_plane[o][:, t * P : (t + 1) * P],
                        rhs=x_codes[:, o, :][:, cols].bitcast(FP8X4),
                        rhs_scale=x_plane[:, o, cols],
                        start=(o == 0),
                        stop=(o == PASSES - 1),
                    )

        def block_relu(engine, s, bank):
            src = banks[bank][:].rearrange("p (t c) -> p c t", t=4)
            dst = token_relu[D][:, (s - D0) * H : (s - D0 + 1) * H].rearrange("p (c t) -> p c t", t=4)
            if engine == SCALAR:
                nc.scalar.activation(dst, src, ACT.Relu)
            else:
                nc.vector.tensor_scalar_max(dst, src, 0.0)

        def block_square(engine, s):
            src = token_relu[D][:, (s - D0) * H : (s - D0 + 1) * H]
            dst = h_values(slice(s * P, (s + 1) * P))
            if engine == SCALAR:
                nc.scalar.activation(dst, src, ACT.Square)
            elif engine == GPSIMD:
                nc.gpsimd.tensor_tensor(dst, src, src, ALU.mult)
            else:
                nc.vector.tensor_tensor(dst, src, src, ALU.mult)

        def slot_pass(b, bank, o):
            e = b * P // C
            nc.tensor.matmul_mx(
                out=banks[bank][:],
                lhsT=slot_codes[o][:, b * P : (b + 1) * P].bitcast(FP8X4),
                lhsT_scale=slot_plane[(b, o)][:],
                rhs=w1_codes[e][:, o, :].bitcast(FP4X4),
                rhs_scale=w1_plane[:, e * PASSES + o, :],
                start=(o == 0),
                stop=(o == PASSES - 1),
            )

        def slot_passes(b, bank):
            for o in range(PASSES):
                slot_pass(b, bank, o)

        def relu(engine, b, bank):
            src = banks[bank][:].rearrange("t (p r) -> t r p", r=4)
            dst = slot_relu[b][:].rearrange("t (r p) -> t r p", r=4)
            if engine == SCALAR:
                nc.scalar.activation(dst, src, ACT.Relu)
            else:
                nc.vector.tensor_scalar_max(dst, src, 0.0)

        def turn(b, bank):
            for r in range(4):
                cols = slice(r * P, (r + 1) * P)
                nc.tensor.transpose(banks[bank][:, cols], slot_relu[b][:, cols], ident[:])

        def square(b, bank):
            src = banks[bank][:].rearrange("p (r t) -> p t r", r=4)
            dst = h_values(slot_block(b)).rearrange("p (t r) -> p t r", r=4)
            nc.scalar.activation(dst, src, ACT.Square)

        def quantize(cols):
            nc.vector.quantize_mx(
                out=h_codes(cols).bitcast(FP8X4),
                scales=h_plane[:, cols],
                in_=h_values(cols),
            )

        def layer2(e, cols, bank, first):
            nc.tensor.matmul_mx(
                out=banks[bank][:, first : first + cols.stop - cols.start],
                lhsT=w2_codes[:, e, :].bitcast(FP4X4),
                lhsT_scale=w2_plane[:, e, :],
                rhs=h_codes(cols).bitcast(FP8X4),
                rhs_scale=h_plane[:, cols],
                start=True,
                stop=True,
            )

        def block(b):
            return slice(b * P, (b + 1) * P)

        def slot_block(b):
            return slice(T + b * P, T + (b + 1) * P)

        def slot_layer2(b, bank):
            layer2(b * P // C, slot_block(b), bank, 0)

        def empty_y(b, bank):
            nc.scalar.copy(slot_y(b), banks[bank][:, 0:P])

        def scatter(b):
            cols = block(b)
            nc.vector.tensor_tensor(window[:].indirect(slots(cols)), slot_y(b), gates[:, cols], ALU.mult)

        def apply_gate(b, bank):
            cols = block(b)
            nc.vector.tensor_tensor(slot_y(b), banks[bank][:, 0:P], gates[:, cols], ALU.mult)

        def scatter_copy(b):
            cols = block(b)
            nc.vector.tensor_copy(window[:].indirect(slots(cols)), slot_y(b))

        def relu_half(engine, b, bank, u):
            src = banks[bank][:].rearrange("t (p r) -> t r p", r=4)[:, 2 * u : 2 * u + 2, :]
            dst = slot_relu[b][:].rearrange("t (r p) -> t r p", r=4)[:, 2 * u : 2 * u + 2, :]
            if engine == SCALAR:
                nc.scalar.activation(dst, src, ACT.Relu)
            else:
                nc.vector.tensor_scalar_max(dst, src, 0.0)

        def add_shared(cols, bank, first):
            nc.vector.tensor_tensor(
                result(cols), banks[bank][:, first : first + cols.stop - cols.start], window[:, cols], ALU.add
            )

        def store(cols):
            nc.sync.dma_start(out=out[:, cols], in_=result(cols))

        def chunk(c):
            return slice(c * CHUNK, (c + 1) * CHUNK)

        def warm_up(bank):
            for repeat in range(WARM_PASSES):
                nc.tensor.matmul_mx(
                    out=banks[bank][:],
                    lhsT=x_codes[:, 0, :][:, 0:P].bitcast(FP8X4),
                    lhsT_scale=ws_rows[:, 1, 0:P],
                    rhs=x_codes[:, 0, :][:, 0 : 2 * P].bitcast(FP4X4),
                    rhs_scale=ws_rows[:, 0, :],
                    start=True,
                    stop=True,
                )

        load_tokens(slice(0, 1), slice(0, T))
        nc.sync.dma_start(offsets[:], offs)
        zero_plane(ws_rows)
        load_scales(ws_rows, w1_scales[SHARED])
        load_w1(ws_words, SHARED, slice(0, PASSES))
        zero_plane(x_plane)
        load_scales(x_plane, x_scales)
        load_tokens(slice(1, PASSES), slice(0, CHUNK))
        nc.vector.memset(zero[:], 0.0)
        zero_plane(w1_plane)
        load_scales(w1_plane, routed_scales)
        load_tokens(slice(1, PASSES), slice(CHUNK, T))
        load_w1(w1_codes[0], 0, slice(0, PASSES))
        load_w1(w1_codes[1], 1, slice(0, PASSES))
        load_w2()
        zero_plane(w2_plane)
        load_scales(w2_plane, w2_scale_rows)
        nc.sync.dma_start(out=gates[:], in_=gate)
        make_identity(nc, ident[:])
        nc.scalar.activation(window[:], zero[:].to_broadcast([P, T]), ACT.Relu)

        first, second = slice(0, C), slice(C, SLOTS)
        low, high = slice(0, P), slice(P, CHUNK)
        warm_up(7)
        gather_words(0, slice(0, SLOTS))
        for o in range(PASSES):
            permute_scales(o)
        for o, u in ((0, 0), (0, 1), (1, 0), (2, 0), (1, 1), (2, 1)):
            permute_words(o, u)
        for b in (R0, R1, R2):
            for o in range(PASSES):
                gather_scales(b, o)
        for cols in (first, second):
            for o in range(1, PASSES):
                gather_words(o, cols)
        token_passes(A, 0, 0)
        for u in range(2):
            token_rest(A, 0, u)
            token_relu_half(SCALAR, A, 0, u)
        token_square(SCALAR, A, low)
        token_half(B, 2, 0)
        token_half(B, 2, 1)
        token_relu_half(SCALAR, B, 2, 0)
        token_relu_half(SCALAR, B, 2, 1)
        slot_passes(R0, 4)
        for o in range(PASSES):
            gather_scales(R3, o)
        slot_passes(R1, 5)
        relu(SCALAR, R0, 4)
        relu(SCALAR, R1, 5)
        slot_passes(R2, 6)
        token_square(SCALAR, A, high)
        turn(R0, 0)
        turn(R1, 1)
        square(R0, 0)
        square(R1, 1)
        relu(VECTOR, R2, 6)
        token_square(VECTOR, B, low)
        token_square(VECTOR, B, high)
        quantize(slot_block(R0))
        quantize(chunk(B))
        slot_passes(R3, 4)
        token_pass(D, 4, 0, 0)
        token_pass(D, 4, 1, 0)
        token_pass(D, 4, 0, 1)
        token_pass(D, 4, 1, 1)
        token_pass(D, 4, 0, 2)
        slot_layer2(R0, 0)
        token_pass(D, 4, 1, 2)
        relu_half(SCALAR, R3, 4, 0)
        relu_half(SCALAR, R3, 4, 1)
        quantize(slot_block(R1))
        quantize(low)
        quantize(high)
        empty_y(R0, 0)
        token_relu_half(SCALAR, D, 4, 0)
        turn(R2, 2)
        slot_layer2(R1, 1)
        turn(R3, 3)
        scatter(R0)
        square(R2, 2)
        empty_y(R1, 1)
        square(R3, 3)
        quantize(slot_block(R2))
        scatter(R1)
        token_pass(D, 4, 2, 0)
        token_pass(D, 4, 3, 0)
        token_pass(D, 4, 2, 1)
        token_pass(D, 4, 3, 1)
        token_pass(D, 4, 2, 2)
        slot_layer2(R2, 2)
        token_pass(D, 4, 3, 2)
        token_relu_part(D, 1, low)
        empty_y(R2, 2)
        quantize(slot_block(R3))
        layer2(SHARED, chunk(A), 6, 0)
        layer2(SHARED, chunk(B), 6, CHUNK)
        scatter(R2)
        token_relu_part(D, 1, high)
        slot_layer2(R3, 2)
        token_square(SCALAR, D, low)
        empty_y(R3, 2)
        token_square(SCALAR, D, high)
        quantize(slice(D0 * P, D1 * P))
        scatter(R3)
        quantize(slice(D1 * P, T))
        layer2(SHARED, block(D0), 0, 0)
        layer2(SHARED, block(D1), 1, 0)
        add_shared(chunk(A), 6, 0)
        store(chunk(A))
        add_shared(chunk(B), 6, CHUNK)
        store(chunk(B))
        add_shared(block(D0), 0, 0)
        add_shared(block(D1), 1, 0)
        store(chunk(D))
